import numpy as np
import ml_dtypes


def mxq(x, axis, fmt="e4m3"):
    dtype, down = {"e4m3": (ml_dtypes.float8_e4m3fn, 7), "e5m2": (ml_dtypes.float8_e5m2, 14)}[fmt]
    v = np.moveaxis(np.asarray(x, np.float32).astype(ml_dtypes.bfloat16).astype(np.float64), axis, -1)
    blocks = v.reshape(v.shape[:-1] + (-1, 32))
    amax = np.abs(blocks).max(-1, keepdims=True)
    byte = np.maximum(np.where(amax > 0, np.frexp(amax)[1] - 1 + 127, 0) - down, 1)
    scale = np.exp2(byte - 127.0)
    codes = (blocks / scale).astype(np.float32).astype(dtype).astype(np.float64)
    return np.moveaxis((codes * scale).reshape(v.shape), -1, axis)


WIDE = False


def mx_kscale(k):
    if not WIDE:
        return np.ones(k)
    levels = np.array([10, -10, 5, -5, 0])
    if k % 512:
        return np.exp2(np.random.permutation(np.resize(levels, k // 32))).repeat(32)
    a = np.empty((k // 512, 16))
    for p in range(k // 512):
        a[p, :8] = np.random.permutation(np.resize(levels, 8))
        for g in range(8):
            far = levels[np.abs(levels - a[p, g]) >= 10]
            a[p, g + 8] = far[np.random.randint(len(far))]
    return np.exp2(a.ravel()).repeat(32)


def f64(x):
    return np.asarray(x).astype(np.float64)


def striped(idx):
    return np.tile(idx.reshape(-1, 16).T, (8, 1)).astype(np.uint16)


def unstriped(offs):
    return offs[:16].T.reshape(-1).astype(np.int64)


E2M1 = np.array([0.0, 0.5, 1.0, 1.5, 2.0, 3.0, 4.0, 6.0, -0.0, -0.5, -1.0, -1.5, -2.0, -3.0, -4.0, -6.0])


def pack_weight(w, fmt):
    k, n = w.shape
    w = f64(np.asarray(w, np.float32).astype(ml_dtypes.bfloat16)).reshape(k // 32, 32, n)
    amax = np.abs(w).max(1)
    if fmt == "e4m3":
        byte = np.frexp(amax)[1] - 1 + 127 - 7
    else:
        mant, ex = np.frexp(amax / 6.0)
        byte = np.where(mant > 0.5, ex, ex - 1) + 127
    byte = np.clip(np.where(amax > 0, byte, 1), 1, 254)
    scaled = (w * np.exp2(127.0 - byte)[:, None, :]).reshape(k, n).astype(np.float32)
    by_word = np.ascontiguousarray(scaled.reshape(k // 512, 128, 4, n).transpose(0, 1, 3, 2))
    if fmt == "e4m3":
        words = by_word.astype(ml_dtypes.float8_e4m3fn).view(np.uint8)
    else:
        c = by_word.astype(ml_dtypes.float4_e2m1fn).view(np.uint8) & 0xF
        words = (c[..., 0::2] | (c[..., 1::2] << 4)).reshape(k // 512, 128, 2 * n)
    return np.ascontiguousarray(words), np.ascontiguousarray(byte.astype(np.uint8).reshape(k // 512, 16, n))


def unpack_weight(words, scales, fmt):
    g, _, n = scales.shape
    words = np.ascontiguousarray(words).reshape(g, 128, n, -1)
    if fmt == "e4m3":
        vals = words.view(ml_dtypes.float8_e4m3fn).astype(np.float64)
    else:
        nib = np.empty((g, 128, n, 4), np.uint8)
        nib[..., 0::2] = words & 0xF
        nib[..., 1::2] = words >> 4
        vals = E2M1[nib]
    vals = vals * np.repeat(np.exp2(scales.astype(np.float64) - 127.0), 8, axis=1)[..., None]
    return vals.transpose(0, 1, 3, 2).reshape(g * 512, n)


def gelu(v):
    return 0.5 * v * (1.0 + np.tanh(np.sqrt(2.0 / np.pi) * (v + 0.044715 * v**3)))


def bf(x):
    return np.asarray(x, np.float32).astype(ml_dtypes.bfloat16)


def planes(Y):
    n, m = Y.shape
    b = f64(bf(Y)).reshape(n // 32, 32, m)
    amax = np.abs(b).max(1)
    byte = np.clip(np.where(amax > 0, np.frexp(amax)[1] - 1 + 127 - 7, 1), 1, 254)
    codes = (b * np.exp2(127.0 - byte)[:, None, :]).reshape(n, m).astype(np.float32).astype(ml_dtypes.float8_e4m3fn).view(np.uint8)
    words = codes.reshape(n // 512, 128, 4, m).transpose(0, 1, 3, 2)
    return np.ascontiguousarray(words), np.ascontiguousarray(byte.astype(np.uint8).reshape(n // 512, 16, m))


K, H, N, T, S, T2 = 1024, 1024, 512, 2048, 512, 1024

def setup_inputs():
    n = np.random.standard_normal
    s = mx_kscale(K)[:, None]
    u = mx_kscale(H)[:, None]
    tab_words, tab_scales = pack_weight(n((K, T)) * s, "e4m3")
    w1_words, w1_scales = pack_weight(n((K, H)) / np.sqrt(K) / s * u.T, "e2m1")
    w2 = n((K, H)) / np.sqrt(K) / s * u.T
    w3 = 0.5 * n((H, N)) / np.sqrt(H) / (u * u) * np.exp(0.8 * n(N))
    return {
        "tab_words": tab_words, "tab_scales": tab_scales,
        "offs": striped(np.random.permutation(T)[:S]),
        "offs2": striped(np.random.permutation(T2)[:S]),
        "offs3": striped(np.random.permutation(T2)[:S]),
        "w1_words": w1_words, "w1_scales": w1_scales,
        "w2": w2.astype(np.float32),
        "wg1": np.exp(0.3 * n((128, S))).astype(np.float32),
        "wg2": np.exp(0.3 * n((128, S))).astype(np.float32),
        "cons": (n((H, T2)) * u).astype(np.float32),
        "w3": w3.astype(np.float32),
    }

def reference(tab_words, tab_scales, offs, offs2, offs3, w1_words, w1_scales, w2, wg1, wg2, cons, w3):
    v = unpack_weight(tab_words, tab_scales, "e4m3")[:, unstriped(offs)]
    h1 = unpack_weight(w1_words, w1_scales, "e2m1").T @ v
    h2 = mxq(f64(w2), 0, "e4m3").T @ v
    claims = np.zeros((H, T2))
    claims[:, unstriped(offs2)] = np.tile(f64(wg1), (H // 128, 1)) * h1
    evid = np.zeros((H, T2))
    evid[:, unstriped(offs3)] = np.tile(f64(wg2), (H // 128, 1)) * h2
    z = np.square(claims + f64(cons)) - np.square(evid)
    y = mxq(f64(w3), 0, "e4m3").T @ mxq(z, 0, "e4m3")
    words, scales = planes(y)
    return y, words, scales

@@ -1,0 +1,318 @@
+from contextlib import ExitStack
+
+import concourse.mybir as mybir
+from concourse.masks import make_identity
+
+K, H, N, T, S, T2 = 1024, 1024, 512, 2048, 512, 1024
+FLOPS = 2 * (2 * K * H * S + H * N * T2)
+
+F32 = mybir.dt.float32
+BF16 = mybir.dt.bfloat16
+I32 = mybir.dt.int32
+U32 = mybir.dt.uint32
+U16 = mybir.dt.uint16
+U8 = mybir.dt.uint8
+FP8X4 = mybir.dt.float8_e4m3fn_x4
+FP4X4 = mybir.dt.float4_e2m1fn_x4
+MULT = mybir.AluOpType.mult
+SUBTRACT = mybir.AluOpType.subtract
+SQUARE = mybir.ActivationFunctionType.Square
+
+P = 128
+PACK = 4
+K_PASS = P * PACK
+PASSES = K // K_PASS
+ROW_TILES = H // P
+BANK = 512
+HALVES = T2 // BANK
+QUARTER = 256
+QUARTERS = T2 // QUARTER
+W2_CHUNKS = [(0, 1), (1, 1), (2, 2), (4, 2), (6, 2)]
+PAGES = 2
+H_RING = 3
+
+
+def tile_list_trench_dispute_features_kernel(
+    tc, tab_words, tab_scales, offs, offs2, offs3, w1_words, w1_scales, w2, wg1, wg2, cons, w3, out_0, out_1, out_2
+):
+    nc = tc.nc
+    with ExitStack() as ctx:
+        lists = ctx.enter_context(tc.tile_pool(name="lists", bufs=1))
+        keep = ctx.enter_context(tc.tile_pool(name="keep", bufs=1))
+        ring = ctx.enter_context(tc.tile_pool(name="ring", bufs=1))
+        psum = ctx.enter_context(tc.psum_pool(name="psum", bufs=1))
+
+        banks = [psum.tile([P, BANK], F32, name=f"bank{i}") for i in range(8)]
+
+        idx_notes = lists.tile([P, S // 16], U16, name="idx_notes")
+        idx_claims = lists.tile([P, S // 16], U16, name="idx_claims")
+        idx_evid = lists.tile([P, S // 16], U16, name="idx_evid")
+
+        tab_w = [keep.tile([P, T], U32, name=f"tab_w{a}", align_bytes=64) for a in range(PASSES)]
+        tab_s = keep.tile([P, PASSES * T], U8, name="tab_s", align_bytes=64)
+        w1_w = keep.tile([P, PASSES * 2 * H], U8, name="w1_w", align_bytes=64)
+        w1_s = keep.tile([P, PASSES * H], U8, name="w1_s", align_bytes=64)
+        v_w = [keep.tile([P, S], U32, name=f"v_w{a}", align_bytes=64) for a in range(PASSES)]
+        v_s = [keep.tile([P, S], U8, name=f"v_s{a}", align_bytes=64) for a in range(PASSES)]
+        gain1 = keep.tile([P, S], F32, name="gain1")
+        gain2 = keep.tile([P, S], F32, name="gain2")
+        ident = keep.tile([P, P], F32, name="ident")
+        claim_pages = [keep.tile([P, T2], F32, name=f"claim_page{i}") for i in range(PAGES)]
+        evid_pages = [keep.tile([P, T2], F32, name=f"evid_page{i}") for i in range(PAGES)]
+        w2_w = [keep.tile([P, PASSES * n * P], U32, name=f"w2_w{c}", align_bytes=64) for c, n in W2_CHUNKS]
+        w2_s = [keep.tile([P, PASSES * n * P], U8, name=f"w2_s{c}", align_bytes=64) for c, n in W2_CHUNKS]
+        h_ring = [keep.tile([P, S], F32, name=f"h{i}") for i in range(H_RING)]
+        w3_w = [keep.tile([P, N], U32, name=f"w3_w{b}", align_bytes=64) for b in range(PASSES)]
+        w3_s = [keep.tile([P, N], U8, name=f"w3_s{b}", align_bytes=64) for b in range(PASSES)]
+        z_t = [keep.tile([P, PACK * T2], BF16, name=f"z_t{b}") for b in range(PASSES)]
+        z_w = [keep.tile([P, T2], U32, name=f"z_w{b}", align_bytes=64) for b in range(PASSES)]
+        z_s = [keep.tile([P, T2], U8, name=f"z_s{b}", align_bytes=64) for b in range(PASSES)]
+        y_w = keep.tile([P, T2], U32, name="y_w", align_bytes=64)
+        y_s = keep.tile([P, T2], U8, name="y_s", align_bytes=64)
+
+        def load_scale_rows(plane, scales):
+            for quad in range(4):
+                nc.sync.dma_start(
+                    out=plane[32 * quad : 32 * quad + 4, :].bitcast(I32).rearrange("i (a c) -> i a c", a=PASSES),
+                    in_=scales[:, 4 * quad : 4 * quad + 4, :].bitcast(I32).rearrange("a i c -> i a c"),
+                )
+
+        def load_tab_words(a):
+            nc.sync.dma_start(
+                out=tab_w[a][:].bitcast(I32), in_=tab_words[a].rearrange("p t i -> p (t i)").bitcast(I32)
+            )
+
+        nc.vector.memset(tab_s[:].bitcast(I32), 0)
+        nc.vector.memset(w1_s[:].bitcast(I32), 0)
+        nc.sync.dma_start(idx_notes[:], offs)
+        load_tab_words(0)
+        load_scale_rows(tab_s, tab_scales)
+        load_tab_words(1)
+        load_scale_rows(w1_s, w1_scales)
+        nc.sync.dma_start(
+            out=w1_w[:].bitcast(I32).rearrange("p (a c) -> p a c", a=PASSES),
+            in_=w1_words.bitcast(I32).rearrange("a p c -> p a c"),
+        )
+        nc.sync.dma_start(idx_claims[:], offs2)
+        nc.sync.dma_start(out=gain1[:], in_=wg1)
+        nc.sync.dma_start(idx_evid[:], offs3)
+        nc.vector.memset(claim_pages[0][:].bitcast(I32), 0)
+        make_identity(nc, ident[:])
+        for page in claim_pages[1:] + evid_pages:
+            nc.gpsimd.memset(page[:].bitcast(I32), 0)
+
+        for a in range(PASSES):
+            nc.vector.tensor_copy(v_w[a][:], tab_w[a][:].indirect(idx_notes[:]))
+            nc.vector.tensor_copy(v_s[a][:], tab_s[:, a * T : (a + 1) * T].indirect(idx_notes[:]))
+
+        w2_raw, w3_raw, cons_rows = {}, {}, {}
+
+        def load_w2(g):
+            first, tiles = W2_CHUNKS[g]
+            for a in range(PASSES):
+                raw = ring.tile([P, PACK * tiles * P], F32, name="w2_raw", bufs=4)
+                rows = w2[a * K_PASS : (a + 1) * K_PASS, first * P : (first + tiles) * P]
+                nc.sync.dma_start(
+                    out=raw[:].rearrange("p (j w) -> p j w", j=PACK), in_=rows.rearrange("(p j) w -> p j w", j=PACK)
+                )
+                w2_raw[g, a] = raw
+
+        def load_w3(b):
+            raw = ring.tile([P, PACK * N], F32, name="w3_raw", bufs=2)
+            nc.sync.dma_start(out=raw[:], in_=w3[b * K_PASS : (b + 1) * K_PASS, :].rearrange("(p j) n -> p (j n)", j=PACK))
+            w3_raw[b] = raw
+
+        def load_cons(c):
+            rows = ring.tile([P, T2], F32, name="cons_rows", bufs=4)
+            nc.sync.dma_start(out=rows[:], in_=cons[c * P : (c + 1) * P, :])
+            cons_rows[c] = rows
+
+        def rounded_tile(columns):
+            return ring.tile([P, PACK * columns], BF16, name="rounded", bufs=4, align_bytes=64)
+
+        def quantize_w2(g):
+            width = PACK * W2_CHUNKS[g][1] * P
+            rounded = rounded_tile(PASSES * width // PACK)
+            for a in range(PASSES):
+                nc.scalar.copy(
+                    rounded[:, a * width : (a + 1) * width].rearrange("p (c i j) -> p c j i", i=4, j=PACK),
+                    w2_raw[g, a][:].rearrange("p (j c i) -> p c j i", j=PACK, i=4),
+                )
+            nc.vector.quantize_mx(out=w2_w[g][:].bitcast(FP8X4), scales=w2_s[g][:], in_=rounded[:])
+
+        def quantize_w3(b):
+            rounded = rounded_tile(N)
+            dst = rounded[:].rearrange("p (s m j) -> p m j s", s=PACK, j=PACK)
+            src = w3_raw[b][:].rearrange("p (j m s) -> p m j s", j=PACK, s=PACK)
+            for m0 in range(0, P, P // 2):
+                nc.scalar.copy(dst[:, m0 : m0 + P // 2], src[:, m0 : m0 + P // 2])
+            nc.vector.quantize_mx(out=w3_w[b][:].bitcast(FP8X4), scales=w3_s[b][:], in_=rounded[:])
+
+        steps = [("claims", 0)]
+        for c in range(ROW_TILES):
+            steps.extend([("claims", c + 1)] if c + 1 < ROW_TILES else [])
+            steps.append(("evidence", c))
+
+        def stationary(kind, c, a):
+            if kind == "claims":
+                col = a * H + c * P
+                return w1_w[:, 2 * col : 2 * (col + P)].bitcast(FP4X4), w1_s[:, col : col + P]
+            g = max(i for i, (first, tiles) in enumerate(W2_CHUNKS) if first <= c)
+            first, tiles = W2_CHUNKS[g]
+            col = (a * tiles + c - first) * P
+            return w2_w[g][:, col : col + P].bitcast(FP8X4), w2_s[g][:, col : col + P]
+
+        def features(k):
+            kind, c = steps[k]
+            if kind == "evidence":
+                for g, (first, tiles) in enumerate(W2_CHUNKS):
+                    if first == c:
+                        quantize_w2(g)
+            for a in range(PASSES):
+                codes, scales = stationary(kind, c, a)
+                nc.tensor.matmul_mx(
+                    out=banks[0][:],
+                    lhsT=codes,
+                    lhsT_scale=scales,
+                    rhs=v_w[a][:].bitcast(FP8X4),
+                    rhs_scale=v_s[a][:],
+                    start=(a == 0),
+                    stop=(a == PASSES - 1),
+                )
+            nc.scalar.copy(h_ring[k % H_RING][:], banks[0][:])
+
+        def squared_transposed(terms, first_bank, name, bufs):
+            squares = ring.tile([P, T2], F32, name=name, bufs=bufs)
+            for f in range(HALVES):
+                bank = banks[first_bank + f]
+                for u in range(BANK // P):
+                    for i, term in enumerate(terms):
+                        nc.tensor.matmul(
+                            bank[:, u * P : (u + 1) * P],
+                            lhsT=term[:, f * BANK + u * P : f * BANK + (u + 1) * P],
+                            rhs=ident[:],
+                            is_transpose=True,
+                            start=(i == 0),
+                            stop=(i == len(terms) - 1),
+                        )
+                nc.scalar.activation(
+                    squares[:, f * BANK : (f + 1) * BANK].rearrange("t (h u q e) -> t h u q e", h=2, u=4, e=2),
+                    bank[:].rearrange("t (u q h e) -> t h u q e", u=4, h=2, e=2),
+                    SQUARE,
+                )
+            return squares
+
+        claim_sq, evid_sq = {}, {}
+
+        def scatter(k):
+            kind, c = steps[k]
+            h = h_ring[k % H_RING]
+            if kind == "claims":
+                page = claim_pages[c % PAGES]
+                nc.vector.tensor_tensor(page[:].indirect(idx_claims[:]), h[:], gain1[:], MULT)
+                claim_sq[c] = squared_transposed([cons_rows[c], page], 2, "claim_sq", 3)
+            else:
+                page = evid_pages[c % PAGES]
+                nc.vector.tensor_tensor(page[:].indirect(idx_evid[:]), h[:], gain2[:], MULT)
+                evid_sq[c] = squared_transposed([page], 4, "evid_sq", 2)
+
+        def difference(c, groups):
+            b, quad = divmod(c, PACK)
+            nc.vector.tensor_tensor(
+                z_t[b][:].rearrange("t (g x) -> t g x", g=16)[:, groups, 64 * quad : 64 * (quad + 1)],
+                claim_sq[c][:].rearrange("t (g x) -> t g x", g=16)[:, groups, :],
+                evid_sq[c][:].rearrange("t (g x) -> t g x", g=16)[:, groups, :],
+                SUBTRACT,
+            )
+
+        def quantize_z(b, quarters, turn_banks):
+            words = z_t[b][:].bitcast(F32)
+            rounded = rounded_tile(len(quarters) * QUARTER)
+            for i, quarter in enumerate(quarters):
+                bank = banks[turn_banks[i]]
+                f, pair = divmod(quarter, 2)
+                for u in range(2):
+                    for h in range(2):
+                        g = 8 * f + 4 * h + 2 * pair + u
+                        nc.tensor.transpose(
+                            bank[:, (2 * u + h) * P : (2 * u + h + 1) * P], words[:, g * P : (g + 1) * P], ident[:]
+                        )
+                nc.scalar.copy(
+                    rounded[:].bitcast(F32)[:, i * BANK : (i + 1) * BANK].rearrange("p (u t h) -> p u t h", u=2, h=2),
+                    bank[:].rearrange("p (u h t) -> p u t h", u=2, h=2),
+                )
+            cols = slice(quarters[0] * QUARTER, (quarters[-1] + 1) * QUARTER)
+            nc.vector.quantize_mx(out=z_w[b][:, cols].bitcast(FP8X4), scales=z_s[b][:, cols], in_=rounded[:])
+
+        y_banks = [(0, 1), (2, 3), (6, 7), (0, 1)]
+
+        def y_pass(b, quarter):
+            cols = slice(quarter * QUARTER, (quarter + 1) * QUARTER)
+            for j in range(PACK):
+                nc.tensor.matmul_mx(
+                    out=banks[y_banks[quarter][j // 2]][:, (j % 2) * QUARTER : (j % 2 + 1) * QUARTER],
+                    lhsT=w3_w[b][:, j * P : (j + 1) * P].bitcast(FP8X4),
+                    lhsT_scale=w3_s[b][:, j * P : (j + 1) * P],
+                    rhs=z_w[b][:, cols].bitcast(FP8X4),
+                    rhs_scale=z_s[b][:, cols],
+                    start=(b == 0 and j % 2 == 0),
+                    stop=(b == PASSES - 1 and j % 2 == 1),
+                )
+
+        y_rows = out_0.rearrange("(p j) t -> p j t", j=PACK)
+        y_words = out_1[0].rearrange("p t i -> p (t i)").bitcast(I32)
+
+        def finish(quarter):
+            cols = slice(quarter * QUARTER, (quarter + 1) * QUARTER)
+            y_all = keep.tile([P, PACK * QUARTER], F32, name=f"y_all{quarter}")
+            for i, bank in enumerate(y_banks[quarter]):
+                nc.scalar.copy(y_all[:, i * BANK : (i + 1) * BANK], banks[bank][:])
+            nc.sync.dma_start(out=y_rows[:, :, cols], in_=y_all[:].rearrange("p (j t) -> p j t", j=PACK))
+            y_rounded = keep.tile([P, PACK * QUARTER], BF16, name=f"y_rounded{quarter}", align_bytes=64)
+            nc.vector.tensor_copy(
+                y_rounded[:].rearrange("p (c i j) -> p c j i", i=4, j=PACK),
+                y_all[:].rearrange("p (j c i) -> p c j i", j=PACK, i=4),
+            )
+            nc.vector.quantize_mx(out=y_w[:, cols].bitcast(FP8X4), scales=y_s[:, cols], in_=y_rounded[:])
+            nc.sync.dma_start(out=y_words[:, cols], in_=y_w[:, cols].bitcast(I32))
+
+        load_w2(0)
+        nc.sync.dma_start(out=gain2[:], in_=wg2)
+        for c in range(4):
+            load_cons(c)
+            load_w2(c + 1)
+        load_w3(0)
+        load_w3(1)
+
+        features(0)
+        for k, (kind, c) in enumerate(steps):
+            if k + 1 < len(steps):
+                features(k + 1)
+            scatter(k)
+            if kind == "claims" and c >= 2:
+                difference(c - 2, slice(0, 16))
+                if c + 2 < ROW_TILES:
+                    load_cons(c + 2)
+            if kind == "evidence" and c in (1, 2):
+                quantize_w3(c - 1)
+            if kind == "evidence" and c == PACK:
+                for f in range(HALVES):
+                    quantize_z(0, [2 * f, 2 * f + 1], [6, 7])
+
+        y_pass(0, 0)
+        y_pass(0, 1)
+        difference(ROW_TILES - 2, slice(0, 16))
+        for f in range(HALVES):
+            difference(ROW_TILES - 1, slice(8 * f, 8 * f + 8))
+        for quarter in range(QUARTERS):
+            quantize_z(1, [quarter], [(6, 7, 4, 5)[quarter]])
+            if quarter >= 2:
+                finish(quarter - 2)
+                y_pass(0, quarter)
+            y_pass(1, quarter)
+        finish(2)
+        finish(3)
+        for quad in range(4):
+            nc.sync.dma_start(
+                out=out_2[0, 4 * quad : 4 * quad + 4, :].bitcast(I32), in_=y_s[32 * quad : 32 * quad + 4, :].bitcast(I32)
+            )

@@ -29,7 +29,8 @@ QUARTER = 256
 QUARTERS = T2 // QUARTER
 W2_CHUNKS = [(0, 1), (1, 1), (2, 2), (4, 2), (6, 2)]
 PAGES = 2
-H_RING = 3
+H_RING = 6
+AHEAD = 4
 
 
 def tile_list_trench_dispute_features_kernel(
@@ -164,10 +165,6 @@ def tile_list_trench_dispute_features_kernel(
 
         def features(k):
             kind, c = steps[k]
-            if kind == "evidence":
-                for g, (first, tiles) in enumerate(W2_CHUNKS):
-                    if first == c:
-                        quantize_w2(g)
             for a in range(PASSES):
                 codes, scales = stationary(kind, c, a)
                 nc.tensor.matmul_mx(
@@ -179,7 +176,10 @@ def tile_list_trench_dispute_features_kernel(
                     start=(a == 0),
                     stop=(a == PASSES - 1),
                 )
-            nc.scalar.copy(h_ring[k % H_RING][:], banks[0][:])
+            h = h_ring[k % H_RING]
+            nc.scalar.copy(h[:], banks[0][:])
+            if k > 0:
+                nc.gpsimd.tensor_tensor(h[:], h[:], (gain1 if kind == "claims" else gain2)[:], MULT)
 
         def squared_transposed(terms, first_bank, name, bufs):
             squares = ring.tile([P, T2], F32, name=name, bufs=bufs)
@@ -209,16 +209,19 @@ def tile_list_trench_dispute_features_kernel(
             h = h_ring[k % H_RING]
             if kind == "claims":
                 page = claim_pages[c % PAGES]
-                nc.vector.tensor_tensor(page[:].indirect(idx_claims[:]), h[:], gain1[:], MULT)
+                if k == 0:
+                    nc.vector.tensor_tensor(page[:].indirect(idx_claims[:]), h[:], gain1[:], MULT)
+                else:
+                    nc.vector.tensor_copy(page[:].indirect(idx_claims[:]), h[:])
                 claim_sq[c] = squared_transposed([cons_rows[c], page], 2, "claim_sq", 3)
             else:
                 page = evid_pages[c % PAGES]
-                nc.vector.tensor_tensor(page[:].indirect(idx_evid[:]), h[:], gain2[:], MULT)
+                nc.vector.tensor_copy(page[:].indirect(idx_evid[:]), h[:])
                 evid_sq[c] = squared_transposed([page], 4, "evid_sq", 2)
 
         def difference(c, groups):
             b, quad = divmod(c, PACK)
-            nc.vector.tensor_tensor(
+            (nc.vector if c == ROW_TILES - 1 else nc.gpsimd).tensor_tensor(
                 z_t[b][:].rearrange("t (g x) -> t g x", g=16)[:, groups, 64 * quad : 64 * (quad + 1)],
                 claim_sq[c][:].rearrange("t (g x) -> t g x", g=16)[:, groups, :],
                 evid_sq[c][:].rearrange("t (g x) -> t g x", g=16)[:, groups, :],
@@ -278,16 +281,23 @@ def tile_list_trench_dispute_features_kernel(
 
         load_w2(0)
         nc.sync.dma_start(out=gain2[:], in_=wg2)
+        load_w2(1)
         for c in range(4):
+            if c + 2 < len(W2_CHUNKS):
+                load_w2(c + 2)
             load_cons(c)
-            load_w2(c + 1)
         load_w3(0)
         load_w3(1)
 
         features(0)
+        features(1)
+        for g in range(len(W2_CHUNKS)):
+            quantize_w2(g)
+        for k in range(2, AHEAD):
+            features(k)
         for k, (kind, c) in enumerate(steps):
-            if k + 1 < len(steps):
-                features(k + 1)
+            if k + AHEAD < len(steps):
+                features(k + AHEAD)
             scatter(k)
             if kind == "claims" and c >= 2:
                 difference(c - 2, slice(0, 16))
@@ -297,11 +307,11 @@ def tile_list_trench_dispute_features_kernel(
                 quantize_w3(c - 1)
             if kind == "evidence" and c == PACK:
                 for f in range(HALVES):
-                    quantize_z(0, [2 * f, 2 * f + 1], [6, 7])
+                    quantize_z(0, [2 * f, 2 * f + 1], [4, 5])
 
+        difference(ROW_TILES - 2, slice(0, 16))
         y_pass(0, 0)
         y_pass(0, 1)
-        difference(ROW_TILES - 2, slice(0, 16))
         for f in range(HALVES):
             difference(ROW_TILES - 1, slice(8 * f, 8 * f + 8))
         for quarter in range(QUARTERS):

@@ -28,6 +28,7 @@ HALVES = T2 // BANK
 QUARTER = 256
 QUARTERS = T2 // QUARTER
 W2_CHUNKS = [(0, 1), (1, 1), (2, 2), (4, 2), (6, 2)]
+W2_CALLS = [[0], [1], [2], [3, 4]]
 PAGES = 2
 H_RING = 6
 AHEAD = 4
@@ -60,11 +61,11 @@ def tile_list_trench_dispute_features_kernel(
         ident = keep.tile([P, P], F32, name="ident")
         claim_pages = [keep.tile([P, T2], F32, name=f"claim_page{i}") for i in range(PAGES)]
         evid_pages = [keep.tile([P, T2], F32, name=f"evid_page{i}") for i in range(PAGES)]
-        w2_w = [keep.tile([P, PASSES * n * P], U32, name=f"w2_w{c}", align_bytes=64) for c, n in W2_CHUNKS]
-        w2_s = [keep.tile([P, PASSES * n * P], U8, name=f"w2_s{c}", align_bytes=64) for c, n in W2_CHUNKS]
+        w2_w = keep.tile([P, PASSES * H], U32, name="w2_w", align_bytes=64)
+        w2_s = keep.tile([P, PASSES * H], U8, name="w2_s", align_bytes=64)
         h_ring = [keep.tile([P, S], F32, name=f"h{i}") for i in range(H_RING)]
-        w3_w = [keep.tile([P, N], U32, name=f"w3_w{b}", align_bytes=64) for b in range(PASSES)]
-        w3_s = [keep.tile([P, N], U8, name=f"w3_s{b}", align_bytes=64) for b in range(PASSES)]
+        w3_w = keep.tile([P, PASSES * N], U32, name="w3_w", align_bytes=64)
+        w3_s = keep.tile([P, PASSES * N], U8, name="w3_s", align_bytes=64)
         z_t = [keep.tile([P, PACK * T2], BF16, name=f"z_t{b}") for b in range(PASSES)]
         z_w = [keep.tile([P, T2], U32, name=f"z_w{b}", align_bytes=64) for b in range(PASSES)]
         z_s = [keep.tile([P, T2], U8, name=f"z_s{b}", align_bytes=64) for b in range(PASSES)]
@@ -131,23 +132,29 @@ def tile_list_trench_dispute_features_kernel(
         def rounded_tile(columns):
             return ring.tile([P, PACK * columns], BF16, name="rounded", bufs=4, align_bytes=64)
 
-        def quantize_w2(g):
-            width = PACK * W2_CHUNKS[g][1] * P
-            rounded = rounded_tile(PASSES * width // PACK)
-            for a in range(PASSES):
-                nc.scalar.copy(
-                    rounded[:, a * width : (a + 1) * width].rearrange("p (c i j) -> p c j i", i=4, j=PACK),
-                    w2_raw[g, a][:].rearrange("p (j c i) -> p c j i", j=PACK, i=4),
-                )
-            nc.vector.quantize_mx(out=w2_w[g][:].bitcast(FP8X4), scales=w2_s[g][:], in_=rounded[:])
+        def quantize_w2(chunks):
+            first = PASSES * P * W2_CHUNKS[chunks[0]][0]
+            columns = PASSES * P * sum(W2_CHUNKS[g][1] for g in chunks)
+            rounded = rounded_tile(columns)
+            for g in chunks:
+                for a in range(PASSES):
+                    width = PACK * P * W2_CHUNKS[g][1]
+                    start = PACK * (PASSES * P * W2_CHUNKS[g][0] - first) + a * width
+                    nc.scalar.copy(
+                        rounded[:, start : start + width].rearrange("p (c i j) -> p c j i", i=4, j=PACK),
+                        w2_raw[g, a][:].rearrange("p (j c i) -> p c j i", j=PACK, i=4),
+                    )
+            cols = slice(first, first + columns)
+            nc.vector.quantize_mx(out=w2_w[:, cols].bitcast(FP8X4), scales=w2_s[:, cols], in_=rounded[:])
 
-        def quantize_w3(b):
-            rounded = rounded_tile(N)
-            dst = rounded[:].rearrange("p (s m j) -> p m j s", s=PACK, j=PACK)
-            src = w3_raw[b][:].rearrange("p (j m s) -> p m j s", j=PACK, s=PACK)
-            for m0 in range(0, P, P // 2):
-                nc.scalar.copy(dst[:, m0 : m0 + P // 2], src[:, m0 : m0 + P // 2])
-            nc.vector.quantize_mx(out=w3_w[b][:].bitcast(FP8X4), scales=w3_s[b][:], in_=rounded[:])
+        def quantize_w3():
+            rounded = rounded_tile(PASSES * N)
+            for b in range(PASSES):
+                dst = rounded[:, b * PACK * N : (b + 1) * PACK * N].rearrange("p (s m j) -> p m j s", s=PACK, j=PACK)
+                src = w3_raw[b][:].rearrange("p (j m s) -> p m j s", j=PACK, s=PACK)
+                for m0 in range(0, P, P // 2):
+                    nc.scalar.copy(dst[:, m0 : m0 + P // 2], src[:, m0 : m0 + P // 2])
+            nc.vector.quantize_mx(out=w3_w[:].bitcast(FP8X4), scales=w3_s[:], in_=rounded[:])
 
         steps = [("claims", 0)]
         for c in range(ROW_TILES):
@@ -160,8 +167,8 @@ def tile_list_trench_dispute_features_kernel(
                 return w1_w[:, 2 * col : 2 * (col + P)].bitcast(FP4X4), w1_s[:, col : col + P]
             g = max(i for i, (first, tiles) in enumerate(W2_CHUNKS) if first <= c)
             first, tiles = W2_CHUNKS[g]
-            col = (a * tiles + c - first) * P
-            return w2_w[g][:, col : col + P].bitcast(FP8X4), w2_s[g][:, col : col + P]
+            col = (PASSES * first + a * tiles + c - first) * P
+            return w2_w[:, col : col + P].bitcast(FP8X4), w2_s[:, col : col + P]
 
         def features(k):
             kind, c = steps[k]
@@ -177,9 +184,12 @@ def tile_list_trench_dispute_features_kernel(
                     stop=(a == PASSES - 1),
                 )
             h = h_ring[k % H_RING]
-            nc.scalar.copy(h[:], banks[0][:])
-            if k > 0:
-                nc.gpsimd.tensor_tensor(h[:], h[:], (gain1 if kind == "claims" else gain2)[:], MULT)
+            gain = gain1 if kind == "claims" else gain2
+            if k == 0:
+                nc.vector.tensor_tensor(h[:], banks[0][:], gain[:], MULT)
+            else:
+                nc.scalar.copy(h[:], banks[0][:])
+                nc.gpsimd.tensor_tensor(h[:], h[:], gain[:], MULT)
 
         def squared_transposed(terms, first_bank, name, bufs):
             squares = ring.tile([P, T2], F32, name=name, bufs=bufs)
@@ -209,10 +219,7 @@ def tile_list_trench_dispute_features_kernel(
             h = h_ring[k % H_RING]
             if kind == "claims":
                 page = claim_pages[c % PAGES]
-                if k == 0:
-                    nc.vector.tensor_tensor(page[:].indirect(idx_claims[:]), h[:], gain1[:], MULT)
-                else:
-                    nc.vector.tensor_copy(page[:].indirect(idx_claims[:]), h[:])
+                nc.vector.tensor_copy(page[:].indirect(idx_claims[:]), h[:])
                 claim_sq[c] = squared_transposed([cons_rows[c], page], 2, "claim_sq", 3)
             else:
                 page = evid_pages[c % PAGES]
@@ -221,7 +228,7 @@ def tile_list_trench_dispute_features_kernel(
 
         def difference(c, groups):
             b, quad = divmod(c, PACK)
-            (nc.vector if c == ROW_TILES - 1 else nc.gpsimd).tensor_tensor(
+            (nc.vector if c >= ROW_TILES - 2 else nc.gpsimd).tensor_tensor(
                 z_t[b][:].rearrange("t (g x) -> t g x", g=16)[:, groups, 64 * quad : 64 * (quad + 1)],
                 claim_sq[c][:].rearrange("t (g x) -> t g x", g=16)[:, groups, :],
                 evid_sq[c][:].rearrange("t (g x) -> t g x", g=16)[:, groups, :],
@@ -240,22 +247,22 @@ def tile_list_trench_dispute_features_kernel(
                         nc.tensor.transpose(
                             bank[:, (2 * u + h) * P : (2 * u + h + 1) * P], words[:, g * P : (g + 1) * P], ident[:]
                         )
-                nc.scalar.copy(
+                (nc.vector.tensor_copy if b == 1 and quarter % 2 == 1 else nc.scalar.copy)(
                     rounded[:].bitcast(F32)[:, i * BANK : (i + 1) * BANK].rearrange("p (u t h) -> p u t h", u=2, h=2),
                     bank[:].rearrange("p (u h t) -> p u t h", u=2, h=2),
                 )
             cols = slice(quarters[0] * QUARTER, (quarters[-1] + 1) * QUARTER)
             nc.vector.quantize_mx(out=z_w[b][:, cols].bitcast(FP8X4), scales=z_s[b][:, cols], in_=rounded[:])
 
-        y_banks = [(0, 1), (2, 3), (6, 7), (0, 1)]
+        y_banks = [(0, 1), (2, 3), (6, 7), (4, 5)]
 
         def y_pass(b, quarter):
             cols = slice(quarter * QUARTER, (quarter + 1) * QUARTER)
             for j in range(PACK):
                 nc.tensor.matmul_mx(
                     out=banks[y_banks[quarter][j // 2]][:, (j % 2) * QUARTER : (j % 2 + 1) * QUARTER],
-                    lhsT=w3_w[b][:, j * P : (j + 1) * P].bitcast(FP8X4),
-                    lhsT_scale=w3_s[b][:, j * P : (j + 1) * P],
+                    lhsT=w3_w[:, b * N + j * P : b * N + (j + 1) * P].bitcast(FP8X4),
+                    lhsT_scale=w3_s[:, b * N + j * P : b * N + (j + 1) * P],
                     rhs=z_w[b][:, cols].bitcast(FP8X4),
                     rhs_scale=z_s[b][:, cols],
                     start=(b == 0 and j % 2 == 0),
@@ -291,8 +298,8 @@ def tile_list_trench_dispute_features_kernel(
 
         features(0)
         features(1)
-        for g in range(len(W2_CHUNKS)):
-            quantize_w2(g)
+        for chunks in W2_CALLS:
+            quantize_w2(chunks)
         for k in range(2, AHEAD):
             features(k)
         for k, (kind, c) in enumerate(steps):
@@ -300,28 +307,27 @@ def tile_list_trench_dispute_features_kernel(
                 features(k + AHEAD)
             scatter(k)
             if kind == "claims" and c >= 2:
-                difference(c - 2, slice(0, 16))
+                for f in range(HALVES):
+                    difference(c - 2, slice(8 * f, 8 * f + 8))
                 if c + 2 < ROW_TILES:
                     load_cons(c + 2)
-            if kind == "evidence" and c in (1, 2):
-                quantize_w3(c - 1)
+            if kind == "evidence" and c == 1:
+                quantize_w3()
             if kind == "evidence" and c == PACK:
-                for f in range(HALVES):
-                    quantize_z(0, [2 * f, 2 * f + 1], [4, 5])
+                quantize_z(0, list(range(QUARTERS)), [4, 5, 4, 5])
 
-        difference(ROW_TILES - 2, slice(0, 16))
         y_pass(0, 0)
         y_pass(0, 1)
+        difference(ROW_TILES - 2, slice(0, 16))
         for f in range(HALVES):
             difference(ROW_TILES - 1, slice(8 * f, 8 * f + 8))
         for quarter in range(QUARTERS):
             quantize_z(1, [quarter], [(6, 7, 4, 5)[quarter]])
+        for quarter in range(QUARTERS):
             if quarter >= 2:
-                finish(quarter - 2)
                 y_pass(0, quarter)
             y_pass(1, quarter)
-        finish(2)
-        finish(3)
+            finish(quarter)
         for quad in range(4):
             nc.sync.dma_start(
                 out=out_2[0, 4 * quad : 4 * quad + 4, :].bitcast(I32), in_=y_s[32 * quad : 32 * quad + 4, :].bitcast(I32)

@@ -191,6 +191,16 @@ def tile_list_trench_dispute_features_kernel(
                 nc.scalar.copy(h[:], banks[0][:])
                 nc.gpsimd.tensor_tensor(h[:], h[:], gain[:], MULT)
 
+        def last_difference(quarter):
+            c = ROW_TILES - 1
+            b, quad = divmod(c, PACK)
+            f, pair = divmod(quarter, 2)
+            views = [
+                tile[:].rearrange("t (f h u x) -> t f h u x", f=2, h=2, u=4)[:, f, :, 2 * pair : 2 * pair + 2, :]
+                for tile in (z_t[b], claim_sq[c], evid_sq[c])
+            ]
+            nc.vector.tensor_tensor(views[0][:, :, :, 64 * quad : 64 * (quad + 1)], views[1], views[2], SUBTRACT)
+
         def squared_transposed(terms, first_bank, name, bufs):
             squares = ring.tile([P, T2], F32, name=name, bufs=bufs)
             for f in range(HALVES):
@@ -254,7 +264,7 @@ def tile_list_trench_dispute_features_kernel(
             cols = slice(quarters[0] * QUARTER, (quarters[-1] + 1) * QUARTER)
             nc.vector.quantize_mx(out=z_w[b][:, cols].bitcast(FP8X4), scales=z_s[b][:, cols], in_=rounded[:])
 
-        y_banks = [(0, 1), (2, 3), (6, 7), (4, 5)]
+        y_banks = [(0, 1), (2, 3), (6, 7), (0, 1)]
 
         def y_pass(b, quarter):
             cols = slice(quarter * QUARTER, (quarter + 1) * QUARTER)
@@ -284,7 +294,6 @@ def tile_list_trench_dispute_features_kernel(
                 y_all[:].rearrange("p (j c i) -> p c j i", j=PACK, i=4),
             )
             nc.vector.quantize_mx(out=y_w[:, cols].bitcast(FP8X4), scales=y_s[:, cols], in_=y_rounded[:])
-            nc.sync.dma_start(out=y_words[:, cols], in_=y_w[:, cols].bitcast(I32))
 
         load_w2(0)
         nc.sync.dma_start(out=gain2[:], in_=wg2)
@@ -318,16 +327,20 @@ def tile_list_trench_dispute_features_kernel(
 
         y_pass(0, 0)
         y_pass(0, 1)
+        y_pass(0, 2)
         difference(ROW_TILES - 2, slice(0, 16))
-        for f in range(HALVES):
-            difference(ROW_TILES - 1, slice(8 * f, 8 * f + 8))
         for quarter in range(QUARTERS):
-            quantize_z(1, [quarter], [(6, 7, 4, 5)[quarter]])
+            last_difference(quarter)
         for quarter in range(QUARTERS):
-            if quarter >= 2:
+            quantize_z(1, [quarter], [4 + quarter % 2])
+        for quarter in range(QUARTERS):
+            if quarter == QUARTERS - 1:
                 y_pass(0, quarter)
             y_pass(1, quarter)
             finish(quarter)
+        for half in range(HALVES):
+            cols = slice(half * BANK, (half + 1) * BANK)
+            nc.sync.dma_start(out=y_words[:, cols], in_=y_w[:, cols].bitcast(I32))
         for quad in range(4):
             nc.sync.dma_start(
                 out=out_2[0, 4 * quad : 4 * quad + 4, :].bitcast(I32), in_=y_s[32 * quad : 32 * quad + 4, :].bitcast(I32)

@@ -30,8 +30,8 @@ QUARTERS = T2 // QUARTER
 W2_CHUNKS = [(0, 1), (1, 1), (2, 2), (4, 2), (6, 2)]
 W2_CALLS = [[0], [1], [2], [3, 4]]
 PAGES = 2
-H_RING = 6
-AHEAD = 4
+H_RING = 8
+AHEAD = 6
 
 
 def tile_list_trench_dispute_features_kernel(
@@ -130,7 +130,7 @@ def tile_list_trench_dispute_features_kernel(
             cons_rows[c] = rows
 
         def rounded_tile(columns):
-            return ring.tile([P, PACK * columns], BF16, name="rounded", bufs=4, align_bytes=64)
+            return ring.tile([P, PACK * columns], BF16, name="rounded", bufs=3, align_bytes=64)
 
         def quantize_w2(chunks):
             first = PASSES * P * W2_CHUNKS[chunks[0]][0]
@@ -264,7 +264,7 @@ def tile_list_trench_dispute_features_kernel(
             cols = slice(quarters[0] * QUARTER, (quarters[-1] + 1) * QUARTER)
             nc.vector.quantize_mx(out=z_w[b][:, cols].bitcast(FP8X4), scales=z_s[b][:, cols], in_=rounded[:])
 
-        y_banks = [(0, 1), (2, 3), (6, 7), (0, 1)]
+        y_banks = [(0, 1), (2, 3), (4, 5), (0, 1)]
 
         def y_pass(b, quarter):
             cols = slice(quarter * QUARTER, (quarter + 1) * QUARTER)
@@ -320,21 +320,21 @@ def tile_list_trench_dispute_features_kernel(
                     difference(c - 2, slice(8 * f, 8 * f + 8))
                 if c + 2 < ROW_TILES:
                     load_cons(c + 2)
+            if k == 14:
+                for quarter in (0, 1):
+                    y_pass(0, quarter)
             if kind == "evidence" and c == 1:
                 quantize_w3()
             if kind == "evidence" and c == PACK:
                 quantize_z(0, list(range(QUARTERS)), [4, 5, 4, 5])
 
-        y_pass(0, 0)
-        y_pass(0, 1)
-        y_pass(0, 2)
         difference(ROW_TILES - 2, slice(0, 16))
         for quarter in range(QUARTERS):
             last_difference(quarter)
         for quarter in range(QUARTERS):
-            quantize_z(1, [quarter], [4 + quarter % 2])
+            quantize_z(1, [quarter], [(6, 7, 4, 5)[quarter]])
         for quarter in range(QUARTERS):
-            if quarter == QUARTERS - 1:
+            if quarter >= 2:
                 y_pass(0, quarter)
             y_pass(1, quarter)
             finish(quarter)

@@ -27,11 +27,14 @@ BANK = 512
 HALVES = T2 // BANK
 QUARTER = 256
 QUARTERS = T2 // QUARTER
+LIST_COLUMNS = S // 16
 W2_CHUNKS = [(0, 1), (1, 1), (2, 2), (4, 2), (6, 2)]
 W2_CALLS = [[0], [1], [2], [3, 4]]
 PAGES = 2
-H_RING = 8
 AHEAD = 6
+H_RING = AHEAD + 2
+W3_AFTER_EVIDENCE = 1
+FIRST_PARTS = 2
 
 
 def tile_list_trench_dispute_features_kernel(
@@ -46,9 +49,9 @@ def tile_list_trench_dispute_features_kernel(
 
         banks = [psum.tile([P, BANK], F32, name=f"bank{i}") for i in range(8)]
 
-        idx_notes = lists.tile([P, S // 16], U16, name="idx_notes")
-        idx_claims = lists.tile([P, S // 16], U16, name="idx_claims")
-        idx_evid = lists.tile([P, S // 16], U16, name="idx_evid")
+        idx_notes = lists.tile([P, LIST_COLUMNS], U16, name="idx_notes")
+        idx_claims = lists.tile([P, LIST_COLUMNS], U16, name="idx_claims")
+        idx_evid = lists.tile([P, LIST_COLUMNS], U16, name="idx_evid")
 
         tab_w = [keep.tile([P, T], U32, name=f"tab_w{a}", align_bytes=64) for a in range(PASSES)]
         tab_s = keep.tile([P, PASSES * T], U8, name="tab_s", align_bytes=64)
@@ -103,9 +106,17 @@ def tile_list_trench_dispute_features_kernel(
         for page in claim_pages[1:] + evid_pages:
             nc.gpsimd.memset(page[:].bitcast(I32), 0)
 
+        def entries(part):
+            return slice(part * S // FIRST_PARTS, (part + 1) * S // FIRST_PARTS)
+
+        def list_columns(part):
+            return slice(part * LIST_COLUMNS // FIRST_PARTS, (part + 1) * LIST_COLUMNS // FIRST_PARTS)
+
+        nc.vector.tensor_copy(v_w[0][:], tab_w[0][:].indirect(idx_notes[:]))
         for a in range(PASSES):
-            nc.vector.tensor_copy(v_w[a][:], tab_w[a][:].indirect(idx_notes[:]))
             nc.vector.tensor_copy(v_s[a][:], tab_s[:, a * T : (a + 1) * T].indirect(idx_notes[:]))
+        for part in range(FIRST_PARTS):
+            nc.vector.tensor_copy(v_w[1][:, entries(part)], tab_w[1][:].indirect(idx_notes[:, list_columns(part)]))
 
         w2_raw, w3_raw, cons_rows = {}, {}, {}
 
@@ -170,6 +181,24 @@ def tile_list_trench_dispute_features_kernel(
             col = (PASSES * first + a * tiles + c - first) * P
             return w2_w[:, col : col + P].bitcast(FP8X4), w2_s[:, col : col + P]
 
+        def first_features():
+            for part in range(FIRST_PARTS):
+                bank, width = banks[1 - part], S // FIRST_PARTS
+                for a in range(PASSES):
+                    codes, scales = stationary("claims", 0, a)
+                    for u in range(width // P):
+                        cols = slice(part * width + u * P, part * width + (u + 1) * P)
+                        nc.tensor.matmul_mx(
+                            out=bank[:, u * P : (u + 1) * P],
+                            lhsT=codes,
+                            lhsT_scale=scales,
+                            rhs=v_w[a][:, cols].bitcast(FP8X4),
+                            rhs_scale=v_s[a][:, cols],
+                            start=(a == 0 and u == 0),
+                            stop=(a == PASSES - 1 and u == width // P - 1),
+                        )
+                nc.vector.tensor_tensor(h_ring[0][:, entries(part)], bank[:, 0:width], gain1[:, entries(part)], MULT)
+
         def features(k):
             kind, c = steps[k]
             for a in range(PASSES):
@@ -185,11 +214,8 @@ def tile_list_trench_dispute_features_kernel(
                 )
             h = h_ring[k % H_RING]
             gain = gain1 if kind == "claims" else gain2
-            if k == 0:
-                nc.vector.tensor_tensor(h[:], banks[0][:], gain[:], MULT)
-            else:
-                nc.scalar.copy(h[:], banks[0][:])
-                nc.gpsimd.tensor_tensor(h[:], h[:], gain[:], MULT)
+            nc.scalar.copy(h[:], banks[0][:])
+            nc.gpsimd.tensor_tensor(h[:], h[:], gain[:], MULT)
 
         def last_difference(quarter):
             c = ROW_TILES - 1
@@ -229,7 +255,11 @@ def tile_list_trench_dispute_features_kernel(
             h = h_ring[k % H_RING]
             if kind == "claims":
                 page = claim_pages[c % PAGES]
-                nc.vector.tensor_copy(page[:].indirect(idx_claims[:]), h[:])
+                if k == 0:
+                    for part in range(FIRST_PARTS):
+                        nc.vector.tensor_copy(page[:].indirect(idx_claims[:, list_columns(part)]), h[:, entries(part)])
+                else:
+                    nc.vector.tensor_copy(page[:].indirect(idx_claims[:]), h[:])
                 claim_sq[c] = squared_transposed([cons_rows[c], page], 2, "claim_sq", 3)
             else:
                 page = evid_pages[c % PAGES]
@@ -257,14 +287,14 @@ def tile_list_trench_dispute_features_kernel(
                         nc.tensor.transpose(
                             bank[:, (2 * u + h) * P : (2 * u + h + 1) * P], words[:, g * P : (g + 1) * P], ident[:]
                         )
-                (nc.vector.tensor_copy if b == 1 and quarter % 2 == 1 else nc.scalar.copy)(
+                (nc.vector.tensor_copy if b == PASSES - 1 and quarter == 1 else nc.scalar.copy)(
                     rounded[:].bitcast(F32)[:, i * BANK : (i + 1) * BANK].rearrange("p (u t h) -> p u t h", u=2, h=2),
                     bank[:].rearrange("p (u h t) -> p u t h", u=2, h=2),
                 )
             cols = slice(quarters[0] * QUARTER, (quarters[-1] + 1) * QUARTER)
             nc.vector.quantize_mx(out=z_w[b][:, cols].bitcast(FP8X4), scales=z_s[b][:, cols], in_=rounded[:])
 
-        y_banks = [(0, 1), (2, 3), (4, 5), (0, 1)]
+        y_banks = [(0, 1), (2, 3), (6, 7), (0, 1)]
 
         def y_pass(b, quarter):
             cols = slice(quarter * QUARTER, (quarter + 1) * QUARTER)
@@ -286,7 +316,8 @@ def tile_list_trench_dispute_features_kernel(
             cols = slice(quarter * QUARTER, (quarter + 1) * QUARTER)
             y_all = keep.tile([P, PACK * QUARTER], F32, name=f"y_all{quarter}")
             for i, bank in enumerate(y_banks[quarter]):
-                nc.scalar.copy(y_all[:, i * BANK : (i + 1) * BANK], banks[bank][:])
+                copy = nc.vector.tensor_copy if quarter == 0 and i == 1 else nc.scalar.copy
+                copy(y_all[:, i * BANK : (i + 1) * BANK], banks[bank][:])
             nc.sync.dma_start(out=y_rows[:, :, cols], in_=y_all[:].rearrange("p (j t) -> p j t", j=PACK))
             y_rounded = keep.tile([P, PACK * QUARTER], BF16, name=f"y_rounded{quarter}", align_bytes=64)
             nc.vector.tensor_copy(
@@ -305,7 +336,7 @@ def tile_list_trench_dispute_features_kernel(
         load_w3(0)
         load_w3(1)
 
-        features(0)
+        first_features()
         features(1)
         for chunks in W2_CALLS:
             quantize_w2(chunks)
@@ -320,10 +351,10 @@ def tile_list_trench_dispute_features_kernel(
                     difference(c - 2, slice(8 * f, 8 * f + 8))
                 if c + 2 < ROW_TILES:
                     load_cons(c + 2)
-            if k == 14:
+            if k == len(steps) - 2:
                 for quarter in (0, 1):
                     y_pass(0, quarter)
-            if kind == "evidence" and c == 1:
+            if kind == "evidence" and c == W3_AFTER_EVIDENCE:
                 quantize_w3()
             if kind == "evidence" and c == PACK:
                 quantize_z(0, list(range(QUARTERS)), [4, 5, 4, 5])

@@ -75,9 +75,9 @@ def tile_list_trench_dispute_features_kernel(
         y_w = keep.tile([P, T2], U32, name="y_w", align_bytes=64)
         y_s = keep.tile([P, T2], U8, name="y_s", align_bytes=64)
 
-        def load_scale_rows(plane, scales):
+        def load_scale_rows(queue, plane, scales):
             for quad in range(4):
-                nc.sync.dma_start(
+                queue.dma_start(
                     out=plane[32 * quad : 32 * quad + 4, :].bitcast(I32).rearrange("i (a c) -> i a c", a=PASSES),
                     in_=scales[:, 4 * quad : 4 * quad + 4, :].bitcast(I32).rearrange("a i c -> i a c"),
                 )
@@ -88,12 +88,12 @@ def tile_list_trench_dispute_features_kernel(
             )
 
         nc.vector.memset(tab_s[:].bitcast(I32), 0)
-        nc.vector.memset(w1_s[:].bitcast(I32), 0)
+        nc.gpsimd.memset(w1_s[:].bitcast(I32), 0)
+        load_scale_rows(nc.gpsimd, w1_s, w1_scales)
         nc.sync.dma_start(idx_notes[:], offs)
         load_tab_words(0)
-        load_scale_rows(tab_s, tab_scales)
+        load_scale_rows(nc.sync, tab_s, tab_scales)
         load_tab_words(1)
-        load_scale_rows(w1_s, w1_scales)
         nc.sync.dma_start(
             out=w1_w[:].bitcast(I32).rearrange("p (a c) -> p a c", a=PASSES),
             in_=w1_words.bitcast(I32).rearrange("a p c -> p a c"),

@@ -28,12 +28,13 @@ HALVES = T2 // BANK
 QUARTER = 256
 QUARTERS = T2 // QUARTER
 LIST_COLUMNS = S // 16
-W2_CHUNKS = [(0, 1), (1, 1), (2, 2), (4, 2), (6, 2)]
-W2_CALLS = [[0], [1], [2], [3, 4]]
-PAGES = 2
-AHEAD = 6
-H_RING = AHEAD + 2
-W3_AFTER_EVIDENCE = 1
+W2_CHUNK = 2
+W2_CALLS = [[0], [1], [2, 3]]
+PAGES = {"claims": 3, "evidence": 2}
+PAIR_SLOTS = {0: "d", 2: "b", 3: "a", 6: "c", 8: "b", 10: "c", 12: "b", 14: "c"}
+W2_SLOTS = {0: "b", 1: "a", 3: "c"}
+LEAD = 2
+W3_AFTER_PAIR = 3
 FIRST_PARTS = 2
 
 
@@ -59,15 +60,13 @@ def tile_list_trench_dispute_features_kernel(
         w1_s = keep.tile([P, PASSES * H], U8, name="w1_s", align_bytes=64)
         v_w = [keep.tile([P, S], U32, name=f"v_w{a}", align_bytes=64) for a in range(PASSES)]
         v_s = [keep.tile([P, S], U8, name=f"v_s{a}", align_bytes=64) for a in range(PASSES)]
-        gain1 = keep.tile([P, S], F32, name="gain1")
-        gain2 = keep.tile([P, S], F32, name="gain2")
+        gains = keep.tile([P, 2 * S], F32, name="gains")
+        gain = {"claims": gains[:, 0:S], "evidence": gains[:, S : 2 * S]}
         ident = keep.tile([P, P], F32, name="ident")
-        claim_pages = [keep.tile([P, T2], F32, name=f"claim_page{i}") for i in range(PAGES)]
-        evid_pages = [keep.tile([P, T2], F32, name=f"evid_page{i}") for i in range(PAGES)]
+        claim_pages = [keep.tile([P, T2], F32, name=f"claim_page{i}") for i in range(PAGES["claims"])]
+        evid_pages = [keep.tile([P, T2], F32, name=f"evid_page{i}") for i in range(PAGES["evidence"])]
         w2_w = keep.tile([P, PASSES * H], U32, name="w2_w", align_bytes=64)
         w2_s = keep.tile([P, PASSES * H], U8, name="w2_s", align_bytes=64)
-        h_ring = [keep.tile([P, S], F32, name=f"h{i}") for i in range(H_RING)]
-        w3_w = keep.tile([P, PASSES * N], U32, name="w3_w", align_bytes=64)
         w3_s = keep.tile([P, PASSES * N], U8, name="w3_s", align_bytes=64)
         z_t = [keep.tile([P, PACK * T2], BF16, name=f"z_t{b}") for b in range(PASSES)]
         z_w = [keep.tile([P, T2], U32, name=f"z_w{b}", align_bytes=64) for b in range(PASSES)]
@@ -89,7 +88,6 @@ def tile_list_trench_dispute_features_kernel(
 
         nc.vector.memset(tab_s[:].bitcast(I32), 0)
         nc.gpsimd.memset(w1_s[:].bitcast(I32), 0)
-        load_scale_rows(nc.gpsimd, w1_s, w1_scales)
         nc.sync.dma_start(idx_notes[:], offs)
         load_tab_words(0)
         load_scale_rows(nc.sync, tab_s, tab_scales)
@@ -98,8 +96,9 @@ def tile_list_trench_dispute_features_kernel(
             out=w1_w[:].bitcast(I32).rearrange("p (a c) -> p a c", a=PASSES),
             in_=w1_words.bitcast(I32).rearrange("a p c -> p a c"),
         )
+        load_scale_rows(nc.sync, w1_s, w1_scales)
         nc.sync.dma_start(idx_claims[:], offs2)
-        nc.sync.dma_start(out=gain1[:], in_=wg1)
+        nc.sync.dma_start(out=gain["claims"], in_=wg1)
         nc.sync.dma_start(idx_evid[:], offs3)
         nc.vector.memset(claim_pages[0][:].bitcast(I32), 0)
         make_identity(nc, ident[:])
@@ -121,9 +120,12 @@ def tile_list_trench_dispute_features_kernel(
         w2_raw, w3_raw, cons_rows = {}, {}, {}
 
         def load_w2(g):
-            first, tiles = W2_CHUNKS[g]
+            first, tiles = g * W2_CHUNK, W2_CHUNK
             for a in range(PASSES):
-                raw = ring.tile([P, PACK * tiles * P], F32, name="w2_raw", bufs=4)
+                if a == PASSES - 1 and g in W2_SLOTS:
+                    raw = ring.tile([P, PACK * tiles * P], F32, name="slot_" + W2_SLOTS[g], bufs=1, align_bytes=64)
+                else:
+                    raw = ring.tile([P, PACK * tiles * P], F32, name="w2_raw", bufs=5)
                 rows = w2[a * K_PASS : (a + 1) * K_PASS, first * P : (first + tiles) * P]
                 nc.sync.dma_start(
                     out=raw[:].rearrange("p (j w) -> p j w", j=PACK), in_=rows.rearrange("(p j) w -> p j w", j=PACK)
@@ -131,59 +133,75 @@ def tile_list_trench_dispute_features_kernel(
                 w2_raw[g, a] = raw
 
         def load_w3(b):
-            raw = ring.tile([P, PACK * N], F32, name="w3_raw", bufs=2)
-            nc.sync.dma_start(out=raw[:], in_=w3[b * K_PASS : (b + 1) * K_PASS, :].rearrange("(p j) n -> p (j n)", j=PACK))
-            w3_raw[b] = raw
+            rows = w3[b * K_PASS : (b + 1) * K_PASS, :].rearrange("(p j) n -> p j n", j=PACK)
+            for half in range(2):
+                raw = ring.tile([P, PACK * N // 2], F32, name="cons_rows", bufs=ROW_TILES)
+                cols = slice(half * N // 2, (half + 1) * N // 2)
+                nc.sync.dma_start(out=raw[:].rearrange("p (j n) -> p j n", j=PACK), in_=rows[:, :, cols])
+                w3_raw[b, half] = raw
 
         def load_cons(c):
-            rows = ring.tile([P, T2], F32, name="cons_rows", bufs=4)
+            rows = ring.tile([P, T2], F32, name="cons_rows", bufs=ROW_TILES)
             nc.sync.dma_start(out=rows[:], in_=cons[c * P : (c + 1) * P, :])
             cons_rows[c] = rows
 
         def rounded_tile(columns):
             return ring.tile([P, PACK * columns], BF16, name="rounded", bufs=3, align_bytes=64)
 
-        def quantize_w2(chunks):
-            first = PASSES * P * W2_CHUNKS[chunks[0]][0]
-            columns = PASSES * P * sum(W2_CHUNKS[g][1] for g in chunks)
+        w2_rounded = {}
+
+        def round_w2(chunks):
+            first = PASSES * P * W2_CHUNK * chunks[0]
+            columns = PASSES * P * W2_CHUNK * len(chunks)
             rounded = rounded_tile(columns)
             for g in chunks:
                 for a in range(PASSES):
-                    width = PACK * P * W2_CHUNKS[g][1]
-                    start = PACK * (PASSES * P * W2_CHUNKS[g][0] - first) + a * width
+                    width = PACK * P * W2_CHUNK
+                    start = PACK * (PASSES * P * W2_CHUNK * g - first) + a * width
                     nc.scalar.copy(
                         rounded[:, start : start + width].rearrange("p (c i j) -> p c j i", i=4, j=PACK),
                         w2_raw[g, a][:].rearrange("p (j c i) -> p c j i", j=PACK, i=4),
                     )
-            cols = slice(first, first + columns)
+            w2_rounded[chunks[0]] = rounded, slice(first, first + columns)
+
+        def quantize_w2(chunks):
+            rounded, cols = w2_rounded[chunks[0]]
             nc.vector.quantize_mx(out=w2_w[:, cols].bitcast(FP8X4), scales=w2_s[:, cols], in_=rounded[:])
 
-        def quantize_w3():
-            rounded = rounded_tile(PASSES * N)
-            for b in range(PASSES):
-                dst = rounded[:, b * PACK * N : (b + 1) * PACK * N].rearrange("p (s m j) -> p m j s", s=PACK, j=PACK)
-                src = w3_raw[b][:].rearrange("p (j m s) -> p m j s", j=PACK, s=PACK)
-                for m0 in range(0, P, P // 2):
-                    nc.scalar.copy(dst[:, m0 : m0 + P // 2], src[:, m0 : m0 + P // 2])
-            nc.vector.quantize_mx(out=w3_w[:].bitcast(FP8X4), scales=w3_s[:], in_=rounded[:])
+        w3_rounded, w3_w = {}, {}
 
-        steps = [("claims", 0)]
+        def round_w3(b):
+            rounded = ring.tile([P, PACK * N], BF16, name="w3_rounded", bufs=PASSES, align_bytes=64)
+            w3_rounded[b] = rounded
+            dst = rounded[:].rearrange("p (s m j) -> p m j s", s=PACK, j=PACK)
+            for half in range(2):
+                src = w3_raw[b, half][:].rearrange("p (j m s) -> p m j s", j=PACK, s=PACK)
+                nc.scalar.copy(dst[:, half * P // 2 : (half + 1) * P // 2], src)
+
+        def quantize_w3(b, tile_name):
+            w3_w[b] = ring.tile([P, N], U32, name=tile_name, bufs=1, align_bytes=64)
+            nc.vector.quantize_mx(
+                out=w3_w[b][:].bitcast(FP8X4), scales=w3_s[:, b * N : (b + 1) * N], in_=w3_rounded[b][:]
+            )
+
+        steps = [("claims", c) for c in range(LEAD)]
         for c in range(ROW_TILES):
-            steps.extend([("claims", c + 1)] if c + 1 < ROW_TILES else [])
+            steps.extend([("claims", c + LEAD)] if c + LEAD < ROW_TILES else [])
             steps.append(("evidence", c))
+        steps[4], steps[5] = steps[5], steps[4]
+        pairs = len(steps) // 2
 
         def stationary(kind, c, a):
             if kind == "claims":
                 col = a * H + c * P
                 return w1_w[:, 2 * col : 2 * (col + P)].bitcast(FP4X4), w1_s[:, col : col + P]
-            g = max(i for i, (first, tiles) in enumerate(W2_CHUNKS) if first <= c)
-            first, tiles = W2_CHUNKS[g]
-            col = (PASSES * first + a * tiles + c - first) * P
+            g, tile = divmod(c, W2_CHUNK)
+            col = ((PASSES * g + a) * W2_CHUNK + tile) * P
             return w2_w[:, col : col + P].bitcast(FP8X4), w2_s[:, col : col + P]
 
         def first_features():
             for part in range(FIRST_PARTS):
-                bank, width = banks[1 - part], S // FIRST_PARTS
+                bank, width = banks[6 + part], S // FIRST_PARTS
                 for a in range(PASSES):
                     codes, scales = stationary("claims", 0, a)
                     for u in range(width // P):
@@ -197,14 +215,14 @@ def tile_list_trench_dispute_features_kernel(
                             start=(a == 0 and u == 0),
                             stop=(a == PASSES - 1 and u == width // P - 1),
                         )
-                nc.vector.tensor_tensor(h_ring[0][:, entries(part)], bank[:, 0:width], gain1[:, entries(part)], MULT)
+                nc.vector.tensor_tensor(h[0][:, entries(part)], bank[:, 0:width], gains[:, entries(part)], MULT)
 
-        def features(k):
+        def product(k, bank):
             kind, c = steps[k]
             for a in range(PASSES):
                 codes, scales = stationary(kind, c, a)
                 nc.tensor.matmul_mx(
-                    out=banks[0][:],
+                    out=banks[bank][:],
                     lhsT=codes,
                     lhsT_scale=scales,
                     rhs=v_w[a][:].bitcast(FP8X4),
@@ -212,10 +230,28 @@ def tile_list_trench_dispute_features_kernel(
                     start=(a == 0),
                     stop=(a == PASSES - 1),
                 )
-            h = h_ring[k % H_RING]
-            gain = gain1 if kind == "claims" else gain2
-            nc.scalar.copy(h[:], banks[0][:])
-            nc.gpsimd.tensor_tensor(h[:], h[:], gain[:], MULT)
+
+        h = {}
+        raw_features = keep.tile([P, S], F32, name="raw_features")
+
+        def new_pair(first, second):
+            both = ring.tile([P, 2 * S], F32, name="slot_" + PAIR_SLOTS[first], bufs=1, align_bytes=64)
+            h[first], h[second] = both[:, 0:S], both[:, S : 2 * S]
+            return both
+
+        def gained_step(k, bank):
+            nc.scalar.copy(h[k], banks[bank][:])
+            nc.gpsimd.tensor_tensor(h[k], h[k], gain[steps[k][0]], MULT)
+
+        def gained_pair(pair):
+            both = new_pair(2 * pair, 2 * pair + 1)
+            nc.scalar.copy(h[2 * pair], banks[0][:])
+            nc.scalar.copy(h[2 * pair + 1], banks[1][:])
+            if steps[2 * pair][0] == "evidence":
+                rows = both[:].rearrange("p (s j) -> p s j", s=2)
+                nc.gpsimd.tensor_tensor(rows, rows, gain["evidence"].unsqueeze(1).to_broadcast([P, 2, S]), MULT)
+            else:
+                nc.gpsimd.tensor_tensor(both[:], both[:], gains[:], MULT)
 
         def last_difference(quarter):
             c = ROW_TILES - 1
@@ -227,10 +263,18 @@ def tile_list_trench_dispute_features_kernel(
             ]
             nc.vector.tensor_tensor(views[0][:, :, :, 64 * quad : 64 * (quad + 1)], views[1], views[2], SUBTRACT)
 
-        def squared_transposed(terms, first_bank, name, bufs):
-            squares = ring.tile([P, T2], F32, name=name, bufs=bufs)
-            for f in range(HALVES):
-                bank = banks[first_bank + f]
+        def page_banks(k):
+            kind, c = steps[k]
+            first = {1: 4, ROW_TILES - 1: 6}.get(c, 2) if kind == "claims" else {ROW_TILES - 2: 2}.get(c, 4)
+            return banks[first : first + HALVES]
+
+        def transposes(k):
+            kind, c = steps[k]
+            if kind == "claims":
+                terms = [cons_rows[c], claim_pages[c % len(claim_pages)]]
+            else:
+                terms = [evid_pages[c % len(evid_pages)]]
+            for f, bank in enumerate(page_banks(k)):
                 for u in range(BANK // P):
                     for i, term in enumerate(terms):
                         nc.tensor.matmul(
@@ -241,30 +285,35 @@ def tile_list_trench_dispute_features_kernel(
                             start=(i == 0),
                             stop=(i == len(terms) - 1),
                         )
+
+        def squares(k):
+            kind, c = steps[k]
+            if kind == "claims":
+                result = ring.tile([P, T2], F32, name="claim_sq", bufs=LEAD + 2)
+                claim_sq[c] = result
+            else:
+                result = ring.tile([P, T2], F32, name="evid_sq", bufs=2)
+                evid_sq[c] = result
+            for f, bank in enumerate(page_banks(k)):
                 nc.scalar.activation(
-                    squares[:, f * BANK : (f + 1) * BANK].rearrange("t (h u q e) -> t h u q e", h=2, u=4, e=2),
+                    result[:, f * BANK : (f + 1) * BANK].rearrange("t (h u q e) -> t h u q e", h=2, u=4, e=2),
                     bank[:].rearrange("t (u q h e) -> t h u q e", u=4, h=2, e=2),
                     SQUARE,
                 )
-            return squares
 
         claim_sq, evid_sq = {}, {}
 
         def scatter(k):
             kind, c = steps[k]
-            h = h_ring[k % H_RING]
-            if kind == "claims":
-                page = claim_pages[c % PAGES]
-                if k == 0:
-                    for part in range(FIRST_PARTS):
-                        nc.vector.tensor_copy(page[:].indirect(idx_claims[:, list_columns(part)]), h[:, entries(part)])
-                else:
-                    nc.vector.tensor_copy(page[:].indirect(idx_claims[:]), h[:])
-                claim_sq[c] = squared_transposed([cons_rows[c], page], 2, "claim_sq", 3)
+            if k == 0:
+                for part in range(FIRST_PARTS):
+                    nc.vector.tensor_copy(
+                        claim_pages[0][:].indirect(idx_claims[:, list_columns(part)]), h[0][:, entries(part)]
+                    )
+            elif kind == "claims":
+                nc.vector.tensor_copy(claim_pages[c % len(claim_pages)][:].indirect(idx_claims[:]), h[k])
             else:
-                page = evid_pages[c % PAGES]
-                nc.vector.tensor_copy(page[:].indirect(idx_evid[:]), h[:])
-                evid_sq[c] = squared_transposed([page], 4, "evid_sq", 2)
+                nc.vector.tensor_copy(evid_pages[c % len(evid_pages)][:].indirect(idx_evid[:]), h[k])
 
         def difference(c, groups):
             b, quad = divmod(c, PACK)
@@ -275,7 +324,9 @@ def tile_list_trench_dispute_features_kernel(
                 SUBTRACT,
             )
 
-        def quantize_z(b, quarters, turn_banks):
+        z_rounded = {}
+
+        def turn_z(b, quarters, turn_banks):
             words = z_t[b][:].bitcast(F32)
             rounded = rounded_tile(len(quarters) * QUARTER)
             for i, quarter in enumerate(quarters):
@@ -291,7 +342,10 @@ def tile_list_trench_dispute_features_kernel(
                     rounded[:].bitcast(F32)[:, i * BANK : (i + 1) * BANK].rearrange("p (u t h) -> p u t h", u=2, h=2),
                     bank[:].rearrange("p (u h t) -> p u t h", u=2, h=2),
                 )
-            cols = slice(quarters[0] * QUARTER, (quarters[-1] + 1) * QUARTER)
+            z_rounded[b] = rounded, slice(quarters[0] * QUARTER, (quarters[-1] + 1) * QUARTER)
+
+        def quantize_z(b):
+            rounded, cols = z_rounded[b]
             nc.vector.quantize_mx(out=z_w[b][:, cols].bitcast(FP8X4), scales=z_s[b][:, cols], in_=rounded[:])
 
         y_banks = [(0, 1), (2, 3), (6, 7), (0, 1)]
@@ -301,7 +355,7 @@ def tile_list_trench_dispute_features_kernel(
             for j in range(PACK):
                 nc.tensor.matmul_mx(
                     out=banks[y_banks[quarter][j // 2]][:, (j % 2) * QUARTER : (j % 2 + 1) * QUARTER],
-                    lhsT=w3_w[:, b * N + j * P : b * N + (j + 1) * P].bitcast(FP8X4),
+                    lhsT=w3_w[b][:, j * P : (j + 1) * P].bitcast(FP8X4),
                     lhsT_scale=w3_s[:, b * N + j * P : b * N + (j + 1) * P],
                     rhs=z_w[b][:, cols].bitcast(FP8X4),
                     rhs_scale=z_s[b][:, cols],
@@ -314,7 +368,7 @@ def tile_list_trench_dispute_features_kernel(
 
         def finish(quarter):
             cols = slice(quarter * QUARTER, (quarter + 1) * QUARTER)
-            y_all = keep.tile([P, PACK * QUARTER], F32, name=f"y_all{quarter}")
+            y_all = ring.tile([P, PACK * QUARTER], F32, name="cons_rows", bufs=ROW_TILES)
             for i, bank in enumerate(y_banks[quarter]):
                 copy = nc.vector.tensor_copy if quarter == 0 and i == 1 else nc.scalar.copy
                 copy(y_all[:, i * BANK : (i + 1) * BANK], banks[bank][:])
@@ -327,43 +381,98 @@ def tile_list_trench_dispute_features_kernel(
             nc.vector.quantize_mx(out=y_w[:, cols].bitcast(FP8X4), scales=y_s[:, cols], in_=y_rounded[:])
 
         load_w2(0)
-        nc.sync.dma_start(out=gain2[:], in_=wg2)
+        nc.sync.dma_start(out=gain["evidence"], in_=wg2)
         load_w2(1)
-        for c in range(4):
-            if c + 2 < len(W2_CHUNKS):
-                load_w2(c + 2)
+        load_cons(0)
+        load_w2(2)
+        load_w2(3)
+        for c in range(1, ROW_TILES):
             load_cons(c)
+
+        new_pair(0, 1)
+        first_features()
+        product(1, 1)
+        product(2, 0)
+        gained_step(1, 1)
+        nc.scalar.copy(raw_features[:], banks[0][:])
+        scatter(0)
+        round_w2(W2_CALLS[0])
+        new_pair(2, 5)
+        nc.gpsimd.tensor_tensor(h[2], raw_features[:], gain["claims"], MULT)
+        scatter(1)
+        round_w2(W2_CALLS[1])
+        quantize_w2(W2_CALLS[0])
+        product(3, 1)
+        product(4, 0)
+        scatter(2)
+        new_pair(3, 4)
+        gained_step(3, 1)
+        product(5, 1)
+        gained_step(4, 0)
+        gained_step(5, 1)
+        transposes(0)
+        squares(0)
+        scatter(3)
+        round_w2(W2_CALLS[2])
+        quantize_w2(W2_CALLS[1])
+        product(6, 0)
+        product(7, 1)
+        scatter(4)
+        gained_pair(3)
+        for k in (1, 2, 3):
+            transposes(k)
+            if k == 2:
+                product(8, 0)
+                product(9, 1)
+            squares(k)
         load_w3(0)
         load_w3(1)
-
-        first_features()
-        features(1)
-        for chunks in W2_CALLS:
-            quantize_w2(chunks)
-        for k in range(2, AHEAD):
-            features(k)
-        for k, (kind, c) in enumerate(steps):
-            if k + AHEAD < len(steps):
-                features(k + AHEAD)
-            scatter(k)
-            if kind == "claims" and c >= 2:
+        difference(0, slice(0, 16))
+        transposes(4)
+        scatter(5)
+        quantize_w2(W2_CALLS[2])
+        for pair in range(3, pairs):
+            first, second = 2 * pair, 2 * pair + 1
+            if pair == W3_AFTER_PAIR + PASSES:
+                quantize_w3(0, "w3_first")
+            if pair == pairs - 1:
+                quantize_z(0)
+            scatter(first)
+            if pair + 1 < pairs:
+                gained_pair(pair + 1)
+            transposes(first - 1)
+            if pair + 2 < pairs:
+                product(2 * pair + 4, 0)
+                product(2 * pair + 5, 1)
+            if pair < pairs - 1:
+                squares(first - 2)
+                squares(first - 1)
+                difference(pair - 2, slice(0, 16))
+            else:
+                squares(first - 1)
                 for f in range(HALVES):
-                    difference(c - 2, slice(8 * f, 8 * f + 8))
-                if c + 2 < ROW_TILES:
-                    load_cons(c + 2)
-            if k == len(steps) - 2:
-                for quarter in (0, 1):
-                    y_pass(0, quarter)
-            if kind == "evidence" and c == W3_AFTER_EVIDENCE:
-                quantize_w3()
-            if kind == "evidence" and c == PACK:
-                quantize_z(0, list(range(QUARTERS)), [4, 5, 4, 5])
+                    difference(pair - 2, slice(8 * f, 8 * f + 8))
+                squares(first - 2)
+            if pair == pairs - 2:
+                turn_z(0, list(range(QUARTERS)), [6, 7, 4, 5])
+            if pair - W3_AFTER_PAIR in range(PASSES):
+                round_w3(pair - W3_AFTER_PAIR)
+            scatter(second)
+            transposes(first)
+        last = len(steps) - 1
+        squares(last - 1)
+        for quarter in (0, 1):
+            y_pass(0, quarter)
+        transposes(last)
+        squares(last)
 
         difference(ROW_TILES - 2, slice(0, 16))
+        quantize_w3(1, "slot_c")
         for quarter in range(QUARTERS):
             last_difference(quarter)
         for quarter in range(QUARTERS):
-            quantize_z(1, [quarter], [(6, 7, 4, 5)[quarter]])
+            turn_z(1, [quarter], [(6, 7, 4, 5)[quarter]])
+            quantize_z(1)
         for quarter in range(QUARTERS):
             if quarter >= 2:
                 y_pass(0, quarter)

@@ -31,10 +31,11 @@ LIST_COLUMNS = S // 16
 W2_CHUNK = 2
 W2_CALLS = [[0], [1], [2, 3]]
 PAGES = {"claims": 3, "evidence": 2}
-PAIR_SLOTS = {0: "d", 2: "b", 3: "a", 6: "c", 8: "b", 10: "c", 12: "b", 14: "c"}
-W2_SLOTS = {0: "b", 1: "a", 3: "c"}
+PAIR_SLOTS = {0: "d", 2: "b", 3: "a", 7: "e", 8: "c", 10: "a", 12: "b"}
+FUSED_STEPS = 6
+W2_SLOTS = {(0, 1): "b", (1, 1): "a", (3, 0): "e", (3, 1): "c"}
 LEAD = 2
-W3_AFTER_PAIR = 3
+W3_AFTER_PAIR = 4
 FIRST_PARTS = 2
 
 
@@ -68,7 +69,7 @@ def tile_list_trench_dispute_features_kernel(
         w2_w = keep.tile([P, PASSES * H], U32, name="w2_w", align_bytes=64)
         w2_s = keep.tile([P, PASSES * H], U8, name="w2_s", align_bytes=64)
         w3_s = keep.tile([P, PASSES * N], U8, name="w3_s", align_bytes=64)
-        z_t = [keep.tile([P, PACK * T2], BF16, name=f"z_t{b}") for b in range(PASSES)]
+        z_t = {1: keep.tile([P, PACK * T2], BF16, name="z_t1")}
         z_w = [keep.tile([P, T2], U32, name=f"z_w{b}", align_bytes=64) for b in range(PASSES)]
         z_s = [keep.tile([P, T2], U8, name=f"z_s{b}", align_bytes=64) for b in range(PASSES)]
         y_w = keep.tile([P, T2], U32, name="y_w", align_bytes=64)
@@ -122,10 +123,10 @@ def tile_list_trench_dispute_features_kernel(
         def load_w2(g):
             first, tiles = g * W2_CHUNK, W2_CHUNK
             for a in range(PASSES):
-                if a == PASSES - 1 and g in W2_SLOTS:
-                    raw = ring.tile([P, PACK * tiles * P], F32, name="slot_" + W2_SLOTS[g], bufs=1, align_bytes=64)
+                if (g, a) in W2_SLOTS:
+                    raw = ring.tile([P, PACK * tiles * P], F32, name="slot_" + W2_SLOTS[g, a], bufs=1, align_bytes=64)
                 else:
-                    raw = ring.tile([P, PACK * tiles * P], F32, name="w2_raw", bufs=5)
+                    raw = ring.tile([P, PACK * tiles * P], F32, name="w2_raw", bufs=4)
                 rows = w2[a * K_PASS : (a + 1) * K_PASS, first * P : (first + tiles) * P]
                 nc.sync.dma_start(
                     out=raw[:].rearrange("p (j w) -> p j w", j=PACK), in_=rows.rearrange("(p j) w -> p j w", j=PACK)
@@ -145,15 +146,15 @@ def tile_list_trench_dispute_features_kernel(
             nc.sync.dma_start(out=rows[:], in_=cons[c * P : (c + 1) * P, :])
             cons_rows[c] = rows
 
-        def rounded_tile(columns):
-            return ring.tile([P, PACK * columns], BF16, name="rounded", bufs=3, align_bytes=64)
+        def rounded_tile(columns, name="rounded"):
+            return ring.tile([P, PACK * columns], BF16, name=name, bufs=1 if name != "rounded" else 3, align_bytes=64)
 
         w2_rounded = {}
 
         def round_w2(chunks):
             first = PASSES * P * W2_CHUNK * chunks[0]
             columns = PASSES * P * W2_CHUNK * len(chunks)
-            rounded = rounded_tile(columns)
+            rounded = rounded_tile(columns, "rounded" if len(chunks) == 1 else "late_w2")
             for g in chunks:
                 for a in range(PASSES):
                     width = PACK * P * W2_CHUNK
@@ -168,10 +169,14 @@ def tile_list_trench_dispute_features_kernel(
             rounded, cols = w2_rounded[chunks[0]]
             nc.vector.quantize_mx(out=w2_w[:, cols].bitcast(FP8X4), scales=w2_s[:, cols], in_=rounded[:])
 
-        w3_rounded, w3_w = {}, {}
+        w3_rounded, w3_w, first_pass = {}, {}, []
 
         def round_w3(b):
-            rounded = ring.tile([P, PACK * N], BF16, name="w3_rounded", bufs=PASSES, align_bytes=64)
+            if b == 0:
+                first_pass.append(rounded_tile(T2 + N, "first_pass"))
+                rounded = first_pass[0][:, PACK * T2 :]
+            else:
+                rounded = rounded_tile(N, "slot_e")
             w3_rounded[b] = rounded
             dst = rounded[:].rearrange("p (s m j) -> p m j s", s=PACK, j=PACK)
             for half in range(2):
@@ -215,7 +220,7 @@ def tile_list_trench_dispute_features_kernel(
                             start=(a == 0 and u == 0),
                             stop=(a == PASSES - 1 and u == width // P - 1),
                         )
-                nc.vector.tensor_tensor(h[0][:, entries(part)], bank[:, 0:width], gains[:, entries(part)], MULT)
+                nc.scalar.copy(h[0][:, entries(part)], bank[:, 0:width])
 
         def product(k, bank):
             kind, c = steps[k]
@@ -232,26 +237,21 @@ def tile_list_trench_dispute_features_kernel(
                 )
 
         h = {}
-        raw_features = keep.tile([P, S], F32, name="raw_features")
 
         def new_pair(first, second):
             both = ring.tile([P, 2 * S], F32, name="slot_" + PAIR_SLOTS[first], bufs=1, align_bytes=64)
             h[first], h[second] = both[:, 0:S], both[:, S : 2 * S]
             return both
 
-        def gained_step(k, bank):
-            nc.scalar.copy(h[k], banks[bank][:])
-            nc.gpsimd.tensor_tensor(h[k], h[k], gain[steps[k][0]], MULT)
-
-        def gained_pair(pair):
+        def copied_pair(pair):
             both = new_pair(2 * pair, 2 * pair + 1)
-            nc.scalar.copy(h[2 * pair], banks[0][:])
-            nc.scalar.copy(h[2 * pair + 1], banks[1][:])
-            if steps[2 * pair][0] == "evidence":
-                rows = both[:].rearrange("p (s j) -> p s j", s=2)
-                nc.gpsimd.tensor_tensor(rows, rows, gain["evidence"].unsqueeze(1).to_broadcast([P, 2, S]), MULT)
-            else:
-                nc.gpsimd.tensor_tensor(both[:], both[:], gains[:], MULT)
+            nc.scalar.copy(h[2 * pair], banks[6][:])
+            nc.scalar.copy(h[2 * pair + 1], banks[7][:])
+            return both[:]
+
+        def gain_pair(pair, result, both):
+            nc.gpsimd.tensor_tensor(result, both, gains[:], MULT)
+            h[2 * pair], h[2 * pair + 1] = result[:, :S], result[:, S:]
 
         def last_difference(quarter):
             c = ROW_TILES - 1
@@ -265,7 +265,7 @@ def tile_list_trench_dispute_features_kernel(
 
         def page_banks(k):
             kind, c = steps[k]
-            first = {1: 4, ROW_TILES - 1: 6}.get(c, 2) if kind == "claims" else {ROW_TILES - 2: 2}.get(c, 4)
+            first = {1: 4, ROW_TILES - 1: 0}.get(c, 2) if kind == "claims" else {ROW_TILES - 2: 6}.get(c, 4)
             return banks[first : first + HALVES]
 
         def transposes(k):
@@ -289,10 +289,10 @@ def tile_list_trench_dispute_features_kernel(
         def squares(k):
             kind, c = steps[k]
             if kind == "claims":
-                result = ring.tile([P, T2], F32, name="claim_sq", bufs=LEAD + 2)
+                result = ring.tile([P, T2], F32, name="claim_sq", bufs=LEAD + 3)
                 claim_sq[c] = result
             else:
-                result = ring.tile([P, T2], F32, name="evid_sq", bufs=2)
+                result = ring.tile([P, T2], F32, name="evid_sq", bufs=3)
                 evid_sq[c] = result
             for f, bank in enumerate(page_banks(k)):
                 nc.scalar.activation(
@@ -305,15 +305,19 @@ def tile_list_trench_dispute_features_kernel(
 
         def scatter(k):
             kind, c = steps[k]
+            if kind == "claims":
+                page, idx = claim_pages[c % len(claim_pages)], idx_claims
+            else:
+                page, idx = evid_pages[c % len(evid_pages)], idx_evid
             if k == 0:
                 for part in range(FIRST_PARTS):
-                    nc.vector.tensor_copy(
-                        claim_pages[0][:].indirect(idx_claims[:, list_columns(part)]), h[0][:, entries(part)]
+                    nc.vector.tensor_tensor(
+                        page[:].indirect(idx[:, list_columns(part)]), h[0][:, entries(part)], gains[:, entries(part)], MULT
                     )
-            elif kind == "claims":
-                nc.vector.tensor_copy(claim_pages[c % len(claim_pages)][:].indirect(idx_claims[:]), h[k])
+            elif k < FUSED_STEPS:
+                nc.vector.tensor_tensor(page[:].indirect(idx[:]), h[k], gain[kind], MULT)
             else:
-                nc.vector.tensor_copy(evid_pages[c % len(evid_pages)][:].indirect(idx_evid[:]), h[k])
+                nc.vector.tensor_copy(page[:].indirect(idx[:]), h[k])
 
         def difference(c, groups):
             b, quad = divmod(c, PACK)
@@ -328,7 +332,7 @@ def tile_list_trench_dispute_features_kernel(
 
         def turn_z(b, quarters, turn_banks):
             words = z_t[b][:].bitcast(F32)
-            rounded = rounded_tile(len(quarters) * QUARTER)
+            rounded = first_pass[0][:, : PACK * T2] if b == 0 else rounded_tile(QUARTER)
             for i, quarter in enumerate(quarters):
                 bank = banks[turn_banks[i]]
                 f, pair = divmod(quarter, 2)
@@ -389,16 +393,16 @@ def tile_list_trench_dispute_features_kernel(
         for c in range(1, ROW_TILES):
             load_cons(c)
 
+        last = len(steps) - 1
         new_pair(0, 1)
         first_features()
         product(1, 1)
         product(2, 0)
-        gained_step(1, 1)
-        nc.scalar.copy(raw_features[:], banks[0][:])
+        nc.scalar.copy(h[1], banks[1][:])
         scatter(0)
         round_w2(W2_CALLS[0])
         new_pair(2, 5)
-        nc.gpsimd.tensor_tensor(h[2], raw_features[:], gain["claims"], MULT)
+        nc.scalar.copy(h[2], banks[0][:])
         scatter(1)
         round_w2(W2_CALLS[1])
         quantize_w2(W2_CALLS[0])
@@ -406,60 +410,72 @@ def tile_list_trench_dispute_features_kernel(
         product(4, 0)
         scatter(2)
         new_pair(3, 4)
-        gained_step(3, 1)
+        nc.scalar.copy(h[3], banks[1][:])
         product(5, 1)
-        gained_step(4, 0)
-        gained_step(5, 1)
+        nc.scalar.copy(h[4], banks[0][:])
+        nc.scalar.copy(h[5], banks[1][:])
+        quantize_w2(W2_CALLS[1])
         transposes(0)
         squares(0)
         scatter(3)
         round_w2(W2_CALLS[2])
-        quantize_w2(W2_CALLS[1])
         product(6, 0)
         product(7, 1)
         scatter(4)
-        gained_pair(3)
+        new_pair(7, last)
+        nc.scalar.copy(h[7], banks[1][:])
+        product(8, 6)
+        product(9, 7)
+        waiting_pair = copied_pair(4)
         for k in (1, 2, 3):
             transposes(k)
-            if k == 2:
-                product(8, 0)
-                product(9, 1)
             squares(k)
         load_w3(0)
         load_w3(1)
-        difference(0, slice(0, 16))
         transposes(4)
         scatter(5)
         quantize_w2(W2_CALLS[2])
+        after_w2 = rounded_tile(T2 + 2 * S, "late_w2")
+        z_t[0] = after_w2[:, : PACK * T2]
+        gained = after_w2[:, PACK * T2 :].bitcast(F32)
+        nc.vector.tensor_tensor(gained[:, :S], banks[0][:], gain["claims"], MULT)
+        nc.gpsimd.tensor_tensor(gained[:, S : 2 * S], h[7], gain["evidence"], MULT)
+        h[6], h[7] = gained[:, :S], gained[:, S : 2 * S]
+        gain_pair(4, gained[:, 2 * S :], waiting_pair)
         for pair in range(3, pairs):
             first, second = 2 * pair, 2 * pair + 1
-            if pair == W3_AFTER_PAIR + PASSES:
-                quantize_w3(0, "w3_first")
             if pair == pairs - 1:
+                quantize_w3(0, "slot_b")
                 quantize_z(0)
+                gained = ring.tile([P, 2 * S], F32, name="first_pass", bufs=1, align_bytes=64)
+                nc.vector.tensor_tensor(gained[:, :S], banks[6][:], gain["evidence"], MULT)
+                nc.gpsimd.tensor_tensor(gained[:, S:], h[last], gain["evidence"], MULT)
+                h[first], h[last] = gained[:, :S], gained[:, S:]
             scatter(first)
-            if pair + 1 < pairs:
-                gained_pair(pair + 1)
-            transposes(first - 1)
             if pair + 2 < pairs:
-                product(2 * pair + 4, 0)
-                product(2 * pair + 5, 1)
-            if pair < pairs - 1:
-                squares(first - 2)
-                squares(first - 1)
-                difference(pair - 2, slice(0, 16))
-            else:
-                squares(first - 1)
-                for f in range(HALVES):
-                    difference(pair - 2, slice(8 * f, 8 * f + 8))
-                squares(first - 2)
+                product(2 * pair + 4, 6)
+                product(2 * pair + 5, 7)
+            if pair + 3 < pairs:
+                both = copied_pair(pair + 2)
+                gain_pair(pair + 2, both, both)
+            if pair + 3 == pairs:
+                nc.scalar.copy(h[last], banks[7][:])
+            if pair == 3:
+                difference(0, slice(0, 16))
+            transposes(first - 1)
+            for k in (first - 1,) if pair == pairs - 1 else (first - 2, first - 1):
+                squares(k)
+            difference(pair - 2, slice(0, 16))
             if pair == pairs - 2:
-                turn_z(0, list(range(QUARTERS)), [6, 7, 4, 5])
-            if pair - W3_AFTER_PAIR in range(PASSES):
-                round_w3(pair - W3_AFTER_PAIR)
+                turn_z(0, list(range(QUARTERS)), [0, 1, 4, 5])
+            if pair == W3_AFTER_PAIR:
+                round_w3(0)
+            if pair == pairs - 1:
+                round_w3(1)
             scatter(second)
             transposes(first)
-        last = len(steps) - 1
+            if pair == pairs - 2:
+                squares(first)
         squares(last - 1)
         for quarter in (0, 1):
             y_pass(0, quarter)
@@ -467,7 +483,7 @@ def tile_list_trench_dispute_features_kernel(
         squares(last)
 
         difference(ROW_TILES - 2, slice(0, 16))
-        quantize_w3(1, "slot_c")
+        quantize_w3(1, "first_pass")
         for quarter in range(QUARTERS):
             last_difference(quarter)
         for quarter in range(QUARTERS):

@@ -126,7 +126,7 @@ def tile_list_trench_dispute_features_kernel(
                 if (g, a) in W2_SLOTS:
                     raw = ring.tile([P, PACK * tiles * P], F32, name="slot_" + W2_SLOTS[g, a], bufs=1, align_bytes=64)
                 else:
-                    raw = ring.tile([P, PACK * tiles * P], F32, name="w2_raw", bufs=4)
+                    raw = ring.tile([P, PACK * tiles * P], F32, name="w2_raw", bufs=4, align_bytes=64)
                 rows = w2[a * K_PASS : (a + 1) * K_PASS, first * P : (first + tiles) * P]
                 nc.sync.dma_start(
                     out=raw[:].rearrange("p (j w) -> p j w", j=PACK), in_=rows.rearrange("(p j) w -> p j w", j=PACK)
@@ -176,7 +176,7 @@ def tile_list_trench_dispute_features_kernel(
                 first_pass.append(rounded_tile(T2 + N, "first_pass"))
                 rounded = first_pass[0][:, PACK * T2 :]
             else:
-                rounded = rounded_tile(N, "slot_e")
+                rounded = rounded_tile(N, "w3_second")
             w3_rounded[b] = rounded
             dst = rounded[:].rearrange("p (s m j) -> p m j s", s=PACK, j=PACK)
             for half in range(2):
@@ -377,7 +377,7 @@ def tile_list_trench_dispute_features_kernel(
                 copy = nc.vector.tensor_copy if quarter == 0 and i == 1 else nc.scalar.copy
                 copy(y_all[:, i * BANK : (i + 1) * BANK], banks[bank][:])
             nc.sync.dma_start(out=y_rows[:, :, cols], in_=y_all[:].rearrange("p (j t) -> p j t", j=PACK))
-            y_rounded = keep.tile([P, PACK * QUARTER], BF16, name=f"y_rounded{quarter}", align_bytes=64)
+            y_rounded = ring.tile([P, PACK * QUARTER], BF16, name="w2_raw", bufs=4, align_bytes=64)
             nc.vector.tensor_copy(
                 y_rounded[:].rearrange("p (c i j) -> p c j i", i=4, j=PACK),
                 y_all[:].rearrange("p (j c i) -> p c j i", j=PACK, i=4),
@@ -468,10 +468,8 @@ def tile_list_trench_dispute_features_kernel(
             difference(pair - 2, slice(0, 16))
             if pair == pairs - 2:
                 turn_z(0, list(range(QUARTERS)), [0, 1, 4, 5])
-            if pair == W3_AFTER_PAIR:
-                round_w3(0)
-            if pair == pairs - 1:
-                round_w3(1)
+            if pair - W3_AFTER_PAIR in range(PASSES):
+                round_w3(pair - W3_AFTER_PAIR)
             scatter(second)
             transposes(first)
             if pair == pairs - 2:

@@ -31,7 +31,7 @@ LIST_COLUMNS = S // 16
 W2_CHUNK = 2
 W2_CALLS = [[0], [1], [2, 3]]
 PAGES = {"claims": 3, "evidence": 2}
-PAIR_SLOTS = {0: "d", 2: "b", 3: "a", 7: "e", 8: "c", 10: "a", 12: "b"}
+PAIR_SLOTS = {0: "d", 2: "b", 3: "a", 7: "e", 9: "c", 11: "a", 12: "b"}
 FUSED_STEPS = 6
 W2_SLOTS = {(0, 1): "b", (1, 1): "a", (3, 0): "e", (3, 1): "c"}
 LEAD = 2
@@ -193,7 +193,8 @@ def tile_list_trench_dispute_features_kernel(
         for c in range(ROW_TILES):
             steps.extend([("claims", c + LEAD)] if c + LEAD < ROW_TILES else [])
             steps.append(("evidence", c))
-        steps[4], steps[5] = steps[5], steps[4]
+        for k in (4, 8, 10):
+            steps[k], steps[k + 1] = steps[k + 1], steps[k]
         pairs = len(steps) // 2
 
         def stationary(kind, c, a):
@@ -243,15 +244,19 @@ def tile_list_trench_dispute_features_kernel(
             h[first], h[second] = both[:, 0:S], both[:, S : 2 * S]
             return both
 
+        def claims_first(pair):
+            return sorted((2 * pair, 2 * pair + 1), key=lambda k: steps[k][0])
+
         def copied_pair(pair):
-            both = new_pair(2 * pair, 2 * pair + 1)
+            both = new_pair(*claims_first(pair))
             nc.scalar.copy(h[2 * pair], banks[6][:])
             nc.scalar.copy(h[2 * pair + 1], banks[7][:])
             return both[:]
 
         def gain_pair(pair, result, both):
             nc.gpsimd.tensor_tensor(result, both, gains[:], MULT)
-            h[2 * pair], h[2 * pair + 1] = result[:, :S], result[:, S:]
+            first, second = claims_first(pair)
+            h[first], h[second] = result[:, :S], result[:, S:]
 
         def last_difference(quarter):
             c = ROW_TILES - 1
@@ -442,38 +447,60 @@ def tile_list_trench_dispute_features_kernel(
         nc.gpsimd.tensor_tensor(gained[:, S : 2 * S], h[7], gain["evidence"], MULT)
         h[6], h[7] = gained[:, :S], gained[:, S : 2 * S]
         gain_pair(4, gained[:, 2 * S :], waiting_pair)
-        for pair in range(3, pairs):
-            first, second = 2 * pair, 2 * pair + 1
-            if pair == pairs - 1:
-                quantize_w3(0, "slot_b")
-                quantize_z(0)
-                gained = ring.tile([P, 2 * S], F32, name="first_pass", bufs=1, align_bytes=64)
-                nc.vector.tensor_tensor(gained[:, :S], banks[6][:], gain["evidence"], MULT)
-                nc.gpsimd.tensor_tensor(gained[:, S:], h[last], gain["evidence"], MULT)
-                h[first], h[last] = gained[:, :S], gained[:, S:]
-            scatter(first)
-            if pair + 2 < pairs:
-                product(2 * pair + 4, 6)
-                product(2 * pair + 5, 7)
-            if pair + 3 < pairs:
-                both = copied_pair(pair + 2)
-                gain_pair(pair + 2, both, both)
-            if pair + 3 == pairs:
-                nc.scalar.copy(h[last], banks[7][:])
-            if pair == 3:
-                difference(0, slice(0, 16))
-            transposes(first - 1)
-            for k in (first - 1,) if pair == pairs - 1 else (first - 2, first - 1):
-                squares(k)
-            difference(pair - 2, slice(0, 16))
-            if pair == pairs - 2:
-                turn_z(0, list(range(QUARTERS)), [0, 1, 4, 5])
-            if pair - W3_AFTER_PAIR in range(PASSES):
-                round_w3(pair - W3_AFTER_PAIR)
-            scatter(second)
-            transposes(first)
-            if pair == pairs - 2:
-                squares(first)
+
+        def squared(k):
+            transposes(k)
+            squares(k)
+
+        def features(pair):
+            product(2 * pair, 6)
+            product(2 * pair + 1, 7)
+            both = copied_pair(pair)
+            gain_pair(pair, both, both)
+
+        whole = slice(0, 16)
+        scatter(6)
+        features(5)
+        difference(0, whole)
+        transposes(5)
+        squares(4)
+        squares(5)
+        difference(1, whole)
+        scatter(7)
+        squared(6)
+        scatter(8)
+        features(6)
+        squared(7)
+        difference(2, whole)
+        round_w3(0)
+        scatter(9)
+        squared(8)
+        difference(3, whole)
+        product(last - 1, 6)
+        product(last, 7)
+        nc.scalar.copy(h[last], banks[7][:])
+        scatter(10)
+        squared(9)
+        round_w3(1)
+        scatter(11)
+        squared(10)
+        difference(4, whole)
+        turn_z(0, list(range(QUARTERS)), [0, 1, 4, 5])
+        scatter(12)
+        squared(11)
+        scatter(13)
+        squared(12)
+        quantize_w3(0, "slot_b")
+        quantize_z(0)
+        gained = ring.tile([P, 2 * S], F32, name="first_pass", bufs=1, align_bytes=64)
+        nc.vector.tensor_tensor(gained[:, :S], banks[6][:], gain["evidence"], MULT)
+        nc.gpsimd.tensor_tensor(gained[:, S:], h[last], gain["evidence"], MULT)
+        h[last - 1], h[last] = gained[:, :S], gained[:, S:]
+        scatter(last - 1)
+        squared(13)
+        difference(5, whole)
+        scatter(last)
+        transposes(last - 1)
         squares(last - 1)
         for quarter in (0, 1):
             y_pass(0, quarter)

@@ -31,7 +31,7 @@ LIST_COLUMNS = S // 16
 W2_CHUNK = 2
 W2_CALLS = [[0], [1], [2, 3]]
 PAGES = {"claims": 3, "evidence": 2}
-PAIR_SLOTS = {0: "d", 2: "b", 3: "a", 7: "e", 9: "c", 11: "a", 12: "b"}
+PAIR_SLOTS = {0: "d", 2: "b", 3: "a", 7: "e", 9: "c", 11: "a", 12: "b", 14: "d"}
 FUSED_STEPS = 6
 W2_SLOTS = {(0, 1): "b", (1, 1): "a", (3, 0): "e", (3, 1): "c"}
 LEAD = 2
@@ -70,7 +70,7 @@ def tile_list_trench_dispute_features_kernel(
         w2_s = keep.tile([P, PASSES * H], U8, name="w2_s", align_bytes=64)
         w3_s = keep.tile([P, PASSES * N], U8, name="w3_s", align_bytes=64)
         z_t = {1: keep.tile([P, PACK * T2], BF16, name="z_t1")}
-        z_w = [keep.tile([P, T2], U32, name=f"z_w{b}", align_bytes=64) for b in range(PASSES)]
+        z_w = {1: keep.tile([P, T2], U32, name="z_w1", align_bytes=64)}
         z_s = [keep.tile([P, T2], U8, name=f"z_s{b}", align_bytes=64) for b in range(PASSES)]
         y_w = keep.tile([P, T2], U32, name="y_w", align_bytes=64)
         y_s = keep.tile([P, T2], U8, name="y_s", align_bytes=64)
@@ -183,8 +183,8 @@ def tile_list_trench_dispute_features_kernel(
                 src = w3_raw[b, half][:].rearrange("p (j m s) -> p m j s", j=PACK, s=PACK)
                 nc.scalar.copy(dst[:, half * P // 2 : (half + 1) * P // 2], src)
 
-        def quantize_w3(b, tile_name):
-            w3_w[b] = ring.tile([P, N], U32, name=tile_name, bufs=1, align_bytes=64)
+        def quantize_w3(b, codes):
+            w3_w[b] = codes
             nc.vector.quantize_mx(
                 out=w3_w[b][:].bitcast(FP8X4), scales=w3_s[:, b * N : (b + 1) * N], in_=w3_rounded[b][:]
             )
@@ -319,7 +319,7 @@ def tile_list_trench_dispute_features_kernel(
                     nc.vector.tensor_tensor(
                         page[:].indirect(idx[:, list_columns(part)]), h[0][:, entries(part)], gains[:, entries(part)], MULT
                     )
-            elif k < FUSED_STEPS:
+            elif k < FUSED_STEPS or k == len(steps) - 2:
                 nc.vector.tensor_tensor(page[:].indirect(idx[:]), h[k], gain[kind], MULT)
             else:
                 nc.vector.tensor_copy(page[:].indirect(idx[:]), h[k])
@@ -427,7 +427,7 @@ def tile_list_trench_dispute_features_kernel(
         product(6, 0)
         product(7, 1)
         scatter(4)
-        new_pair(7, last)
+        h[7] = ring.tile([P, S], F32, name="slot_e", bufs=1, align_bytes=64)[:]
         nc.scalar.copy(h[7], banks[1][:])
         product(8, 6)
         product(9, 7)
@@ -476,26 +476,27 @@ def tile_list_trench_dispute_features_kernel(
         scatter(9)
         squared(8)
         difference(3, whole)
-        product(last - 1, 6)
-        product(last, 7)
-        nc.scalar.copy(h[last], banks[7][:])
+        product(last, 6)
+        new_pair(last - 1, last)
+        nc.scalar.copy(h[last], banks[6][:])
         scatter(10)
         squared(9)
         round_w3(1)
         scatter(11)
         squared(10)
         difference(4, whole)
+        nc.gpsimd.tensor_tensor(h[last], h[last], gain["evidence"], MULT)
         turn_z(0, list(range(QUARTERS)), [0, 1, 4, 5])
+        product(last - 1, 5)
+        nc.scalar.copy(h[last - 1], banks[5][:])
         scatter(12)
         squared(11)
         scatter(13)
         squared(12)
-        quantize_w3(0, "slot_b")
+        first_codes = ring.tile([P, T2 + N], U32, name="slot_b", bufs=1, align_bytes=64)
+        z_w[0] = first_codes[:, :T2]
+        quantize_w3(0, first_codes[:, T2:])
         quantize_z(0)
-        gained = ring.tile([P, 2 * S], F32, name="first_pass", bufs=1, align_bytes=64)
-        nc.vector.tensor_tensor(gained[:, :S], banks[6][:], gain["evidence"], MULT)
-        nc.gpsimd.tensor_tensor(gained[:, S:], h[last], gain["evidence"], MULT)
-        h[last - 1], h[last] = gained[:, :S], gained[:, S:]
         scatter(last - 1)
         squared(13)
         difference(5, whole)
@@ -508,7 +509,7 @@ def tile_list_trench_dispute_features_kernel(
         squares(last)
 
         difference(ROW_TILES - 2, slice(0, 16))
-        quantize_w3(1, "first_pass")
+        quantize_w3(1, ring.tile([P, N], U32, name="slot_d", bufs=1, align_bytes=64))
         for quarter in range(QUARTERS):
             last_difference(quarter)
         for quarter in range(QUARTERS):

@@ -221,7 +221,7 @@ def tile_list_trench_dispute_features_kernel(
                             start=(a == 0 and u == 0),
                             stop=(a == PASSES - 1 and u == width // P - 1),
                         )
-                nc.scalar.copy(h[0][:, entries(part)], bank[:, 0:width])
+                nc.vector.tensor_tensor(h[0][:, entries(part)], bank[:, 0:width], gains[:, entries(part)], MULT)
 
         def product(k, bank):
             kind, c = steps[k]
@@ -247,9 +247,9 @@ def tile_list_trench_dispute_features_kernel(
         def claims_first(pair):
             return sorted((2 * pair, 2 * pair + 1), key=lambda k: steps[k][0])
 
-        def copied_pair(pair):
+        def copied_pair(pair, first_bank=6):
             both = new_pair(*claims_first(pair))
-            nc.scalar.copy(h[2 * pair], banks[6][:])
+            nc.scalar.copy(h[2 * pair], banks[first_bank][:])
             nc.scalar.copy(h[2 * pair + 1], banks[7][:])
             return both[:]
 
@@ -270,7 +270,7 @@ def tile_list_trench_dispute_features_kernel(
 
         def page_banks(k):
             kind, c = steps[k]
-            first = {1: 4, ROW_TILES - 1: 0}.get(c, 2) if kind == "claims" else {ROW_TILES - 2: 6}.get(c, 4)
+            first = {1: 6, ROW_TILES - 1: 0}.get(c, 2) if kind == "claims" else {0: 6, 1: 6, ROW_TILES - 2: 6}.get(c, 4)
             return banks[first : first + HALVES]
 
         def transposes(k):
@@ -316,9 +316,7 @@ def tile_list_trench_dispute_features_kernel(
                 page, idx = evid_pages[c % len(evid_pages)], idx_evid
             if k == 0:
                 for part in range(FIRST_PARTS):
-                    nc.vector.tensor_tensor(
-                        page[:].indirect(idx[:, list_columns(part)]), h[0][:, entries(part)], gains[:, entries(part)], MULT
-                    )
+                    nc.vector.tensor_copy(page[:].indirect(idx[:, list_columns(part)]), h[0][:, entries(part)])
             elif k < FUSED_STEPS or k == len(steps) - 2:
                 nc.vector.tensor_tensor(page[:].indirect(idx[:]), h[k], gain[kind], MULT)
             else:
@@ -401,7 +399,11 @@ def tile_list_trench_dispute_features_kernel(
         last = len(steps) - 1
         new_pair(0, 1)
         first_features()
+        product(6, 0)
         product(1, 1)
+        h[6] = keep.tile([P, S], F32, name="early_features")[:]
+        nc.scalar.copy(h[6], banks[0][:])
+        nc.gpsimd.tensor_tensor(h[6], h[6], gain["claims"], MULT)
         product(2, 0)
         nc.scalar.copy(h[1], banks[1][:])
         scatter(0)
@@ -424,7 +426,6 @@ def tile_list_trench_dispute_features_kernel(
         squares(0)
         scatter(3)
         round_w2(W2_CALLS[2])
-        product(6, 0)
         product(7, 1)
         scatter(4)
         h[7] = ring.tile([P, S], F32, name="slot_e", bufs=1, align_bytes=64)[:]
@@ -432,39 +433,37 @@ def tile_list_trench_dispute_features_kernel(
         product(8, 6)
         product(9, 7)
         waiting_pair = copied_pair(4)
-        for k in (1, 2, 3):
+        for k in (1, 3, 2):
             transposes(k)
             squares(k)
         load_w3(0)
         load_w3(1)
         transposes(4)
         scatter(5)
+        raw_features, h[7] = h[7], ring.tile([P, S], F32, name="slot_b", bufs=1, align_bytes=64)[:]
+        nc.gpsimd.tensor_tensor(h[7], raw_features, gain["evidence"], MULT)
         quantize_w2(W2_CALLS[2])
-        after_w2 = rounded_tile(T2 + 2 * S, "late_w2")
+        after_w2 = rounded_tile(T2 + S, "late_w2")
         z_t[0] = after_w2[:, : PACK * T2]
         gained = after_w2[:, PACK * T2 :].bitcast(F32)
-        nc.vector.tensor_tensor(gained[:, :S], banks[0][:], gain["claims"], MULT)
-        nc.gpsimd.tensor_tensor(gained[:, S : 2 * S], h[7], gain["evidence"], MULT)
-        h[6], h[7] = gained[:, :S], gained[:, S : 2 * S]
-        gain_pair(4, gained[:, 2 * S :], waiting_pair)
+        gain_pair(4, gained, waiting_pair)
 
         def squared(k):
             transposes(k)
             squares(k)
 
-        def features(pair):
-            product(2 * pair, 6)
+        def features(pair, first_bank=6):
+            product(2 * pair, first_bank)
             product(2 * pair + 1, 7)
-            both = copied_pair(pair)
+            both = copied_pair(pair, first_bank)
             gain_pair(pair, both, both)
 
         whole = slice(0, 16)
         scatter(6)
-        features(5)
-        difference(0, whole)
-        transposes(5)
         squares(4)
-        squares(5)
+        difference(0, whole)
+        features(5)
+        squared(5)
         difference(1, whole)
         scatter(7)
         squared(6)

@@ -270,8 +270,10 @@ def tile_list_trench_dispute_features_kernel(
 
         def page_banks(k):
             kind, c = steps[k]
-            first = {1: 6, ROW_TILES - 1: 0}.get(c, 2) if kind == "claims" else {0: 6, 1: 6, ROW_TILES - 2: 6}.get(c, 4)
-            return banks[first : first + HALVES]
+            if k == len(steps) - 2:
+                return [(0, 0, 2), (1, 2, 2), (2, 4, 1), (3, 5, 1), (6, 6, 1), (7, 7, 1)]
+            first = {1: 6, ROW_TILES - 1: 0}.get(c, 2) if kind == "claims" else {0: 6, 1: 6, ROW_TILES - 1: 6}.get(c, 4)
+            return [(first + f, 4 * f, 4) for f in range(HALVES)]
 
         def transposes(k):
             kind, c = steps[k]
@@ -279,12 +281,12 @@ def tile_list_trench_dispute_features_kernel(
                 terms = [cons_rows[c], claim_pages[c % len(claim_pages)]]
             else:
                 terms = [evid_pages[c % len(evid_pages)]]
-            for f, bank in enumerate(page_banks(k)):
-                for u in range(BANK // P):
+            for bank, first, blocks in page_banks(k):
+                for u in range(blocks):
                     for i, term in enumerate(terms):
                         nc.tensor.matmul(
-                            bank[:, u * P : (u + 1) * P],
-                            lhsT=term[:, f * BANK + u * P : f * BANK + (u + 1) * P],
+                            banks[bank][:, u * P : (u + 1) * P],
+                            lhsT=term[:, (first + u) * P : (first + u + 1) * P],
                             rhs=ident[:],
                             is_transpose=True,
                             start=(i == 0),
@@ -296,13 +298,18 @@ def tile_list_trench_dispute_features_kernel(
             if kind == "claims":
                 result = ring.tile([P, T2], F32, name="claim_sq", bufs=LEAD + 3)
                 claim_sq[c] = result
-            else:
+            elif c < ROW_TILES - 1:
                 result = ring.tile([P, T2], F32, name="evid_sq", bufs=3)
                 evid_sq[c] = result
-            for f, bank in enumerate(page_banks(k)):
+            else:
+                result = ring.tile([P, T2], F32, name="slot_c", bufs=1, align_bytes=64)
+                evid_sq[c] = result
+            groups = result[:].rearrange("t (f h u q e) -> t f h u q e", f=HALVES, h=2, u=4, e=2)
+            for bank, first, blocks in page_banks(k):
+                f, u = divmod(first, 4)
                 nc.scalar.activation(
-                    result[:, f * BANK : (f + 1) * BANK].rearrange("t (h u q e) -> t h u q e", h=2, u=4, e=2),
-                    bank[:].rearrange("t (u q h e) -> t h u q e", u=4, h=2, e=2),
+                    groups[:, f, :, u : u + blocks],
+                    banks[bank][:, : blocks * P].rearrange("t (u q h e) -> t h u q e", h=2, e=2, q=32),
                     SQUARE,
                 )
 
@@ -345,7 +352,7 @@ def tile_list_trench_dispute_features_kernel(
                         nc.tensor.transpose(
                             bank[:, (2 * u + h) * P : (2 * u + h + 1) * P], words[:, g * P : (g + 1) * P], ident[:]
                         )
-                (nc.vector.tensor_copy if b == PASSES - 1 and quarter == 1 else nc.scalar.copy)(
+                (nc.vector.tensor_copy if b == PASSES - 1 and quarter == 2 else nc.scalar.copy)(
                     rounded[:].bitcast(F32)[:, i * BANK : (i + 1) * BANK].rearrange("p (u t h) -> p u t h", u=2, h=2),
                     bank[:].rearrange("p (u h t) -> p u t h", u=2, h=2),
                 )
@@ -355,7 +362,7 @@ def tile_list_trench_dispute_features_kernel(
             rounded, cols = z_rounded[b]
             nc.vector.quantize_mx(out=z_w[b][:, cols].bitcast(FP8X4), scales=z_s[b][:, cols], in_=rounded[:])
 
-        y_banks = [(0, 1), (2, 3), (6, 7), (0, 1)]
+        y_banks = [(0, 1), (2, 3), (4, 5), (6, 7)]
 
         def y_pass(b, quarter):
             cols = slice(quarter * QUARTER, (quarter + 1) * QUARTER)
@@ -508,11 +515,11 @@ def tile_list_trench_dispute_features_kernel(
         squares(last)
 
         difference(ROW_TILES - 2, slice(0, 16))
-        quantize_w3(1, ring.tile([P, N], U32, name="slot_d", bufs=1, align_bytes=64))
         for quarter in range(QUARTERS):
             last_difference(quarter)
+        quantize_w3(1, ring.tile([P, N], U32, name="slot_c", bufs=1, align_bytes=64))
         for quarter in range(QUARTERS):
-            turn_z(1, [quarter], [(6, 7, 4, 5)[quarter]])
+            turn_z(1, [quarter], [4 + quarter])
             quantize_z(1)
         for quarter in range(QUARTERS):
             if quarter >= 2:

@@ -23,20 +23,16 @@ PACK = 4
 K_PASS = P * PACK
 PASSES = K // K_PASS
 ROW_TILES = H // P
+LAST = ROW_TILES - 1
 BANK = 512
 HALVES = T2 // BANK
 QUARTER = 256
 QUARTERS = T2 // QUARTER
 LIST_COLUMNS = S // 16
 W2_CHUNK = 2
-W2_CALLS = [[0], [1], [2, 3]]
-PAGES = {"claims": 3, "evidence": 2}
-PAIR_SLOTS = {0: "d", 2: "b", 3: "a", 7: "e", 9: "c", 11: "a", 12: "b", 14: "d"}
-FUSED_STEPS = 6
-W2_SLOTS = {(0, 1): "b", (1, 1): "a", (3, 0): "e", (3, 1): "c"}
-LEAD = 2
-W3_AFTER_PAIR = 4
+W2_CHUNKS = ROW_TILES // W2_CHUNK
 FIRST_PARTS = 2
+CLAIMS, EVIDENCE = 0, 1
 
 
 def tile_list_trench_dispute_features_kernel(
@@ -51,33 +47,37 @@ def tile_list_trench_dispute_features_kernel(
 
         banks = [psum.tile([P, BANK], F32, name=f"bank{i}") for i in range(8)]
 
-        idx_notes = lists.tile([P, LIST_COLUMNS], U16, name="idx_notes")
-        idx_claims = lists.tile([P, LIST_COLUMNS], U16, name="idx_claims")
-        idx_evid = lists.tile([P, LIST_COLUMNS], U16, name="idx_evid")
+        def slot(name, columns, dtype):
+            return ring.tile([P, columns], dtype, name=name, bufs=1, align_bytes=64)
 
-        tab_w = [keep.tile([P, T], U32, name=f"tab_w{a}", align_bytes=64) for a in range(PASSES)]
+        idx_notes = lists.tile([P, LIST_COLUMNS], U16, name="idx_notes")
+        idx_pages = [lists.tile([P, LIST_COLUMNS], U16, name=f"idx_page{kind}") for kind in (CLAIMS, EVIDENCE)]
+
+        tab_w = [slot(f"table{a}", T, U32) for a in range(PASSES)]
         tab_s = keep.tile([P, PASSES * T], U8, name="tab_s", align_bytes=64)
         w1_w = keep.tile([P, PASSES * 2 * H], U8, name="w1_w", align_bytes=64)
         w1_s = keep.tile([P, PASSES * H], U8, name="w1_s", align_bytes=64)
         v_w = [keep.tile([P, S], U32, name=f"v_w{a}", align_bytes=64) for a in range(PASSES)]
         v_s = [keep.tile([P, S], U8, name=f"v_s{a}", align_bytes=64) for a in range(PASSES)]
         gains = keep.tile([P, 2 * S], F32, name="gains")
-        gain = {"claims": gains[:, 0:S], "evidence": gains[:, S : 2 * S]}
+        gain = [gains[:, 0:S], gains[:, S : 2 * S]]
         ident = keep.tile([P, P], F32, name="ident")
-        claim_pages = [keep.tile([P, T2], F32, name=f"claim_page{i}") for i in range(PAGES["claims"])]
-        evid_pages = [keep.tile([P, T2], F32, name=f"evid_page{i}") for i in range(PAGES["evidence"])]
+        pages = [
+            [keep.tile([P, T2], F32, name=f"page{kind}_{i}") for i in range(count)]
+            for kind, count in ((CLAIMS, 3), (EVIDENCE, 2))
+        ]
         w2_w = keep.tile([P, PASSES * H], U32, name="w2_w", align_bytes=64)
         w2_s = keep.tile([P, PASSES * H], U8, name="w2_s", align_bytes=64)
         w3_s = keep.tile([P, PASSES * N], U8, name="w3_s", align_bytes=64)
         z_t = {1: keep.tile([P, PACK * T2], BF16, name="z_t1")}
-        z_w = {1: keep.tile([P, T2], U32, name="z_w1", align_bytes=64)}
         z_s = [keep.tile([P, T2], U8, name=f"z_s{b}", align_bytes=64) for b in range(PASSES)]
+        z_last = keep.tile([P, T2], U32, name="z_last", align_bytes=64)
         y_w = keep.tile([P, T2], U32, name="y_w", align_bytes=64)
         y_s = keep.tile([P, T2], U8, name="y_s", align_bytes=64)
 
-        def load_scale_rows(queue, plane, scales):
+        def load_scale_rows(plane, scales):
             for quad in range(4):
-                queue.dma_start(
+                nc.sync.dma_start(
                     out=plane[32 * quad : 32 * quad + 4, :].bitcast(I32).rearrange("i (a c) -> i a c", a=PASSES),
                     in_=scales[:, 4 * quad : 4 * quad + 4, :].bitcast(I32).rearrange("a i c -> i a c"),
                 )
@@ -91,19 +91,19 @@ def tile_list_trench_dispute_features_kernel(
         nc.gpsimd.memset(w1_s[:].bitcast(I32), 0)
         nc.sync.dma_start(idx_notes[:], offs)
         load_tab_words(0)
-        load_scale_rows(nc.sync, tab_s, tab_scales)
+        load_scale_rows(tab_s, tab_scales)
         load_tab_words(1)
         nc.sync.dma_start(
             out=w1_w[:].bitcast(I32).rearrange("p (a c) -> p a c", a=PASSES),
             in_=w1_words.bitcast(I32).rearrange("a p c -> p a c"),
         )
-        load_scale_rows(nc.sync, w1_s, w1_scales)
-        nc.sync.dma_start(idx_claims[:], offs2)
-        nc.sync.dma_start(out=gain["claims"], in_=wg1)
-        nc.sync.dma_start(idx_evid[:], offs3)
-        nc.vector.memset(claim_pages[0][:].bitcast(I32), 0)
+        load_scale_rows(w1_s, w1_scales)
+        nc.sync.dma_start(idx_pages[CLAIMS][:], offs2)
+        nc.sync.dma_start(out=gain[CLAIMS], in_=wg1)
+        nc.sync.dma_start(idx_pages[EVIDENCE][:], offs3)
+        nc.vector.memset(pages[CLAIMS][0][:].bitcast(I32), 0)
         make_identity(nc, ident[:])
-        for page in claim_pages[1:] + evid_pages:
+        for page in pages[CLAIMS][1:] + pages[EVIDENCE]:
             nc.gpsimd.memset(page[:].bitcast(I32), 0)
 
         def entries(part):
@@ -121,110 +121,86 @@ def tile_list_trench_dispute_features_kernel(
         w2_raw, w3_raw, cons_rows = {}, {}, {}
 
         def load_w2(g):
-            first, tiles = g * W2_CHUNK, W2_CHUNK
+            width = PACK * W2_CHUNK * P
+            both = slot("raw_last", PASSES * width, F32) if g == W2_CHUNKS - 1 else None
             for a in range(PASSES):
-                if (g, a) in W2_SLOTS:
-                    raw = ring.tile([P, PACK * tiles * P], F32, name="slot_" + W2_SLOTS[g, a], bufs=1, align_bytes=64)
-                else:
-                    raw = ring.tile([P, PACK * tiles * P], F32, name="w2_raw", bufs=4, align_bytes=64)
-                rows = w2[a * K_PASS : (a + 1) * K_PASS, first * P : (first + tiles) * P]
+                raw = slot(f"raw{PASSES * g + a}", width, F32) if both is None else both[:, a * width : (a + 1) * width]
+                rows = w2[a * K_PASS : (a + 1) * K_PASS, g * W2_CHUNK * P : (g + 1) * W2_CHUNK * P]
                 nc.sync.dma_start(
                     out=raw[:].rearrange("p (j w) -> p j w", j=PACK), in_=rows.rearrange("(p j) w -> p j w", j=PACK)
                 )
                 w2_raw[g, a] = raw
 
         def load_w3(b):
-            rows = w3[b * K_PASS : (b + 1) * K_PASS, :].rearrange("(p j) n -> p j n", j=PACK)
-            for half in range(2):
-                raw = ring.tile([P, PACK * N // 2], F32, name="cons_rows", bufs=ROW_TILES)
-                cols = slice(half * N // 2, (half + 1) * N // 2)
-                nc.sync.dma_start(out=raw[:].rearrange("p (j n) -> p j n", j=PACK), in_=rows[:, :, cols])
-                w3_raw[b, half] = raw
+            raw = slot(f"table{b}", PACK * N, F32)
+            nc.sync.dma_start(out=raw[:], in_=w3[b * K_PASS : (b + 1) * K_PASS, :].rearrange("(p j) n -> p (j n)", j=PACK))
+            w3_raw[b] = raw
 
         def load_cons(c):
             rows = ring.tile([P, T2], F32, name="cons_rows", bufs=ROW_TILES)
             nc.sync.dma_start(out=rows[:], in_=cons[c * P : (c + 1) * P, :])
             cons_rows[c] = rows
 
-        def rounded_tile(columns, name="rounded"):
-            return ring.tile([P, PACK * columns], BF16, name=name, bufs=1 if name != "rounded" else 3, align_bytes=64)
+        chunk_words = PASSES * W2_CHUNK * P
 
-        w2_rounded = {}
+        def round_w2(g, rounded):
+            for a in range(PASSES):
+                width = PACK * W2_CHUNK * P
+                nc.scalar.copy(
+                    rounded[:, a * width : (a + 1) * width].rearrange("p (c i j) -> p c j i", i=4, j=PACK),
+                    w2_raw[g, a][:].rearrange("p (j c i) -> p c j i", j=PACK, i=4),
+                )
 
-        def round_w2(chunks):
-            first = PASSES * P * W2_CHUNK * chunks[0]
-            columns = PASSES * P * W2_CHUNK * len(chunks)
-            rounded = rounded_tile(columns, "rounded" if len(chunks) == 1 else "late_w2")
-            for g in chunks:
-                for a in range(PASSES):
-                    width = PACK * P * W2_CHUNK
-                    start = PACK * (PASSES * P * W2_CHUNK * g - first) + a * width
-                    nc.scalar.copy(
-                        rounded[:, start : start + width].rearrange("p (c i j) -> p c j i", i=4, j=PACK),
-                        w2_raw[g, a][:].rearrange("p (j c i) -> p c j i", j=PACK, i=4),
-                    )
-            w2_rounded[chunks[0]] = rounded, slice(first, first + columns)
+        def quantize_w2(first, count, rounded):
+            cols = slice(first * chunk_words, (first + count) * chunk_words)
+            nc.vector.quantize_mx(out=w2_w[:, cols].bitcast(FP8X4), scales=w2_s[:, cols], in_=rounded)
 
-        def quantize_w2(chunks):
-            rounded, cols = w2_rounded[chunks[0]]
-            nc.vector.quantize_mx(out=w2_w[:, cols].bitcast(FP8X4), scales=w2_s[:, cols], in_=rounded[:])
+        w3_rounded, w3_w = {}, {}
 
-        w3_rounded, w3_w, first_pass = {}, {}, []
-
-        def round_w3(b):
-            if b == 0:
-                first_pass.append(rounded_tile(T2 + N, "first_pass"))
-                rounded = first_pass[0][:, PACK * T2 :]
-            else:
-                rounded = rounded_tile(N, "w3_second")
+        def round_w3(b, name):
+            rounded = slot(name, PACK * N, BF16)
             w3_rounded[b] = rounded
             dst = rounded[:].rearrange("p (s m j) -> p m j s", s=PACK, j=PACK)
+            src = w3_raw[b][:].rearrange("p (j m s) -> p m j s", j=PACK, s=PACK)
             for half in range(2):
-                src = w3_raw[b, half][:].rearrange("p (j m s) -> p m j s", j=PACK, s=PACK)
-                nc.scalar.copy(dst[:, half * P // 2 : (half + 1) * P // 2], src)
+                rows = slice(half * P // 2, (half + 1) * P // 2)
+                nc.scalar.copy(dst[:, rows], src[:, rows])
 
         def quantize_w3(b, codes):
             w3_w[b] = codes
             nc.vector.quantize_mx(
-                out=w3_w[b][:].bitcast(FP8X4), scales=w3_s[:, b * N : (b + 1) * N], in_=w3_rounded[b][:]
+                out=codes.bitcast(FP8X4), scales=w3_s[:, b * N : (b + 1) * N], in_=w3_rounded[b][:]
             )
 
-        steps = [("claims", c) for c in range(LEAD)]
-        for c in range(ROW_TILES):
-            steps.extend([("claims", c + LEAD)] if c + LEAD < ROW_TILES else [])
-            steps.append(("evidence", c))
-        for k in (4, 8, 10):
-            steps[k], steps[k + 1] = steps[k + 1], steps[k]
-        pairs = len(steps) // 2
-
         def stationary(kind, c, a):
-            if kind == "claims":
+            if kind == CLAIMS:
                 col = a * H + c * P
                 return w1_w[:, 2 * col : 2 * (col + P)].bitcast(FP4X4), w1_s[:, col : col + P]
             g, tile = divmod(c, W2_CHUNK)
             col = ((PASSES * g + a) * W2_CHUNK + tile) * P
             return w2_w[:, col : col + P].bitcast(FP8X4), w2_s[:, col : col + P]
 
+        h = {}
+
         def first_features():
             for part in range(FIRST_PARTS):
                 bank, width = banks[6 + part], S // FIRST_PARTS
                 for a in range(PASSES):
-                    codes, scales = stationary("claims", 0, a)
-                    for u in range(width // P):
-                        cols = slice(part * width + u * P, part * width + (u + 1) * P)
-                        nc.tensor.matmul_mx(
-                            out=bank[:, u * P : (u + 1) * P],
-                            lhsT=codes,
-                            lhsT_scale=scales,
-                            rhs=v_w[a][:, cols].bitcast(FP8X4),
-                            rhs_scale=v_s[a][:, cols],
-                            start=(a == 0 and u == 0),
-                            stop=(a == PASSES - 1 and u == width // P - 1),
-                        )
-                nc.vector.tensor_tensor(h[0][:, entries(part)], bank[:, 0:width], gains[:, entries(part)], MULT)
+                    codes, scales = stationary(CLAIMS, 0, a)
+                    nc.tensor.matmul_mx(
+                        out=bank[:, 0:width],
+                        lhsT=codes,
+                        lhsT_scale=scales,
+                        rhs=v_w[a][:, entries(part)].bitcast(FP8X4),
+                        rhs_scale=v_s[a][:, entries(part)],
+                        start=(a == 0),
+                        stop=(a == PASSES - 1),
+                    )
+                nc.vector.tensor_tensor(
+                    h[CLAIMS, 0][:, entries(part)], bank[:, 0:width], gains[:, entries(part)], MULT
+                )
 
-        def product(k, bank):
-            kind, c = steps[k]
+        def product(kind, c, bank):
             for a in range(PASSES):
                 codes, scales = stationary(kind, c, a)
                 nc.tensor.matmul_mx(
@@ -237,130 +213,112 @@ def tile_list_trench_dispute_features_kernel(
                     stop=(a == PASSES - 1),
                 )
 
-        h = {}
+        def features(kind, c, bank, into):
+            product(kind, c, bank)
+            nc.scalar.copy(into, banks[bank][:])
+            h[kind, c] = into
 
-        def new_pair(first, second):
-            both = ring.tile([P, 2 * S], F32, name="slot_" + PAIR_SLOTS[first], bufs=1, align_bytes=64)
-            h[first], h[second] = both[:, 0:S], both[:, S : 2 * S]
+        def feature_pair(claim, evid, both, pair_banks):
+            features(CLAIMS, claim, pair_banks[0], both[:, :S])
+            features(EVIDENCE, evid, pair_banks[1], both[:, S:])
             return both
 
-        def claims_first(pair):
-            return sorted((2 * pair, 2 * pair + 1), key=lambda k: steps[k][0])
-
-        def copied_pair(pair, first_bank=6):
-            both = new_pair(*claims_first(pair))
-            nc.scalar.copy(h[2 * pair], banks[first_bank][:])
-            nc.scalar.copy(h[2 * pair + 1], banks[7][:])
-            return both[:]
-
-        def gain_pair(pair, result, both):
+        def gain_pair(claim, evid, both, result):
             nc.gpsimd.tensor_tensor(result, both, gains[:], MULT)
-            first, second = claims_first(pair)
-            h[first], h[second] = result[:, :S], result[:, S:]
+            h[CLAIMS, claim], h[EVIDENCE, evid] = result[:, :S], result[:, S:]
 
-        def last_difference(quarter):
-            c = ROW_TILES - 1
-            b, quad = divmod(c, PACK)
-            f, pair = divmod(quarter, 2)
-            views = [
-                tile[:].rearrange("t (f h u x) -> t f h u x", f=2, h=2, u=4)[:, f, :, 2 * pair : 2 * pair + 2, :]
-                for tile in (z_t[b], claim_sq[c], evid_sq[c])
-            ]
-            nc.vector.tensor_tensor(views[0][:, :, :, 64 * quad : 64 * (quad + 1)], views[1], views[2], SUBTRACT)
+        def gain_one(kind, c, result):
+            nc.gpsimd.tensor_tensor(result, h[kind, c], gain[kind], MULT)
+            h[kind, c] = result
 
-        def page_banks(k):
-            kind, c = steps[k]
-            if k == len(steps) - 2:
-                return [(0, 0, 2), (1, 2, 2), (2, 4, 1), (3, 5, 1), (6, 6, 1), (7, 7, 1)]
-            first = {1: 6, ROW_TILES - 1: 0}.get(c, 2) if kind == "claims" else {0: 6, 1: 6, ROW_TILES - 1: 6}.get(c, 4)
-            return [(first + f, 4 * f, 4) for f in range(HALVES)]
+        def page_of(kind, c):
+            if kind == CLAIMS:
+                return pages[CLAIMS][c if c < 3 else 0]
+            return pages[EVIDENCE][c % 2 if c < 3 else 1]
 
-        def transposes(k):
-            kind, c = steps[k]
-            if kind == "claims":
-                terms = [cons_rows[c], claim_pages[c % len(claim_pages)]]
+        def scatter(kind, c, fused=False):
+            window = page_of(kind, c)[:].indirect(idx_pages[kind][:])
+            if fused:
+                nc.vector.tensor_tensor(window, h[kind, c], gain[kind], MULT)
             else:
-                terms = [evid_pages[c % len(evid_pages)]]
-            for bank, first, blocks in page_banks(k):
-                for u in range(blocks):
-                    for i, term in enumerate(terms):
-                        nc.tensor.matmul(
-                            banks[bank][:, u * P : (u + 1) * P],
-                            lhsT=term[:, (first + u) * P : (first + u + 1) * P],
-                            rhs=ident[:],
-                            is_transpose=True,
-                            start=(i == 0),
-                            stop=(i == len(terms) - 1),
-                        )
+                nc.vector.tensor_copy(window, h[kind, c])
 
-        def squares(k):
-            kind, c = steps[k]
-            if kind == "claims":
-                result = ring.tile([P, T2], F32, name="claim_sq", bufs=LEAD + 3)
-                claim_sq[c] = result
-            elif c < ROW_TILES - 1:
-                result = ring.tile([P, T2], F32, name="evid_sq", bufs=3)
-                evid_sq[c] = result
-            else:
-                result = ring.tile([P, T2], F32, name="slot_c", bufs=1, align_bytes=64)
-                evid_sq[c] = result
+        squares = {}
+
+        def squared(kind, c, page_banks, result=None):
+            blocks = T2 // P // len(page_banks)
+            terms = [cons_rows[c], page_of(kind, c)] if kind == CLAIMS else [page_of(kind, c)]
+            if result is None:
+                result = ring.tile([P, T2], F32, name=f"squares{kind}", bufs=(4, 3)[kind])
+            squares[kind, c] = result
             groups = result[:].rearrange("t (f h u q e) -> t f h u q e", f=HALVES, h=2, u=4, e=2)
-            for bank, first, blocks in page_banks(k):
-                f, u = divmod(first, 4)
+
+
+            def transposes(i, n):
+                for u in range(blocks):
+                    block = n * blocks + u
+                    nc.tensor.matmul(
+                        banks[page_banks[n]][:, u * P : (u + 1) * P],
+                        lhsT=terms[i][:, block * P : (block + 1) * P],
+                        rhs=ident[:],
+                        is_transpose=True,
+                        start=(len(terms) == 1 or (i == 0 and u == 0)),
+                        stop=(len(terms) == 1 or (i == 1 and u == blocks - 1)),
+                    )
+
+            if kind == CLAIMS:
+                for n in range(len(page_banks)):
+                    transposes(0, n)
+            for n, bank in enumerate(page_banks):
+                transposes(len(terms) - 1, n)
+                f, u = divmod(n * blocks, 4)
                 nc.scalar.activation(
                     groups[:, f, :, u : u + blocks],
                     banks[bank][:, : blocks * P].rearrange("t (u q h e) -> t h u q e", h=2, e=2, q=32),
                     SQUARE,
                 )
 
-        claim_sq, evid_sq = {}, {}
-
-        def scatter(k):
-            kind, c = steps[k]
-            if kind == "claims":
-                page, idx = claim_pages[c % len(claim_pages)], idx_claims
-            else:
-                page, idx = evid_pages[c % len(evid_pages)], idx_evid
-            if k == 0:
-                for part in range(FIRST_PARTS):
-                    nc.vector.tensor_copy(page[:].indirect(idx[:, list_columns(part)]), h[0][:, entries(part)])
-            elif k < FUSED_STEPS or k == len(steps) - 2:
-                nc.vector.tensor_tensor(page[:].indirect(idx[:]), h[k], gain[kind], MULT)
-            else:
-                nc.vector.tensor_copy(page[:].indirect(idx[:]), h[k])
-
-        def difference(c, groups):
+        def difference(c):
             b, quad = divmod(c, PACK)
-            (nc.vector if c >= ROW_TILES - 2 else nc.gpsimd).tensor_tensor(
-                z_t[b][:].rearrange("t (g x) -> t g x", g=16)[:, groups, 64 * quad : 64 * (quad + 1)],
-                claim_sq[c][:].rearrange("t (g x) -> t g x", g=16)[:, groups, :],
-                evid_sq[c][:].rearrange("t (g x) -> t g x", g=16)[:, groups, :],
+            nc.gpsimd.tensor_tensor(
+                z_t[b][:].rearrange("t (g x) -> t g x", g=16)[:, :, 64 * quad : 64 * (quad + 1)],
+                squares[CLAIMS, c][:].rearrange("t (g x) -> t g x", g=16),
+                squares[EVIDENCE, c][:].rearrange("t (g x) -> t g x", g=16),
                 SUBTRACT,
             )
 
-        z_rounded = {}
+        def last_difference(quarter):
+            b, quad = divmod(LAST, PACK)
+            f, pair = divmod(quarter, 2)
+            views = [
+                tile[:].rearrange("t (f h u x) -> t f h u x", f=2, h=2, u=4)[:, f, :, 2 * pair : 2 * pair + 2, :]
+                for tile in (z_t[b], squares[CLAIMS, LAST], squares[EVIDENCE, LAST])
+            ]
+            nc.vector.tensor_tensor(views[0][:, :, :, 64 * quad : 64 * (quad + 1)], views[1], views[2], SUBTRACT)
 
-        def turn_z(b, quarters, turn_banks):
+        def turn_z(b, quarter, bank, rounded):
             words = z_t[b][:].bitcast(F32)
-            rounded = first_pass[0][:, : PACK * T2] if b == 0 else rounded_tile(QUARTER)
-            for i, quarter in enumerate(quarters):
-                bank = banks[turn_banks[i]]
-                f, pair = divmod(quarter, 2)
-                for u in range(2):
-                    for h in range(2):
-                        g = 8 * f + 4 * h + 2 * pair + u
-                        nc.tensor.transpose(
-                            bank[:, (2 * u + h) * P : (2 * u + h + 1) * P], words[:, g * P : (g + 1) * P], ident[:]
-                        )
-                (nc.vector.tensor_copy if b == PASSES - 1 and quarter == 2 else nc.scalar.copy)(
-                    rounded[:].bitcast(F32)[:, i * BANK : (i + 1) * BANK].rearrange("p (u t h) -> p u t h", u=2, h=2),
-                    bank[:].rearrange("p (u h t) -> p u t h", u=2, h=2),
-                )
-            z_rounded[b] = rounded, slice(quarters[0] * QUARTER, (quarters[-1] + 1) * QUARTER)
+            f, pair = divmod(quarter, 2)
+            for u in range(2):
+                for half in range(2):
+                    g = 8 * f + 4 * half + 2 * pair + u
+                    nc.tensor.transpose(
+                        banks[bank][:, (2 * u + half) * P : (2 * u + half + 1) * P],
+                        words[:, g * P : (g + 1) * P],
+                        ident[:],
+                    )
+            nc.scalar.copy(
+                rounded.bitcast(F32).rearrange("p (u t h) -> p u t h", u=2, h=2),
+                banks[bank][:].rearrange("p (u h t) -> p u t h", u=2, h=2),
+            )
 
-        def quantize_z(b):
-            rounded, cols = z_rounded[b]
-            nc.vector.quantize_mx(out=z_w[b][:, cols].bitcast(FP8X4), scales=z_s[b][:, cols], in_=rounded[:])
+        z_w = {}
+
+        def quantize_z(b, first, count, rounded, codes):
+            for i in range(count):
+                z_w[b, first + i] = codes[:, i * QUARTER : (i + 1) * QUARTER]
+            cols = slice(first * QUARTER, (first + count) * QUARTER)
+            nc.vector.quantize_mx(out=codes.bitcast(FP8X4), scales=z_s[b][:, cols], in_=rounded)
 
         y_banks = [(0, 1), (2, 3), (4, 5), (6, 7)]
 
@@ -371,7 +329,7 @@ def tile_list_trench_dispute_features_kernel(
                     out=banks[y_banks[quarter][j // 2]][:, (j % 2) * QUARTER : (j % 2 + 1) * QUARTER],
                     lhsT=w3_w[b][:, j * P : (j + 1) * P].bitcast(FP8X4),
                     lhsT_scale=w3_s[:, b * N + j * P : b * N + (j + 1) * P],
-                    rhs=z_w[b][:, cols].bitcast(FP8X4),
+                    rhs=z_w[b, quarter].bitcast(FP8X4),
                     rhs_scale=z_s[b][:, cols],
                     start=(b == 0 and j % 2 == 0),
                     stop=(b == PASSES - 1 and j % 2 == 1),
@@ -387,7 +345,7 @@ def tile_list_trench_dispute_features_kernel(
                 copy = nc.vector.tensor_copy if quarter == 0 and i == 1 else nc.scalar.copy
                 copy(y_all[:, i * BANK : (i + 1) * BANK], banks[bank][:])
             nc.sync.dma_start(out=y_rows[:, :, cols], in_=y_all[:].rearrange("p (j t) -> p j t", j=PACK))
-            y_rounded = ring.tile([P, PACK * QUARTER], BF16, name="w2_raw", bufs=4, align_bytes=64)
+            y_rounded = ring.tile([P, PACK * QUARTER], BF16, name="y_rounded", bufs=QUARTERS, align_bytes=64)
             nc.vector.tensor_copy(
                 y_rounded[:].rearrange("p (c i j) -> p c j i", i=4, j=PACK),
                 y_all[:].rearrange("p (j c i) -> p c j i", j=PACK, i=4),
@@ -395,132 +353,113 @@ def tile_list_trench_dispute_features_kernel(
             nc.vector.quantize_mx(out=y_w[:, cols].bitcast(FP8X4), scales=y_s[:, cols], in_=y_rounded[:])
 
         load_w2(0)
-        nc.sync.dma_start(out=gain["evidence"], in_=wg2)
-        load_w2(1)
-        load_cons(0)
-        load_w2(2)
-        load_w2(3)
-        for c in range(1, ROW_TILES):
+        nc.sync.dma_start(out=gain[EVIDENCE], in_=wg2)
+        for g in range(1, W2_CHUNKS):
+            load_w2(g)
+        for c in range(ROW_TILES):
             load_cons(c)
+        for b in range(PASSES):
+            load_w3(b)
 
-        last = len(steps) - 1
-        new_pair(0, 1)
+        chunk_values = PACK * chunk_words
+        opening = keep.tile([P, 3 * S], F32, name="opening")
+        h[CLAIMS, 0] = opening[:, :S]
         first_features()
-        product(6, 0)
-        product(1, 1)
-        h[6] = keep.tile([P, S], F32, name="early_features")[:]
-        nc.scalar.copy(h[6], banks[0][:])
-        nc.gpsimd.tensor_tensor(h[6], h[6], gain["claims"], MULT)
-        product(2, 0)
-        nc.scalar.copy(h[1], banks[1][:])
-        scatter(0)
-        round_w2(W2_CALLS[0])
-        new_pair(2, 5)
-        nc.scalar.copy(h[2], banks[0][:])
-        scatter(1)
-        round_w2(W2_CALLS[1])
-        quantize_w2(W2_CALLS[0])
-        product(3, 1)
-        product(4, 0)
-        scatter(2)
-        new_pair(3, 4)
-        nc.scalar.copy(h[3], banks[1][:])
-        product(5, 1)
-        nc.scalar.copy(h[4], banks[0][:])
-        nc.scalar.copy(h[5], banks[1][:])
-        quantize_w2(W2_CALLS[1])
-        transposes(0)
-        squares(0)
-        scatter(3)
-        round_w2(W2_CALLS[2])
-        product(7, 1)
-        scatter(4)
-        h[7] = ring.tile([P, S], F32, name="slot_e", bufs=1, align_bytes=64)[:]
-        nc.scalar.copy(h[7], banks[1][:])
-        product(8, 6)
-        product(9, 7)
-        waiting_pair = copied_pair(4)
-        for k in (1, 3, 2):
-            transposes(k)
-            squares(k)
-        load_w3(0)
-        load_w3(1)
-        transposes(4)
-        scatter(5)
-        raw_features, h[7] = h[7], ring.tile([P, S], F32, name="slot_b", bufs=1, align_bytes=64)[:]
-        nc.gpsimd.tensor_tensor(h[7], raw_features, gain["evidence"], MULT)
-        quantize_w2(W2_CALLS[2])
-        after_w2 = rounded_tile(T2 + S, "late_w2")
-        z_t[0] = after_w2[:, : PACK * T2]
-        gained = after_w2[:, PACK * T2 :].bitcast(F32)
-        gain_pair(4, gained, waiting_pair)
+        features(CLAIMS, 3, 0, opening[:, 2 * S :])
+        gain_one(CLAIMS, 3, h[CLAIMS, 3])
+        features(CLAIMS, 1, 1, opening[:, S : 2 * S])
+        product(CLAIMS, 2, 0)
+        for part in range(FIRST_PARTS):
+            window = page_of(CLAIMS, 0)[:].indirect(idx_pages[CLAIMS][:, list_columns(part)])
+            nc.vector.tensor_copy(window, h[CLAIMS, 0][:, entries(part)])
+        rounded = [slot(f"rounded{g}", chunk_values, BF16) for g in range(2)]
+        late_rounded = slot("late_rounded", 2 * chunk_values, BF16)
+        round_w2(0, rounded[0])
+        h[CLAIMS, 2] = slot("raw1", S, F32)[:]
+        nc.scalar.copy(h[CLAIMS, 2], banks[0][:])
+        scatter(CLAIMS, 1, fused=True)
+        round_w2(1, rounded[1])
+        quantize_w2(0, 1, rounded[0][:])
+        features(EVIDENCE, 0, 1, slot("raw3", S, F32)[:])
+        product(EVIDENCE, 1, 0)
+        scatter(CLAIMS, 2, fused=True)
+        quantize_w2(1, 1, rounded[1][:])
+        round_w2(2, late_rounded[:, :chunk_values])
+        scatter(EVIDENCE, 0, fused=True)
+        round_w2(3, late_rounded[:, chunk_values:])
+        held = slot("raw_last", 5 * S, F32)
+        h[EVIDENCE, 1] = held[:, :S]
+        nc.scalar.copy(h[EVIDENCE, 1], banks[0][:])
+        features(EVIDENCE, 2, 1, held[:, S : 2 * S])
+        pair = feature_pair(4, 3, held[:, 3 * S :], (6, 7))
+        quantize_w2(2, 2, late_rounded[:])
+        z_t[0] = slot("late_rounded", PACK * T2, BF16)
+        squared(CLAIMS, 0, (0, 1))
+        squared(EVIDENCE, 0, (6, 7))
+        scatter(EVIDENCE, 1, fused=True)
 
-        def squared(k):
-            transposes(k)
-            squares(k)
-
-        def features(pair, first_bank=6):
-            product(2 * pair, first_bank)
-            product(2 * pair + 1, 7)
-            both = copied_pair(pair, first_bank)
-            gain_pair(pair, both, both)
-
-        whole = slice(0, 16)
-        scatter(6)
-        squares(4)
-        difference(0, whole)
-        features(5)
-        squared(5)
-        difference(1, whole)
-        scatter(7)
-        squared(6)
-        scatter(8)
-        features(6)
-        squared(7)
-        difference(2, whole)
-        round_w3(0)
-        scatter(9)
-        squared(8)
-        difference(3, whole)
-        product(last, 6)
-        new_pair(last - 1, last)
-        nc.scalar.copy(h[last], banks[6][:])
-        scatter(10)
-        squared(9)
-        round_w3(1)
-        scatter(11)
-        squared(10)
-        difference(4, whole)
-        nc.gpsimd.tensor_tensor(h[last], h[last], gain["evidence"], MULT)
-        turn_z(0, list(range(QUARTERS)), [0, 1, 4, 5])
-        product(last - 1, 5)
-        nc.scalar.copy(h[last - 1], banks[5][:])
-        scatter(12)
-        squared(11)
-        scatter(13)
-        squared(12)
-        first_codes = ring.tile([P, T2 + N], U32, name="slot_b", bufs=1, align_bytes=64)
-        z_w[0] = first_codes[:, :T2]
-        quantize_w3(0, first_codes[:, T2:])
-        quantize_z(0)
-        scatter(last - 1)
-        squared(13)
-        difference(5, whole)
-        scatter(last)
-        transposes(last - 1)
-        squares(last - 1)
+        gain_one(EVIDENCE, 2, held[:, :S])
+        gain_pair(4, 3, pair, held[:, S : 3 * S])
+        difference(0)
+        squared(CLAIMS, 1, (0, 1))
+        squared(EVIDENCE, 1, (4, 5))
+        scatter(CLAIMS, 3)
+        difference(1)
+        pairs = {5: feature_pair(5, 4, slot("raw4", 2 * S, F32)[:], (2, 3))}
+        squared(CLAIMS, 2, (6, 7))
+        squared(CLAIMS, 3, (0, 1))
+        scatter(EVIDENCE, 2)
+        gain_pair(5, 4, pairs[5], pairs[5])
+        squared(EVIDENCE, 2, (4, 5))
+        features(EVIDENCE, 5, 7, slot("raw5", S, F32)[:])
+        scatter(EVIDENCE, 3)
+        difference(2)
+        squared(EVIDENCE, 3, (4, 5))
+        pairs[6] = feature_pair(6, 6, slot("raw2", 2 * S, F32)[:], (6, 7))
+        scatter(CLAIMS, 4)
+        difference(3)
+        gain_one(EVIDENCE, 5, h[EVIDENCE, 5])
+        gain_pair(6, 6, pairs[6], pairs[6])
+        squared(CLAIMS, 4, (2, 3))
+        round_w3(0, "rounded0")
+        scatter(EVIDENCE, 4)
+        squared(EVIDENCE, 4, (4, 5))
+        pairs[7] = feature_pair(7, 7, slot("raw1", 2 * S, F32)[:], (6, 7))
+        first_pass = [slot(name, 2 * PACK * QUARTER, BF16) for name in ("raw0", "raw3")]
+        for quarter in range(QUARTERS):
+            f, pair_of = divmod(quarter, 2)
+            turn_z(0, quarter, (0, 1, 6, 7)[quarter], first_pass[f][:, pair_of * PACK * QUARTER : (pair_of + 1) * PACK * QUARTER])
+        scatter(CLAIMS, 5)
+        difference(4)
+        gain_pair(7, 7, pairs[7], pairs[7])
+        squared(CLAIMS, 5, (2, 3))
+        scatter(EVIDENCE, 5)
+        squared(EVIDENCE, 5, (4, 5))
+        round_w3(1, "rounded1")
+        scatter(CLAIMS, 6)
+        difference(5)
+        squared(CLAIMS, 6, (2, 3))
+        scatter(EVIDENCE, 6)
+        codes = slot("raw2", BANK + N, U32)
+        quantize_z(0, 0, 2, first_pass[0][:], codes[:, :BANK])
+        quantize_w3(0, codes[:, BANK:])
+        squared(EVIDENCE, 6, (4, 5))
+        difference(6)
+        scatter(CLAIMS, LAST)
+        squared(CLAIMS, LAST, range(8))
         for quarter in (0, 1):
             y_pass(0, quarter)
-        transposes(last)
-        squares(last)
+        scatter(EVIDENCE, LAST)
 
-        difference(ROW_TILES - 2, slice(0, 16))
+        quantize_z(0, 2, 2, first_pass[1][:], slot("raw1", BANK, U32)[:])
+        squared(EVIDENCE, LAST, (4, 5, 6, 7), slot("raw6", T2, F32))
         for quarter in range(QUARTERS):
             last_difference(quarter)
-        quantize_w3(1, ring.tile([P, N], U32, name="slot_c", bufs=1, align_bytes=64))
+        quantize_w3(1, slot("raw6", N, U32)[:])
         for quarter in range(QUARTERS):
-            turn_z(1, [quarter], [4 + quarter])
-            quantize_z(1)
+            turned = ring.tile([P, PACK * QUARTER], BF16, name="turned", bufs=QUARTERS, align_bytes=64)
+            turn_z(1, quarter, 4 + quarter, turned[:])
+            quantize_z(1, quarter, 1, turned[:], z_last[:, quarter * QUARTER : (quarter + 1) * QUARTER])
         for quarter in range(QUARTERS):
             if quarter >= 2:
                 y_pass(0, quarter)

@@ -33,6 +33,8 @@ W2_CHUNK = 2
 W2_CHUNKS = ROW_TILES // W2_CHUNK
 FIRST_PARTS = 2
 CLAIMS, EVIDENCE = 0, 1
+ROWS = [0, 2, 3, 1, 4, 5, 6, 7]
+EARLY = 2 * P
 
 
 def tile_list_trench_dispute_features_kernel(
@@ -55,7 +57,10 @@ def tile_list_trench_dispute_features_kernel(
 
         tab_w = [slot(f"table{a}", T, U32) for a in range(PASSES)]
         tab_s = keep.tile([P, PASSES * T], U8, name="tab_s", align_bytes=64)
-        w1_w = keep.tile([P, PASSES * 2 * H], U8, name="w1_w", align_bytes=64)
+        w1_pieces = [(0, EARLY), (EARLY, H - EARLY)]
+        w1_w = [
+            keep.tile([P, PASSES * 2 * count], U8, name=f"w1_w{first}", align_bytes=64) for first, count in w1_pieces
+        ]
         w1_s = keep.tile([P, PASSES * H], U8, name="w1_s", align_bytes=64)
         v_w = [keep.tile([P, S], U32, name=f"v_w{a}", align_bytes=64) for a in range(PASSES)]
         v_s = [keep.tile([P, S], U8, name=f"v_s{a}", align_bytes=64) for a in range(PASSES)]
@@ -82,6 +87,13 @@ def tile_list_trench_dispute_features_kernel(
                     in_=scales[:, 4 * quad : 4 * quad + 4, :].bitcast(I32).rearrange("a i c -> i a c"),
                 )
 
+        def load_w1(piece):
+            first, count = w1_pieces[piece]
+            nc.sync.dma_start(
+                out=w1_w[piece][:].bitcast(I32).rearrange("p (a c) -> p a c", a=PASSES),
+                in_=w1_words[:, :, 2 * first : 2 * (first + count)].bitcast(I32).rearrange("a p c -> p a c"),
+            )
+
         def load_tab_words(a):
             nc.sync.dma_start(
                 out=tab_w[a][:].bitcast(I32), in_=tab_words[a].rearrange("p t i -> p (t i)").bitcast(I32)
@@ -93,14 +105,11 @@ def tile_list_trench_dispute_features_kernel(
         load_tab_words(0)
         load_scale_rows(tab_s, tab_scales)
         load_tab_words(1)
-        nc.sync.dma_start(
-            out=w1_w[:].bitcast(I32).rearrange("p (a c) -> p a c", a=PASSES),
-            in_=w1_words.bitcast(I32).rearrange("a p c -> p a c"),
-        )
+        load_w1(0)
         load_scale_rows(w1_s, w1_scales)
         nc.sync.dma_start(idx_pages[CLAIMS][:], offs2)
         nc.sync.dma_start(out=gain[CLAIMS], in_=wg1)
-        nc.sync.dma_start(idx_pages[EVIDENCE][:], offs3)
+        load_w1(1)
         nc.vector.memset(pages[CLAIMS][0][:].bitcast(I32), 0)
         make_identity(nc, ident[:])
         for page in pages[CLAIMS][1:] + pages[EVIDENCE]:
@@ -138,7 +147,7 @@ def tile_list_trench_dispute_features_kernel(
 
         def load_cons(c):
             rows = ring.tile([P, T2], F32, name="cons_rows", bufs=ROW_TILES)
-            nc.sync.dma_start(out=rows[:], in_=cons[c * P : (c + 1) * P, :])
+            nc.sync.dma_start(out=rows[:], in_=cons[ROWS[c] * P : (ROWS[c] + 1) * P, :])
             cons_rows[c] = rows
 
         chunk_words = PASSES * W2_CHUNK * P
@@ -174,9 +183,11 @@ def tile_list_trench_dispute_features_kernel(
 
         def stationary(kind, c, a):
             if kind == CLAIMS:
-                col = a * H + c * P
-                return w1_w[:, 2 * col : 2 * (col + P)].bitcast(FP4X4), w1_s[:, col : col + P]
-            g, tile = divmod(c, W2_CHUNK)
+                piece = int(ROWS[c] * P >= EARLY)
+                first, count = w1_pieces[piece]
+                col = a * count + ROWS[c] * P - first
+                return w1_w[piece][:, 2 * col : 2 * (col + P)].bitcast(FP4X4), w1_s[:, a * H + ROWS[c] * P : a * H + (ROWS[c] + 1) * P]
+            g, tile = divmod(ROWS[c], W2_CHUNK)
             col = ((PASSES * g + a) * W2_CHUNK + tile) * P
             return w2_w[:, col : col + P].bitcast(FP8X4), w2_s[:, col : col + P]
 
@@ -279,7 +290,7 @@ def tile_list_trench_dispute_features_kernel(
                 )
 
         def difference(c):
-            b, quad = divmod(c, PACK)
+            b, quad = divmod(ROWS[c], PACK)
             nc.gpsimd.tensor_tensor(
                 z_t[b][:].rearrange("t (g x) -> t g x", g=16)[:, :, 64 * quad : 64 * (quad + 1)],
                 squares[CLAIMS, c][:].rearrange("t (g x) -> t g x", g=16),
@@ -353,8 +364,10 @@ def tile_list_trench_dispute_features_kernel(
             nc.vector.quantize_mx(out=y_w[:, cols].bitcast(FP8X4), scales=y_s[:, cols], in_=y_rounded[:])
 
         load_w2(0)
+        load_w2(1)
         nc.sync.dma_start(out=gain[EVIDENCE], in_=wg2)
-        for g in range(1, W2_CHUNKS):
+        nc.sync.dma_start(idx_pages[EVIDENCE][:], offs3)
+        for g in range(2, W2_CHUNKS):
             load_w2(g)
         for c in range(ROW_TILES):
             load_cons(c)
@@ -381,9 +394,9 @@ def tile_list_trench_dispute_features_kernel(
         round_w2(1, rounded[1])
         quantize_w2(0, 1, rounded[0][:])
         features(EVIDENCE, 0, 1, slot("raw3", S, F32)[:])
-        product(EVIDENCE, 1, 0)
         scatter(CLAIMS, 2, fused=True)
         quantize_w2(1, 1, rounded[1][:])
+        product(EVIDENCE, 1, 0)
         round_w2(2, late_rounded[:, :chunk_values])
         scatter(EVIDENCE, 0, fused=True)
         round_w2(3, late_rounded[:, chunk_values:])

@@ -100,7 +100,7 @@ def tile_list_trench_dispute_features_kernel(
             )
 
         nc.vector.memset(tab_s[:].bitcast(I32), 0)
-        nc.gpsimd.memset(w1_s[:].bitcast(I32), 0)
+        nc.vector.memset(w1_s[:].bitcast(I32), 0)
         nc.sync.dma_start(idx_notes[:], offs)
         load_tab_words(0)
         load_scale_rows(tab_s, tab_scales)
@@ -110,9 +110,10 @@ def tile_list_trench_dispute_features_kernel(
         nc.sync.dma_start(idx_pages[CLAIMS][:], offs2)
         nc.sync.dma_start(out=gain[CLAIMS], in_=wg1)
         load_w1(1)
-        nc.vector.memset(pages[CLAIMS][0][:].bitcast(I32), 0)
+        for page in pages[CLAIMS][:2]:
+            nc.vector.memset(page[:].bitcast(I32), 0)
         make_identity(nc, ident[:])
-        for page in pages[CLAIMS][1:] + pages[EVIDENCE]:
+        for page in pages[CLAIMS][2:] + pages[EVIDENCE]:
             nc.gpsimd.memset(page[:].bitcast(I32), 0)
 
         def entries(part):
@@ -382,9 +383,7 @@ def tile_list_trench_dispute_features_kernel(
         gain_one(CLAIMS, 3, h[CLAIMS, 3])
         features(CLAIMS, 1, 1, opening[:, S : 2 * S])
         product(CLAIMS, 2, 0)
-        for part in range(FIRST_PARTS):
-            window = page_of(CLAIMS, 0)[:].indirect(idx_pages[CLAIMS][:, list_columns(part)])
-            nc.vector.tensor_copy(window, h[CLAIMS, 0][:, entries(part)])
+        scatter(CLAIMS, 0)
         rounded = [slot(f"rounded{g}", chunk_values, BF16) for g in range(2)]
         late_rounded = slot("late_rounded", 2 * chunk_values, BF16)
         round_w2(0, rounded[0])

@@ -437,43 +437,44 @@ def tile_list_trench_dispute_features_kernel(
         scatter(EVIDENCE, 4)
         squared(EVIDENCE, 4, (4, 5))
         pairs[7] = feature_pair(7, 7, slot("raw1", 2 * S, F32)[:], (6, 7))
-        first_pass = [slot(name, 2 * PACK * QUARTER, BF16) for name in ("raw0", "raw3")]
-        for quarter in range(QUARTERS):
-            f, pair_of = divmod(quarter, 2)
-            turn_z(0, quarter, (0, 1, 6, 7)[quarter], first_pass[f][:, pair_of * PACK * QUARTER : (pair_of + 1) * PACK * QUARTER])
         scatter(CLAIMS, 5)
         difference(4)
         gain_pair(7, 7, pairs[7], pairs[7])
         squared(CLAIMS, 5, (2, 3))
         scatter(EVIDENCE, 5)
         squared(EVIDENCE, 5, (4, 5))
+        first_pass = [slot(name, 2 * PACK * QUARTER, BF16) for name in ("raw0", "raw3")]
+        for quarter in range(QUARTERS):
+            f, pair_of = divmod(quarter, 2)
+            turn_z(0, quarter, (0, 1, 6, 7)[quarter], first_pass[f][:, pair_of * PACK * QUARTER : (pair_of + 1) * PACK * QUARTER])
         round_w3(1, "rounded1")
         scatter(CLAIMS, 6)
         difference(5)
         squared(CLAIMS, 6, (2, 3))
         scatter(EVIDENCE, 6)
-        codes = slot("raw2", BANK + N, U32)
-        quantize_z(0, 0, 2, first_pass[0][:], codes[:, :BANK])
-        quantize_w3(0, codes[:, BANK:])
         squared(EVIDENCE, 6, (4, 5))
         difference(6)
         scatter(CLAIMS, LAST)
-        squared(CLAIMS, LAST, range(8))
-        for quarter in (0, 1):
-            y_pass(0, quarter)
+        squared(CLAIMS, LAST, (0, 1))
         scatter(EVIDENCE, LAST)
 
-        quantize_z(0, 2, 2, first_pass[1][:], slot("raw1", BANK, U32)[:])
+        codes = slot("raw1", BANK + N, U32)
+        quantize_w3(0, codes[:, BANK:])
+        quantize_z(0, 0, 2, first_pass[0][:], codes[:, :BANK])
         squared(EVIDENCE, LAST, (4, 5, 6, 7), slot("raw6", T2, F32))
         for quarter in range(QUARTERS):
             last_difference(quarter)
-        quantize_w3(1, slot("raw6", N, U32)[:])
+        codes = slot("raw6", BANK + N, U32)
+        quantize_w3(1, codes[:, BANK:])
+        y_pass(0, 0)
         for quarter in range(QUARTERS):
             turned = ring.tile([P, PACK * QUARTER], BF16, name="turned", bufs=QUARTERS, align_bytes=64)
             turn_z(1, quarter, 4 + quarter, turned[:])
             quantize_z(1, quarter, 1, turned[:], z_last[:, quarter * QUARTER : (quarter + 1) * QUARTER])
+            if quarter == 0:
+                quantize_z(0, 2, 2, first_pass[1][:], codes[:, :BANK])
         for quarter in range(QUARTERS):
-            if quarter >= 2:
+            if quarter >= 1:
                 y_pass(0, quarter)
             y_pass(1, quarter)
             finish(quarter)

@@ -257,21 +257,20 @@ def tile_list_trench_dispute_features_kernel(
 
         squares = {}
 
-        def squared(kind, c, page_banks, result=None):
-            blocks = T2 // P // len(page_banks)
+        def squared(kind, c, page_banks, result=None, widths=None):
+            widths = widths or [T2 // P // len(page_banks)] * len(page_banks)
+            pieces = [(bank, sum(widths[:n]), widths[n]) for n, bank in enumerate(page_banks)]
             terms = [cons_rows[c], page_of(kind, c)] if kind == CLAIMS else [page_of(kind, c)]
             if result is None:
                 result = ring.tile([P, T2], F32, name=f"squares{kind}", bufs=(4, 3)[kind])
             squares[kind, c] = result
             groups = result[:].rearrange("t (f h u q e) -> t f h u q e", f=HALVES, h=2, u=4, e=2)
 
-
-            def transposes(i, n):
+            def transposes(i, bank, first, blocks):
                 for u in range(blocks):
-                    block = n * blocks + u
                     nc.tensor.matmul(
-                        banks[page_banks[n]][:, u * P : (u + 1) * P],
-                        lhsT=terms[i][:, block * P : (block + 1) * P],
+                        banks[bank][:, u * P : (u + 1) * P],
+                        lhsT=terms[i][:, (first + u) * P : (first + u + 1) * P],
                         rhs=ident[:],
                         is_transpose=True,
                         start=(len(terms) == 1 or (i == 0 and u == 0)),
@@ -279,11 +278,11 @@ def tile_list_trench_dispute_features_kernel(
                     )
 
             if kind == CLAIMS:
-                for n in range(len(page_banks)):
-                    transposes(0, n)
-            for n, bank in enumerate(page_banks):
-                transposes(len(terms) - 1, n)
-                f, u = divmod(n * blocks, 4)
+                for piece in pieces:
+                    transposes(0, *piece)
+            for bank, first, blocks in pieces:
+                transposes(len(terms) - 1, bank, first, blocks)
+                f, u = divmod(first, 4)
                 nc.scalar.activation(
                     groups[:, f, :, u : u + blocks],
                     banks[bank][:, : blocks * P].rearrange("t (u q h e) -> t h u q e", h=2, e=2, q=32),
@@ -455,17 +454,29 @@ def tile_list_trench_dispute_features_kernel(
         squared(EVIDENCE, 6, (4, 5))
         difference(6)
         scatter(CLAIMS, LAST)
-        squared(CLAIMS, LAST, (0, 1))
+        squared(CLAIMS, LAST, (2, 4, 5, 6, 7, 0, 1), widths=[2, 1, 1, 1, 1, 1, 1])
+        for a in (0, 1, 0):
+            codes, scales = stationary(EVIDENCE, LAST, a)
+            nc.tensor.matmul_mx(
+                out=banks[2][:],
+                lhsT=codes,
+                lhsT_scale=scales,
+                rhs=v_w[a][:].bitcast(FP8X4),
+                rhs_scale=v_s[a][:],
+                start=True,
+                stop=True,
+            )
         scatter(EVIDENCE, LAST)
 
         codes = slot("raw1", BANK + N, U32)
         quantize_w3(0, codes[:, BANK:])
-        quantize_z(0, 0, 2, first_pass[0][:], codes[:, :BANK])
+        quantize_z(0, 0, 1, first_pass[0][:, : PACK * QUARTER], codes[:, :QUARTER])
         squared(EVIDENCE, LAST, (4, 5, 6, 7), slot("raw6", T2, F32))
         for quarter in range(QUARTERS):
             last_difference(quarter)
-        codes = slot("raw6", BANK + N, U32)
-        quantize_w3(1, codes[:, BANK:])
+        codes = slot("raw6", BANK + N + QUARTER, U32)
+        quantize_w3(1, codes[:, BANK : BANK + N])
+        quantize_z(0, 1, 1, first_pass[0][:, PACK * QUARTER :], codes[:, BANK + N :])
         y_pass(0, 0)
         for quarter in range(QUARTERS):
             turned = ring.tile([P, PACK * QUARTER], BF16, name="turned", bufs=QUARTERS, align_bytes=64)
@@ -482,6 +493,6 @@ def tile_list_trench_dispute_features_kernel(
             cols = slice(half * BANK, (half + 1) * BANK)
             nc.sync.dma_start(out=y_words[:, cols], in_=y_w[:, cols].bitcast(I32))
         for quad in range(4):
-            nc.sync.dma_start(
+            (nc.sync, nc.scalar)[quad % 2].dma_start(
                 out=out_2[0, 4 * quad : 4 * quad + 4, :].bitcast(I32), in_=y_s[32 * quad : 32 * quad + 4, :].bitcast(I32)
             )

@@ -79,6 +79,10 @@ def tile_list_trench_dispute_features_kernel(
         z_last = keep.tile([P, T2], U32, name="z_last", align_bytes=64)
         y_w = keep.tile([P, T2], U32, name="y_w", align_bytes=64)
         y_s = keep.tile([P, T2], U8, name="y_s", align_bytes=64)
+        y_rounded = [
+            keep.tile([P, PACK * QUARTER * count], BF16, name=f"y_rounded{i}", align_bytes=64)
+            for i, count in enumerate((2, 1, 1))
+        ]
 
         def load_scale_rows(plane, scales):
             for quad in range(4):
@@ -208,9 +212,14 @@ def tile_list_trench_dispute_features_kernel(
                         start=(a == 0),
                         stop=(a == PASSES - 1),
                     )
-                nc.vector.tensor_tensor(
-                    h[CLAIMS, 0][:, entries(part)], bank[:, 0:width], gains[:, entries(part)], MULT
-                )
+                values = h[CLAIMS, 0][:, entries(part)]
+                if part == 0:
+                    nc.vector.tensor_tensor(values, bank[:, 0:width], gains[:, entries(part)], MULT)
+                else:
+                    nc.scalar.copy(values, bank[:, 0:width])
+                    nc.gpsimd.tensor_tensor(values, values, gains[:, entries(part)], MULT)
+                window = page_of(CLAIMS, 0)[:].indirect(idx_pages[CLAIMS][:, list_columns(part)])
+                nc.vector.tensor_copy(window, values)
 
         def product(kind, c, bank):
             for a in range(PASSES):
@@ -244,9 +253,7 @@ def tile_list_trench_dispute_features_kernel(
             h[kind, c] = result
 
         def page_of(kind, c):
-            if kind == CLAIMS:
-                return pages[CLAIMS][c if c < 3 else 0]
-            return pages[EVIDENCE][c % 2 if c < 3 else 1]
+            return pages[kind][((0, 1, 2, 0, 0, 0, 2, 1), (0, 1, 0, 1, 1, 0, 1, 1))[kind][c]]
 
         def scatter(kind, c, fused=False):
             window = page_of(kind, c)[:].indirect(idx_pages[kind][:])
@@ -353,15 +360,23 @@ def tile_list_trench_dispute_features_kernel(
             cols = slice(quarter * QUARTER, (quarter + 1) * QUARTER)
             y_all = ring.tile([P, PACK * QUARTER], F32, name="cons_rows", bufs=ROW_TILES)
             for i, bank in enumerate(y_banks[quarter]):
-                copy = nc.vector.tensor_copy if quarter == 0 and i == 1 else nc.scalar.copy
-                copy(y_all[:, i * BANK : (i + 1) * BANK], banks[bank][:])
-            nc.sync.dma_start(out=y_rows[:, :, cols], in_=y_all[:].rearrange("p (j t) -> p j t", j=PACK))
-            y_rounded = ring.tile([P, PACK * QUARTER], BF16, name="y_rounded", bufs=QUARTERS, align_bytes=64)
+                copy = nc.vector.tensor_copy if quarter == 1 and i == 0 else nc.scalar.copy
+                part = y_all[:, i * BANK : (i + 1) * BANK]
+                copy(part, banks[bank][:])
+                nc.sync.dma_start(out=y_rows[:, 2 * i : 2 * i + 2, cols], in_=part.rearrange("p (j t) -> p j t", j=2))
+            rounded = y_rounded[max(quarter - 1, 0)]
+            first = PACK * QUARTER if quarter == 1 else 0
             nc.vector.tensor_copy(
-                y_rounded[:].rearrange("p (c i j) -> p c j i", i=4, j=PACK),
+                rounded[:, first : first + PACK * QUARTER].rearrange("p (c i j) -> p c j i", i=4, j=PACK),
                 y_all[:].rearrange("p (j c i) -> p c j i", j=PACK, i=4),
             )
-            nc.vector.quantize_mx(out=y_w[:, cols].bitcast(FP8X4), scales=y_s[:, cols], in_=y_rounded[:])
+            if quarter > 0:
+                ready = slice(0 if quarter == 1 else cols.start, cols.stop)
+                nc.vector.quantize_mx(
+                    out=y_w[:, ready].bitcast(FP8X4),
+                    scales=y_s[:, ready],
+                    in_=rounded[:],
+                )
 
         load_w2(0)
         load_w2(1)
@@ -382,7 +397,6 @@ def tile_list_trench_dispute_features_kernel(
         gain_one(CLAIMS, 3, h[CLAIMS, 3])
         features(CLAIMS, 1, 1, opening[:, S : 2 * S])
         product(CLAIMS, 2, 0)
-        scatter(CLAIMS, 0)
         rounded = [slot(f"rounded{g}", chunk_values, BF16) for g in range(2)]
         late_rounded = slot("late_rounded", 2 * chunk_values, BF16)
         round_w2(0, rounded[0])
@@ -451,7 +465,7 @@ def tile_list_trench_dispute_features_kernel(
         difference(5)
         squared(CLAIMS, 6, (2, 3))
         scatter(EVIDENCE, 6)
-        squared(EVIDENCE, 6, (4, 5))
+        squared(EVIDENCE, 6, (0, 1))
         difference(6)
         scatter(CLAIMS, LAST)
         squared(CLAIMS, LAST, (2, 4, 5, 6, 7, 0, 1), widths=[2, 1, 1, 1, 1, 1, 1])
@@ -475,8 +489,8 @@ def tile_list_trench_dispute_features_kernel(
         for quarter in range(QUARTERS):
             last_difference(quarter)
         codes = slot("raw6", BANK + N + QUARTER, U32)
-        quantize_w3(1, codes[:, BANK : BANK + N])
         quantize_z(0, 1, 1, first_pass[0][:, PACK * QUARTER :], codes[:, BANK + N :])
+        quantize_w3(1, codes[:, BANK : BANK + N])
         y_pass(0, 0)
         for quarter in range(QUARTERS):
             turned = ring.tile([P, PACK * QUARTER], BF16, name="turned", bufs=QUARTERS, align_bytes=64)
@@ -484,13 +498,13 @@ def tile_list_trench_dispute_features_kernel(
             quantize_z(1, quarter, 1, turned[:], z_last[:, quarter * QUARTER : (quarter + 1) * QUARTER])
             if quarter == 0:
                 quantize_z(0, 2, 2, first_pass[1][:], codes[:, :BANK])
+        y_pass(0, 1)
         for quarter in range(QUARTERS):
-            if quarter >= 1:
+            if quarter >= 2:
                 y_pass(0, quarter)
             y_pass(1, quarter)
             finish(quarter)
-        for half in range(HALVES):
-            cols = slice(half * BANK, (half + 1) * BANK)
+        for cols in (slice(0, 3 * QUARTER), slice(3 * QUARTER, T2)):
             nc.sync.dma_start(out=y_words[:, cols], in_=y_w[:, cols].bitcast(I32))
         for quad in range(4):
             (nc.sync, nc.scalar)[quad % 2].dma_start(

@@ -79,10 +79,6 @@ def tile_list_trench_dispute_features_kernel(
         z_last = keep.tile([P, T2], U32, name="z_last", align_bytes=64)
         y_w = keep.tile([P, T2], U32, name="y_w", align_bytes=64)
         y_s = keep.tile([P, T2], U8, name="y_s", align_bytes=64)
-        y_rounded = [
-            keep.tile([P, PACK * QUARTER * count], BF16, name=f"y_rounded{i}", align_bytes=64)
-            for i, count in enumerate((2, 1, 1))
-        ]
 
         def load_scale_rows(plane, scales):
             for quad in range(4):
@@ -151,7 +147,7 @@ def tile_list_trench_dispute_features_kernel(
             w3_raw[b] = raw
 
         def load_cons(c):
-            rows = ring.tile([P, T2], F32, name="cons_rows", bufs=ROW_TILES)
+            rows = ring.tile([P, T2], F32, name="cons_rows", bufs=LAST) if c < LAST else slot("cons_last", T2, F32)
             nc.sync.dma_start(out=rows[:], in_=cons[ROWS[c] * P : (ROWS[c] + 1) * P, :])
             cons_rows[c] = rows
 
@@ -325,7 +321,7 @@ def tile_list_trench_dispute_features_kernel(
                         words[:, g * P : (g + 1) * P],
                         ident[:],
                     )
-            nc.scalar.copy(
+            (nc.vector.tensor_copy if b == PASSES - 1 and quarter == QUARTERS - 1 else nc.scalar.copy)(
                 rounded.bitcast(F32).rearrange("p (u t h) -> p u t h", u=2, h=2),
                 banks[bank][:].rearrange("p (u h t) -> p u t h", u=2, h=2),
             )
@@ -338,7 +334,7 @@ def tile_list_trench_dispute_features_kernel(
             cols = slice(first * QUARTER, (first + count) * QUARTER)
             nc.vector.quantize_mx(out=codes.bitcast(FP8X4), scales=z_s[b][:, cols], in_=rounded)
 
-        y_banks = [(0, 1), (2, 3), (4, 5), (6, 7)]
+        y_banks = [(0, 1), (4, 5), (2, 3), (6, 7)]
 
         def y_pass(b, quarter):
             cols = slice(quarter * QUARTER, (quarter + 1) * QUARTER)
@@ -358,25 +354,17 @@ def tile_list_trench_dispute_features_kernel(
 
         def finish(quarter):
             cols = slice(quarter * QUARTER, (quarter + 1) * QUARTER)
-            y_all = ring.tile([P, PACK * QUARTER], F32, name="cons_rows", bufs=ROW_TILES)
+            y_all = ring.tile([P, PACK * QUARTER], F32, name="cons_rows", bufs=LAST)
             for i, bank in enumerate(y_banks[quarter]):
-                copy = nc.vector.tensor_copy if quarter == 1 and i == 0 else nc.scalar.copy
                 part = y_all[:, i * BANK : (i + 1) * BANK]
-                copy(part, banks[bank][:])
+                nc.scalar.copy(part, banks[bank][:])
                 nc.sync.dma_start(out=y_rows[:, 2 * i : 2 * i + 2, cols], in_=part.rearrange("p (j t) -> p j t", j=2))
-            rounded = y_rounded[max(quarter - 1, 0)]
-            first = PACK * QUARTER if quarter == 1 else 0
+            y_rounded = ring.tile([P, PACK * QUARTER], BF16, name="y_rounded", bufs=QUARTERS, align_bytes=64)
             nc.vector.tensor_copy(
-                rounded[:, first : first + PACK * QUARTER].rearrange("p (c i j) -> p c j i", i=4, j=PACK),
+                y_rounded[:].rearrange("p (c i j) -> p c j i", i=4, j=PACK),
                 y_all[:].rearrange("p (j c i) -> p c j i", j=PACK, i=4),
             )
-            if quarter > 0:
-                ready = slice(0 if quarter == 1 else cols.start, cols.stop)
-                nc.vector.quantize_mx(
-                    out=y_w[:, ready].bitcast(FP8X4),
-                    scales=y_s[:, ready],
-                    in_=rounded[:],
-                )
+            nc.vector.quantize_mx(out=y_w[:, cols].bitcast(FP8X4), scales=y_s[:, cols], in_=y_rounded[:])
 
         load_w2(0)
         load_w2(1)
@@ -482,25 +470,25 @@ def tile_list_trench_dispute_features_kernel(
             )
         scatter(EVIDENCE, LAST)
 
-        codes = slot("raw1", BANK + N, U32)
+        codes = slot("cons_last", BANK + N, U32)
         quantize_w3(0, codes[:, BANK:])
-        quantize_z(0, 0, 1, first_pass[0][:, : PACK * QUARTER], codes[:, :QUARTER])
+        quantize_z(0, 0, 2, first_pass[0][:], codes[:, :BANK])
         squared(EVIDENCE, LAST, (4, 5, 6, 7), slot("raw6", T2, F32))
         for quarter in range(QUARTERS):
             last_difference(quarter)
-        codes = slot("raw6", BANK + N + QUARTER, U32)
-        quantize_z(0, 1, 1, first_pass[0][:, PACK * QUARTER :], codes[:, BANK + N :])
-        quantize_w3(1, codes[:, BANK : BANK + N])
+        codes = slot("raw6", BANK + N, U32)
+        quantize_z(0, 2, 1, first_pass[1][:, : PACK * QUARTER], codes[:, :QUARTER])
+        quantize_w3(1, codes[:, BANK:])
         y_pass(0, 0)
         for quarter in range(QUARTERS):
             turned = ring.tile([P, PACK * QUARTER], BF16, name="turned", bufs=QUARTERS, align_bytes=64)
             turn_z(1, quarter, 4 + quarter, turned[:])
             quantize_z(1, quarter, 1, turned[:], z_last[:, quarter * QUARTER : (quarter + 1) * QUARTER])
             if quarter == 0:
-                quantize_z(0, 2, 2, first_pass[1][:], codes[:, :BANK])
-        y_pass(0, 1)
+                quantize_z(0, 3, 1, first_pass[1][:, PACK * QUARTER :], codes[:, QUARTER:BANK])
+        y_pass(0, 2)
         for quarter in range(QUARTERS):
-            if quarter >= 2:
+            if quarter % 2 == 1:
                 y_pass(0, quarter)
             y_pass(1, quarter)
             finish(quarter)

@@ -61,7 +61,7 @@ def tile_list_trench_dispute_features_kernel(
         w1_w = [
             keep.tile([P, PASSES * 2 * count], U8, name=f"w1_w{first}", align_bytes=64) for first, count in w1_pieces
         ]
-        w1_s = keep.tile([P, PASSES * H], U8, name="w1_s", align_bytes=64)
+        w1_s = [keep.tile([P, PASSES * count], U8, name=f"w1_s{first}", align_bytes=64) for first, count in w1_pieces]
         v_w = [keep.tile([P, S], U32, name=f"v_w{a}", align_bytes=64) for a in range(PASSES)]
         v_s = [keep.tile([P, S], U8, name=f"v_s{a}", align_bytes=64) for a in range(PASSES)]
         gains = keep.tile([P, 2 * S], F32, name="gains")
@@ -80,11 +80,11 @@ def tile_list_trench_dispute_features_kernel(
         y_w = keep.tile([P, T2], U32, name="y_w", align_bytes=64)
         y_s = keep.tile([P, T2], U8, name="y_s", align_bytes=64)
 
-        def load_scale_rows(plane, scales):
+        def load_scale_rows(plane, scales, cols):
             for quad in range(4):
                 nc.sync.dma_start(
                     out=plane[32 * quad : 32 * quad + 4, :].bitcast(I32).rearrange("i (a c) -> i a c", a=PASSES),
-                    in_=scales[:, 4 * quad : 4 * quad + 4, :].bitcast(I32).rearrange("a i c -> i a c"),
+                    in_=scales[:, 4 * quad : 4 * quad + 4, cols].bitcast(I32).rearrange("a i c -> i a c"),
                 )
 
         def load_w1(piece):
@@ -93,6 +93,7 @@ def tile_list_trench_dispute_features_kernel(
                 out=w1_w[piece][:].bitcast(I32).rearrange("p (a c) -> p a c", a=PASSES),
                 in_=w1_words[:, :, 2 * first : 2 * (first + count)].bitcast(I32).rearrange("a p c -> p a c"),
             )
+            load_scale_rows(w1_s[piece], w1_scales, slice(first, first + count))
 
         def load_tab_words(a):
             nc.sync.dma_start(
@@ -100,13 +101,13 @@ def tile_list_trench_dispute_features_kernel(
             )
 
         nc.vector.memset(tab_s[:].bitcast(I32), 0)
-        nc.vector.memset(w1_s[:].bitcast(I32), 0)
+        for plane in w1_s:
+            nc.vector.memset(plane[:].bitcast(I32), 0)
         nc.sync.dma_start(idx_notes[:], offs)
         load_tab_words(0)
-        load_scale_rows(tab_s, tab_scales)
+        load_scale_rows(tab_s, tab_scales, slice(0, T))
         load_tab_words(1)
         load_w1(0)
-        load_scale_rows(w1_s, w1_scales)
         nc.sync.dma_start(idx_pages[CLAIMS][:], offs2)
         nc.sync.dma_start(out=gain[CLAIMS], in_=wg1)
         load_w1(1)
@@ -187,7 +188,7 @@ def tile_list_trench_dispute_features_kernel(
                 piece = int(ROWS[c] * P >= EARLY)
                 first, count = w1_pieces[piece]
                 col = a * count + ROWS[c] * P - first
-                return w1_w[piece][:, 2 * col : 2 * (col + P)].bitcast(FP4X4), w1_s[:, a * H + ROWS[c] * P : a * H + (ROWS[c] + 1) * P]
+                return w1_w[piece][:, 2 * col : 2 * (col + P)].bitcast(FP4X4), w1_s[piece][:, col : col + P]
             g, tile = divmod(ROWS[c], W2_CHUNK)
             col = ((PASSES * g + a) * W2_CHUNK + tile) * P
             return w2_w[:, col : col + P].bitcast(FP8X4), w2_s[:, col : col + P]

@@ -44,28 +44,24 @@ def tile_list_trench_dispute_features_kernel(
     with ExitStack() as ctx:
         lists = ctx.enter_context(tc.tile_pool(name="lists", bufs=1))
         keep = ctx.enter_context(tc.tile_pool(name="keep", bufs=1))
-        ring = ctx.enter_context(tc.tile_pool(name="ring", bufs=1))
+        tables = ctx.enter_context(tc.tile_pool(name="tables", bufs=1))
         psum = ctx.enter_context(tc.psum_pool(name="psum", bufs=1))
 
         banks = [psum.tile([P, BANK], F32, name=f"bank{i}") for i in range(8)]
 
-        def slot(name, columns, dtype):
-            return ring.tile([P, columns], dtype, name=name, bufs=1, align_bytes=64)
+        def table_slot(a, columns, dtype):
+            return tables.tile([P, columns], dtype, name=f"table{a}", bufs=1, align_bytes=64)
 
         idx_notes = lists.tile([P, LIST_COLUMNS], U16, name="idx_notes")
         idx_pages = [lists.tile([P, LIST_COLUMNS], U16, name=f"idx_page{kind}") for kind in (CLAIMS, EVIDENCE)]
 
-        tab_w = [slot(f"table{a}", T, U32) for a in range(PASSES)]
-        tab_s = keep.tile([P, PASSES * T], U8, name="tab_s", align_bytes=64)
+        tab_w = [table_slot(a, T, U32) for a in range(PASSES)]
+        picked_s = keep.tile([P, S], U8, name="picked_s", align_bytes=64)
+        v_planes = keep.tile([P, PASSES * S], U8, name="v_planes", align_bytes=64)
         w1_pieces = [(0, EARLY), (EARLY, H - EARLY)]
-        w1_w = [
-            keep.tile([P, PASSES * 2 * count], U8, name=f"w1_w{first}", align_bytes=64) for first, count in w1_pieces
-        ]
-        w1_s = [keep.tile([P, PASSES * count], U8, name=f"w1_s{first}", align_bytes=64) for first, count in w1_pieces]
+        w1_s = [keep.tile([P, PASSES * EARLY], U8, name="w1_s0", align_bytes=64)]
         v_w = [keep.tile([P, S], U32, name=f"v_w{a}", align_bytes=64) for a in range(PASSES)]
-        v_s = [keep.tile([P, S], U8, name=f"v_s{a}", align_bytes=64) for a in range(PASSES)]
-        gains = keep.tile([P, 2 * S], F32, name="gains")
-        gain = [gains[:, 0:S], gains[:, S : 2 * S]]
+        v_s = [v_planes[:, a * S : (a + 1) * S] for a in range(PASSES)]
         ident = keep.tile([P, P], F32, name="ident")
         pages = [
             [keep.tile([P, T2], F32, name=f"page{kind}_{i}") for i in range(count)]
@@ -93,24 +89,47 @@ def tile_list_trench_dispute_features_kernel(
                 out=w1_w[piece][:].bitcast(I32).rearrange("p (a c) -> p a c", a=PASSES),
                 in_=w1_words[:, :, 2 * first : 2 * (first + count)].bitcast(I32).rearrange("a p c -> p a c"),
             )
-            load_scale_rows(w1_s[piece], w1_scales, slice(first, first + count))
 
         def load_tab_words(a):
             nc.sync.dma_start(
                 out=tab_w[a][:].bitcast(I32), in_=tab_words[a].rearrange("p t i -> p (t i)").bitcast(I32)
             )
 
-        nc.vector.memset(tab_s[:].bitcast(I32), 0)
-        for plane in w1_s:
-            nc.vector.memset(plane[:].bitcast(I32), 0)
-        nc.sync.dma_start(idx_notes[:], offs)
-        load_tab_words(0)
-        load_scale_rows(tab_s, tab_scales, slice(0, T))
-        load_tab_words(1)
+        with tc.tile_pool(name="early", bufs=1) as early:
+            tab_s = early.tile([P, T], U8, name="tab_s", align_bytes=64)
+            nc.vector.memset(tab_s[:].bitcast(I32), 0)
+            nc.vector.memset(w1_s[0][:].bitcast(I32), 0)
+            nc.vector.memset(v_planes[:].bitcast(I32), 0)
+            nc.sync.dma_start(idx_notes[:], offs)
+            load_tab_words(0)
+            nc.scalar.dma_start(
+                out=tab_s[0:P:4, :].bitcast(I32), in_=tab_scales.bitcast(I32).rearrange("a q c -> q a c")
+            )
+            nc.sync.dma_start(idx_pages[CLAIMS][:], offs2)
+            load_scale_rows(w1_s[0], w1_scales, slice(0, EARLY))
+            load_tab_words(1)
+            nc.sync.dma_start(idx_pages[EVIDENCE][:], offs3)
+            nc.vector.tensor_copy(picked_s[:], tab_s[:].indirect(idx_notes[:]))
+
+        ring = ctx.enter_context(tc.tile_pool(name="ring", bufs=1))
+
+        def slot(name, columns, dtype):
+            return ring.tile([P, columns], dtype, name=name, bufs=1, align_bytes=64)
+
+        w1_w = [slot(f"w1_w{first}", PASSES * 2 * count, U8) for first, count in w1_pieces]
+        w1_s.append(slot("w1_s1", PASSES * (H - EARLY), U8))
+        gains = slot("gains", 2 * S, F32)
+        gain = [gains[:, 0:S], gains[:, S : 2 * S]]
+        for quad in range(4):
+            nc.sync.dma_start(
+                out=v_planes[32 * quad : 32 * quad + 4, :].bitcast(I32),
+                in_=picked_s[32 * quad : 32 * quad + 32 : 4, :].bitcast(I32),
+            )
         load_w1(0)
-        nc.sync.dma_start(idx_pages[CLAIMS][:], offs2)
         nc.sync.dma_start(out=gain[CLAIMS], in_=wg1)
         load_w1(1)
+        nc.gpsimd.memset(w1_s[1][:].bitcast(I32), 0)
+        load_scale_rows(w1_s[1], w1_scales, slice(EARLY, H))
         for page in pages[CLAIMS][:2]:
             nc.vector.memset(page[:].bitcast(I32), 0)
         make_identity(nc, ident[:])
@@ -124,8 +143,6 @@ def tile_list_trench_dispute_features_kernel(
             return slice(part * LIST_COLUMNS // FIRST_PARTS, (part + 1) * LIST_COLUMNS // FIRST_PARTS)
 
         nc.vector.tensor_copy(v_w[0][:], tab_w[0][:].indirect(idx_notes[:]))
-        for a in range(PASSES):
-            nc.vector.tensor_copy(v_s[a][:], tab_s[:, a * T : (a + 1) * T].indirect(idx_notes[:]))
         for part in range(FIRST_PARTS):
             nc.vector.tensor_copy(v_w[1][:, entries(part)], tab_w[1][:].indirect(idx_notes[:, list_columns(part)]))
 
@@ -143,7 +160,7 @@ def tile_list_trench_dispute_features_kernel(
                 w2_raw[g, a] = raw
 
         def load_w3(b):
-            raw = slot(f"table{b}", PACK * N, F32)
+            raw = table_slot(b, PACK * N, F32)
             nc.sync.dma_start(out=raw[:], in_=w3[b * K_PASS : (b + 1) * K_PASS, :].rearrange("(p j) n -> p (j n)", j=PACK))
             w3_raw[b] = raw
 
@@ -226,7 +243,7 @@ def tile_list_trench_dispute_features_kernel(
                     lhsT=codes,
                     lhsT_scale=scales,
                     rhs=v_w[a][:].bitcast(FP8X4),
-                    rhs_scale=v_s[a][:],
+                    rhs_scale=v_s[a],
                     start=(a == 0),
                     stop=(a == PASSES - 1),
                 )
@@ -370,7 +387,6 @@ def tile_list_trench_dispute_features_kernel(
         load_w2(0)
         load_w2(1)
         nc.sync.dma_start(out=gain[EVIDENCE], in_=wg2)
-        nc.sync.dma_start(idx_pages[EVIDENCE][:], offs3)
         for g in range(2, W2_CHUNKS):
             load_w2(g)
         for c in range(ROW_TILES):
@@ -465,7 +481,7 @@ def tile_list_trench_dispute_features_kernel(
                 lhsT=codes,
                 lhsT_scale=scales,
                 rhs=v_w[a][:].bitcast(FP8X4),
-                rhs_scale=v_s[a][:],
+                rhs_scale=v_s[a],
                 start=True,
                 stop=True,
             )

@@ -58,7 +58,8 @@ def tile_list_trench_dispute_features_kernel(
         tab_w = [table_slot(a, T, U32) for a in range(PASSES)]
         picked_s = keep.tile([P, S], U8, name="picked_s", align_bytes=64)
         v_planes = keep.tile([P, PASSES * S], U8, name="v_planes", align_bytes=64)
-        w1_pieces = [(0, EARLY), (EARLY, H - EARLY)]
+        w1_pieces = [(0, EARLY), (EARLY, EARLY), (2 * EARLY, H - 2 * EARLY)]
+        w1_w = [keep.tile([P, PASSES * 2 * EARLY], U8, name="w1_w0", align_bytes=64)]
         w1_s = [keep.tile([P, PASSES * EARLY], U8, name="w1_s0", align_bytes=64)]
         v_w = [keep.tile([P, S], U32, name=f"v_w{a}", align_bytes=64) for a in range(PASSES)]
         v_s = [v_planes[:, a * S : (a + 1) * S] for a in range(PASSES)]
@@ -109,6 +110,7 @@ def tile_list_trench_dispute_features_kernel(
             load_scale_rows(w1_s[0], w1_scales, slice(0, EARLY))
             load_tab_words(1)
             nc.sync.dma_start(idx_pages[EVIDENCE][:], offs3)
+            load_w1(0)
             nc.vector.tensor_copy(picked_s[:], tab_s[:].indirect(idx_notes[:]))
 
         ring = ctx.enter_context(tc.tile_pool(name="ring", bufs=1))
@@ -116,7 +118,7 @@ def tile_list_trench_dispute_features_kernel(
         def slot(name, columns, dtype):
             return ring.tile([P, columns], dtype, name=name, bufs=1, align_bytes=64)
 
-        w1_w = [slot(f"w1_w{first}", PASSES * 2 * count, U8) for first, count in w1_pieces]
+        w1_w.extend(slot(f"w1_w{first}", PASSES * 2 * count, U8) for first, count in w1_pieces[1:])
         w1_s.append(slot("w1_s1", PASSES * (H - EARLY), U8))
         gains = slot("gains", 2 * S, F32)
         gain = [gains[:, 0:S], gains[:, S : 2 * S]]
@@ -125,7 +127,6 @@ def tile_list_trench_dispute_features_kernel(
                 out=v_planes[32 * quad : 32 * quad + 4, :].bitcast(I32),
                 in_=picked_s[32 * quad : 32 * quad + 32 : 4, :].bitcast(I32),
             )
-        load_w1(0)
         nc.sync.dma_start(out=gain[CLAIMS], in_=wg1)
         load_w1(1)
         nc.gpsimd.memset(w1_s[1][:].bitcast(I32), 0)
@@ -202,10 +203,12 @@ def tile_list_trench_dispute_features_kernel(
 
         def stationary(kind, c, a):
             if kind == CLAIMS:
-                piece = int(ROWS[c] * P >= EARLY)
+                piece = min(ROWS[c] * P // EARLY, 2)
                 first, count = w1_pieces[piece]
                 col = a * count + ROWS[c] * P - first
-                return w1_w[piece][:, 2 * col : 2 * (col + P)].bitcast(FP4X4), w1_s[piece][:, col : col + P]
+                late = min(piece, 1)
+                row = a * (EARLY, H - EARLY)[late] + ROWS[c] * P - late * EARLY
+                return w1_w[piece][:, 2 * col : 2 * (col + P)].bitcast(FP4X4), w1_s[late][:, row : row + P]
             g, tile = divmod(ROWS[c], W2_CHUNK)
             col = ((PASSES * g + a) * W2_CHUNK + tile) * P
             return w2_w[:, col : col + P].bitcast(FP8X4), w2_s[:, col : col + P]
@@ -319,29 +322,29 @@ def tile_list_trench_dispute_features_kernel(
                 SUBTRACT,
             )
 
-        def last_difference(quarter):
+        def last_difference(first, blocks):
             b, quad = divmod(LAST, PACK)
-            f, pair = divmod(quarter, 2)
+            f, u = divmod(first, 4)
             views = [
-                tile[:].rearrange("t (f h u x) -> t f h u x", f=2, h=2, u=4)[:, f, :, 2 * pair : 2 * pair + 2, :]
+                tile[:].rearrange("t (f h u x) -> t f h u x", f=2, h=2, u=4)[:, f, :, u : u + blocks, :]
                 for tile in (z_t[b], squares[CLAIMS, LAST], squares[EVIDENCE, LAST])
             ]
             nc.vector.tensor_tensor(views[0][:, :, :, 64 * quad : 64 * (quad + 1)], views[1], views[2], SUBTRACT)
 
-        def turn_z(b, quarter, bank, rounded):
+        def turn_z(b, first, blocks, bank, rounded):
             words = z_t[b][:].bitcast(F32)
-            f, pair = divmod(quarter, 2)
-            for u in range(2):
+            f, u0 = divmod(first, 4)
+            for u in range(blocks):
                 for half in range(2):
-                    g = 8 * f + 4 * half + 2 * pair + u
+                    g = 8 * f + 4 * half + u0 + u
                     nc.tensor.transpose(
                         banks[bank][:, (2 * u + half) * P : (2 * u + half + 1) * P],
                         words[:, g * P : (g + 1) * P],
                         ident[:],
                     )
-            (nc.vector.tensor_copy if b == PASSES - 1 and quarter == QUARTERS - 1 else nc.scalar.copy)(
-                rounded.bitcast(F32).rearrange("p (u t h) -> p u t h", u=2, h=2),
-                banks[bank][:].rearrange("p (u h t) -> p u t h", u=2, h=2),
+            (nc.vector.tensor_copy if b == PASSES - 1 and first == 6 else nc.scalar.copy)(
+                rounded.bitcast(F32).rearrange("p (u t h) -> p u t h", u=blocks, h=2),
+                banks[bank][:, : 2 * blocks * P].rearrange("p (u h t) -> p u t h", u=blocks, h=2),
             )
 
         z_w = {}
@@ -352,11 +355,11 @@ def tile_list_trench_dispute_features_kernel(
             cols = slice(first * QUARTER, (first + count) * QUARTER)
             nc.vector.quantize_mx(out=codes.bitcast(FP8X4), scales=z_s[b][:, cols], in_=rounded)
 
-        y_banks = [(0, 1), (4, 5), (2, 3), (6, 7)]
+        y_banks = [(0, 1), (2, 3), (5, 6), (7, 4)]
 
-        def y_pass(b, quarter):
+        def y_pass(b, quarter, rows=range(PACK)):
             cols = slice(quarter * QUARTER, (quarter + 1) * QUARTER)
-            for j in range(PACK):
+            for j in rows:
                 nc.tensor.matmul_mx(
                     out=banks[y_banks[quarter][j // 2]][:, (j % 2) * QUARTER : (j % 2 + 1) * QUARTER],
                     lhsT=w3_w[b][:, j * P : (j + 1) * P].bitcast(FP8X4),
@@ -389,6 +392,7 @@ def tile_list_trench_dispute_features_kernel(
         nc.sync.dma_start(out=gain[EVIDENCE], in_=wg2)
         for g in range(2, W2_CHUNKS):
             load_w2(g)
+        load_w1(2)
         for c in range(ROW_TILES):
             load_cons(c)
         for b in range(PASSES):
@@ -464,7 +468,7 @@ def tile_list_trench_dispute_features_kernel(
         first_pass = [slot(name, 2 * PACK * QUARTER, BF16) for name in ("raw0", "raw3")]
         for quarter in range(QUARTERS):
             f, pair_of = divmod(quarter, 2)
-            turn_z(0, quarter, (0, 1, 6, 7)[quarter], first_pass[f][:, pair_of * PACK * QUARTER : (pair_of + 1) * PACK * QUARTER])
+            turn_z(0, 2 * quarter, 2, (0, 1, 6, 7)[quarter], first_pass[f][:, pair_of * PACK * QUARTER : (pair_of + 1) * PACK * QUARTER])
         round_w3(1, "rounded1")
         scatter(CLAIMS, 6)
         difference(5)
@@ -487,27 +491,42 @@ def tile_list_trench_dispute_features_kernel(
             )
         scatter(EVIDENCE, LAST)
 
-        codes = slot("cons_last", BANK + N, U32)
-        quantize_w3(0, codes[:, BANK:])
-        quantize_z(0, 0, 2, first_pass[0][:], codes[:, :BANK])
-        squared(EVIDENCE, LAST, (4, 5, 6, 7), slot("raw6", T2, F32))
-        for quarter in range(QUARTERS):
-            last_difference(quarter)
-        codes = slot("raw6", BANK + N, U32)
-        quantize_z(0, 2, 1, first_pass[1][:, : PACK * QUARTER], codes[:, :QUARTER])
-        quantize_w3(1, codes[:, BANK:])
+        def quantize_first(quarter, codes):
+            f, pair_of = divmod(quarter, 2)
+            width = PACK * QUARTER
+            quantize_z(0, quarter, 1, first_pass[f][:, pair_of * width : (pair_of + 1) * width], codes)
+
+        def quantize_last(quarter):
+            quantize_z(1, quarter, 1, turned[quarter][:], z_last[:, quarter * QUARTER : (quarter + 1) * QUARTER])
+
+        pieces = [(0, 1), (1, 1), (2, 2), (4, 2), (6, 2)]
+        codes = slot("cons_last", QUARTER + N, U32)
+        quantize_first(0, codes[:, :QUARTER])
+        quantize_w3(0, codes[:, QUARTER:])
+        squared(EVIDENCE, LAST, (4, 5, 6, 7, 3), slot("raw6", T2, F32), widths=[blocks for first, blocks in pieces])
+        for first, blocks in pieces:
+            last_difference(first, blocks)
+        codes = slot("raw6", QUARTER + N, U32)
+        quantize_first(1, codes[:, :QUARTER])
+        quantize_w3(1, codes[:, QUARTER:])
         y_pass(0, 0)
+        turned = [slot(f"turned{quarter}", PACK * QUARTER, BF16) for quarter in range(QUARTERS)]
+        for (first, blocks), bank in zip(pieces[:-1], (4, 5, 6, 7)):
+            quarter, u = divmod(first, 2)
+            turn_z(1, first, blocks, bank, turned[quarter][:, u * PACK * P : (u + blocks) * PACK * P])
+        quantize_last(0)
+        quantize_last(1)
+        quantize_first(2, slot("turned0", QUARTER, U32)[:])
+        turn_z(1, 6, 2, 4, turned[3][:])
+        y_pass(0, 1)
+        quantize_last(2)
+        quantize_first(3, slot("turned1", QUARTER, U32)[:])
+        quantize_last(3)
         for quarter in range(QUARTERS):
-            turned = ring.tile([P, PACK * QUARTER], BF16, name="turned", bufs=QUARTERS, align_bytes=64)
-            turn_z(1, quarter, 4 + quarter, turned[:])
-            quantize_z(1, quarter, 1, turned[:], z_last[:, quarter * QUARTER : (quarter + 1) * QUARTER])
-            if quarter == 0:
-                quantize_z(0, 3, 1, first_pass[1][:, PACK * QUARTER :], codes[:, QUARTER:BANK])
-        y_pass(0, 2)
-        for quarter in range(QUARTERS):
-            if quarter % 2 == 1:
-                y_pass(0, quarter)
-            y_pass(1, quarter)
+            for rows in ((0, 1), (2, 3)):
+                if quarter >= 2:
+                    y_pass(0, quarter, rows)
+                y_pass(1, quarter, rows)
             finish(quarter)
         for cols in (slice(0, 3 * QUARTER), slice(3 * QUARTER, T2)):
             nc.sync.dma_start(out=y_words[:, cols], in_=y_w[:, cols].bitcast(I32))

@@ -370,8 +370,27 @@ def tile_list_trench_dispute_features_kernel(
                     stop=(b == PASSES - 1 and j % 2 == 1),
                 )
 
+        def y_block(b, block):
+            cols = slice(block * P, (block + 1) * P)
+            for j in range(PACK):
+                nc.tensor.matmul_mx(
+                    out=banks[y_banks[0][block]][:, j * P : (j + 1) * P],
+                    lhsT=w3_w[b][:, j * P : (j + 1) * P].bitcast(FP8X4),
+                    lhsT_scale=w3_s[:, b * N + j * P : b * N + (j + 1) * P],
+                    rhs=z_w[b, 0][:, cols].bitcast(FP8X4),
+                    rhs_scale=z_s[b][:, cols],
+                    start=(b == 0 and j == 0),
+                    stop=(b == PASSES - 1 and j == PACK - 1),
+                )
+
         y_rows = out_0.rearrange("(p j) t -> p j t", j=PACK)
         y_words = out_1[0].rearrange("p t i -> p (t i)").bitcast(I32)
+
+        y_bf16 = {}
+
+        def quantize_y(quarter):
+            cols = slice(quarter * QUARTER, (quarter + 1) * QUARTER)
+            nc.vector.quantize_mx(out=y_w[:, cols].bitcast(FP8X4), scales=y_s[:, cols], in_=y_bf16[quarter][:])
 
         def finish(quarter):
             cols = slice(quarter * QUARTER, (quarter + 1) * QUARTER)
@@ -379,13 +398,20 @@ def tile_list_trench_dispute_features_kernel(
             for i, bank in enumerate(y_banks[quarter]):
                 part = y_all[:, i * BANK : (i + 1) * BANK]
                 nc.scalar.copy(part, banks[bank][:])
-                nc.sync.dma_start(out=y_rows[:, 2 * i : 2 * i + 2, cols], in_=part.rearrange("p (j t) -> p j t", j=2))
+                if quarter == 0:
+                    target, rows = y_rows[:, :, i * P : (i + 1) * P], PACK
+                else:
+                    target, rows = y_rows[:, 2 * i : 2 * i + 2, cols], 2
+                nc.sync.dma_start(out=target, in_=part.rearrange("p (j t) -> p j t", j=rows))
             y_rounded = ring.tile([P, PACK * QUARTER], BF16, name="y_rounded", bufs=QUARTERS, align_bytes=64)
+            blocks = 2 if quarter == 0 else 1
             nc.vector.tensor_copy(
-                y_rounded[:].rearrange("p (c i j) -> p c j i", i=4, j=PACK),
-                y_all[:].rearrange("p (j c i) -> p c j i", j=PACK, i=4),
+                y_rounded[:].rearrange("p (b c i j) -> p b c j i", b=blocks, i=4, j=PACK),
+                y_all[:].rearrange("p (b j c i) -> p b c j i", b=blocks, j=PACK, i=4),
             )
-            nc.vector.quantize_mx(out=y_w[:, cols].bitcast(FP8X4), scales=y_s[:, cols], in_=y_rounded[:])
+            y_bf16[quarter] = y_rounded
+            if quarter > 0:
+                quantize_y(quarter - 1)
 
         load_w2(0)
         load_w2(1)
@@ -497,7 +523,7 @@ def tile_list_trench_dispute_features_kernel(
             quantize_z(0, quarter, 1, first_pass[f][:, pair_of * width : (pair_of + 1) * width], codes)
 
         def quantize_last(quarter):
-            quantize_z(1, quarter, 1, turned[quarter][:], z_last[:, quarter * QUARTER : (quarter + 1) * QUARTER])
+            quantize_z(1, quarter, 1, turned[2 * quarter][:], z_last[:, quarter * QUARTER : (quarter + 1) * QUARTER])
 
         pieces = [(0, 1), (1, 1), (2, 2), (4, 2), (6, 2)]
         codes = slot("cons_last", QUARTER + N, U32)
@@ -506,28 +532,34 @@ def tile_list_trench_dispute_features_kernel(
         squared(EVIDENCE, LAST, (4, 5, 6, 7, 3), slot("raw6", T2, F32), widths=[blocks for first, blocks in pieces])
         for first, blocks in pieces:
             last_difference(first, blocks)
-        codes = slot("raw6", QUARTER + N, U32)
-        quantize_first(1, codes[:, :QUARTER])
-        quantize_w3(1, codes[:, QUARTER:])
-        y_pass(0, 0)
-        turned = [slot(f"turned{quarter}", PACK * QUARTER, BF16) for quarter in range(QUARTERS)]
+        quantize_w3(1, slot("raw6", N, U32)[:])
+        for block in range(2):
+            y_block(0, block)
+        turned = {
+            first: slot(f"turned{first}", blocks * PACK * P, BF16) for first, blocks in pieces
+        }
         for (first, blocks), bank in zip(pieces[:-1], (4, 5, 6, 7)):
-            quarter, u = divmod(first, 2)
-            turn_z(1, first, blocks, bank, turned[quarter][:, u * PACK * P : (u + blocks) * PACK * P])
-        quantize_last(0)
+            turn_z(1, first, blocks, bank, turned[first][:])
+        z_w[1, 0] = z_last[:, :QUARTER]
+        for block in range(2):
+            cols = slice(block * P, (block + 1) * P)
+            nc.vector.quantize_mx(out=z_last[:, cols].bitcast(FP8X4), scales=z_s[1][:, cols], in_=turned[block][:])
+        quantize_first(1, slot("turned0", QUARTER, U32)[:])
         quantize_last(1)
-        quantize_first(2, slot("turned0", QUARTER, U32)[:])
-        turn_z(1, 6, 2, 4, turned[3][:])
-        y_pass(0, 1)
+        quantize_first(2, slot("turned1", QUARTER, U32)[:])
+        turn_z(1, 6, 2, 4, turned[6][:])
         quantize_last(2)
-        quantize_first(3, slot("turned1", QUARTER, U32)[:])
+        quantize_first(3, slot("turned2", QUARTER, U32)[:])
         quantize_last(3)
-        for quarter in range(QUARTERS):
+        for block in range(2):
+            y_block(1, block)
+        finish(0)
+        for quarter in range(1, QUARTERS):
             for rows in ((0, 1), (2, 3)):
-                if quarter >= 2:
-                    y_pass(0, quarter, rows)
+                y_pass(0, quarter, rows)
                 y_pass(1, quarter, rows)
             finish(quarter)
+        quantize_y(QUARTERS - 1)
         for cols in (slice(0, 3 * QUARTER), slice(3 * QUARTER, T2)):
             nc.sync.dma_start(out=y_words[:, cols], in_=y_w[:, cols].bitcast(I32))
         for quad in range(4):

@@ -58,15 +58,15 @@ def tile_list_trench_dispute_features_kernel(
         tab_w = [table_slot(a, T, U32) for a in range(PASSES)]
         picked_s = keep.tile([P, S], U8, name="picked_s", align_bytes=64)
         v_planes = keep.tile([P, PASSES * S], U8, name="v_planes", align_bytes=64)
-        w1_pieces = [(0, EARLY), (EARLY, EARLY), (2 * EARLY, H - 2 * EARLY)]
-        w1_w = [keep.tile([P, PASSES * 2 * EARLY], U8, name="w1_w0", align_bytes=64)]
+        w1_pieces = [(0, P), (P, 3 * P), (4 * P, 4 * P)]
+        w1_w = [keep.tile([P, PASSES * 2 * P], U8, name="w1_w0", align_bytes=64)]
         w1_s = [keep.tile([P, PASSES * EARLY], U8, name="w1_s0", align_bytes=64)]
         v_w = [keep.tile([P, S], U32, name=f"v_w{a}", align_bytes=64) for a in range(PASSES)]
         v_s = [v_planes[:, a * S : (a + 1) * S] for a in range(PASSES)]
         ident = keep.tile([P, P], F32, name="ident")
         pages = [
             [keep.tile([P, T2], F32, name=f"page{kind}_{i}") for i in range(count)]
-            for kind, count in ((CLAIMS, 3), (EVIDENCE, 2))
+            for kind, count in ((CLAIMS, 4), (EVIDENCE, 2))
         ]
         w2_w = keep.tile([P, PASSES * H], U32, name="w2_w", align_bytes=64)
         w2_s = keep.tile([P, PASSES * H], U8, name="w2_s", align_bytes=64)
@@ -203,10 +203,10 @@ def tile_list_trench_dispute_features_kernel(
 
         def stationary(kind, c, a):
             if kind == CLAIMS:
-                piece = min(ROWS[c] * P // EARLY, 2)
+                piece = (ROWS[c] > 0) + (ROWS[c] > 3)
                 first, count = w1_pieces[piece]
                 col = a * count + ROWS[c] * P - first
-                late = min(piece, 1)
+                late = int(ROWS[c] * P >= EARLY)
                 row = a * (EARLY, H - EARLY)[late] + ROWS[c] * P - late * EARLY
                 return w1_w[piece][:, 2 * col : 2 * (col + P)].bitcast(FP4X4), w1_s[late][:, row : row + P]
             g, tile = divmod(ROWS[c], W2_CHUNK)
@@ -235,7 +235,7 @@ def tile_list_trench_dispute_features_kernel(
                 else:
                     nc.scalar.copy(values, bank[:, 0:width])
                     nc.gpsimd.tensor_tensor(values, values, gains[:, entries(part)], MULT)
-                window = page_of(CLAIMS, 0)[:].indirect(idx_pages[CLAIMS][:, list_columns(part)])
+                window = pages[CLAIMS][3 * part][:].indirect(idx_pages[CLAIMS][:, list_columns(part)])
                 nc.vector.tensor_copy(window, values)
 
         def product(kind, c, bank):
@@ -285,6 +285,8 @@ def tile_list_trench_dispute_features_kernel(
             widths = widths or [T2 // P // len(page_banks)] * len(page_banks)
             pieces = [(bank, sum(widths[:n]), widths[n]) for n, bank in enumerate(page_banks)]
             terms = [cons_rows[c], page_of(kind, c)] if kind == CLAIMS else [page_of(kind, c)]
+            if (kind, c) == (CLAIMS, 0):
+                terms.append(pages[CLAIMS][3])
             if result is None:
                 result = ring.tile([P, T2], F32, name=f"squares{kind}", bufs=(4, 3)[kind])
             squares[kind, c] = result
@@ -298,12 +300,12 @@ def tile_list_trench_dispute_features_kernel(
                         rhs=ident[:],
                         is_transpose=True,
                         start=(len(terms) == 1 or (i == 0 and u == 0)),
-                        stop=(len(terms) == 1 or (i == 1 and u == blocks - 1)),
+                        stop=(len(terms) == 1 or (i == len(terms) - 1 and u == blocks - 1)),
                     )
 
-            if kind == CLAIMS:
+            for i in range(len(terms) - 1):
                 for piece in pieces:
-                    transposes(0, *piece)
+                    transposes(i, *piece)
             for bank, first, blocks in pieces:
                 transposes(len(terms) - 1, bank, first, blocks)
                 f, u = divmod(first, 4)

@@ -33,8 +33,6 @@ W2_CHUNK = 2
 W2_CHUNKS = ROW_TILES // W2_CHUNK
 FIRST_PARTS = 2
 CLAIMS, EVIDENCE = 0, 1
-ROWS = [0, 2, 3, 1, 4, 5, 6, 7]
-EARLY = 2 * P
 
 
 def tile_list_trench_dispute_features_kernel(
@@ -58,20 +56,20 @@ def tile_list_trench_dispute_features_kernel(
         tab_w = [table_slot(a, T, U32) for a in range(PASSES)]
         picked_s = keep.tile([P, S], U8, name="picked_s", align_bytes=64)
         v_planes = keep.tile([P, PASSES * S], U8, name="v_planes", align_bytes=64)
-        w1_pieces = [(0, P), (P, 3 * P), (4 * P, 4 * P)]
-        w1_w = [keep.tile([P, PASSES * 2 * P], U8, name="w1_w0", align_bytes=64)]
-        w1_s = [keep.tile([P, PASSES * EARLY], U8, name="w1_s0", align_bytes=64)]
+        w1_pieces = [slice(0, 2 * P), slice(2 * P, 4 * P), slice(4 * P, H)]
+        w1_w = [keep.tile([P, PASSES * 4 * P], U8, name="w1_w0", align_bytes=64)]
+        w1_s = [keep.tile([P, PASSES * 2 * P], U8, name="w1_s0", align_bytes=64)]
         v_w = [keep.tile([P, S], U32, name=f"v_w{a}", align_bytes=64) for a in range(PASSES)]
         v_s = [v_planes[:, a * S : (a + 1) * S] for a in range(PASSES)]
         ident = keep.tile([P, P], F32, name="ident")
         pages = [
             [keep.tile([P, T2], F32, name=f"page{kind}_{i}") for i in range(count)]
-            for kind, count in ((CLAIMS, 4), (EVIDENCE, 2))
+            for kind, count in ((CLAIMS, 3), (EVIDENCE, 2))
         ]
         w2_w = keep.tile([P, PASSES * H], U32, name="w2_w", align_bytes=64)
         w2_s = keep.tile([P, PASSES * H], U8, name="w2_s", align_bytes=64)
         w3_s = keep.tile([P, PASSES * N], U8, name="w3_s", align_bytes=64)
-        z_t = {1: keep.tile([P, PACK * T2], BF16, name="z_t1")}
+        z_t = [keep.tile([P, PACK * T2], BF16, name=f"z_t{b}") for b in range(PASSES)]
         z_s = [keep.tile([P, T2], U8, name=f"z_s{b}", align_bytes=64) for b in range(PASSES)]
         z_last = keep.tile([P, T2], U32, name="z_last", align_bytes=64)
         y_w = keep.tile([P, T2], U32, name="y_w", align_bytes=64)
@@ -85,10 +83,10 @@ def tile_list_trench_dispute_features_kernel(
                 )
 
         def load_w1(piece):
-            first, count = w1_pieces[piece]
+            cols = w1_pieces[piece]
             nc.sync.dma_start(
                 out=w1_w[piece][:].bitcast(I32).rearrange("p (a c) -> p a c", a=PASSES),
-                in_=w1_words[:, :, 2 * first : 2 * (first + count)].bitcast(I32).rearrange("a p c -> p a c"),
+                in_=w1_words[:, :, 2 * cols.start : 2 * cols.stop].bitcast(I32).rearrange("a p c -> p a c"),
             )
 
         def load_tab_words(a):
@@ -107,7 +105,7 @@ def tile_list_trench_dispute_features_kernel(
                 out=tab_s[0:P:4, :].bitcast(I32), in_=tab_scales.bitcast(I32).rearrange("a q c -> q a c")
             )
             nc.sync.dma_start(idx_pages[CLAIMS][:], offs2)
-            load_scale_rows(w1_s[0], w1_scales, slice(0, EARLY))
+            load_scale_rows(w1_s[0], w1_scales, w1_pieces[0])
             load_tab_words(1)
             nc.sync.dma_start(idx_pages[EVIDENCE][:], offs3)
             load_w1(0)
@@ -118,8 +116,9 @@ def tile_list_trench_dispute_features_kernel(
         def slot(name, columns, dtype):
             return ring.tile([P, columns], dtype, name=name, bufs=1, align_bytes=64)
 
-        w1_w.extend(slot(f"w1_w{first}", PASSES * 2 * count, U8) for first, count in w1_pieces[1:])
-        w1_s.append(slot("w1_s1", PASSES * (H - EARLY), U8))
+        for piece, cols in list(enumerate(w1_pieces))[1:]:
+            w1_w.append(slot(f"w1_w{piece}", PASSES * 2 * (cols.stop - cols.start), U8))
+            w1_s.append(slot(f"w1_s{piece}", PASSES * (cols.stop - cols.start), U8))
         gains = slot("gains", 2 * S, F32)
         gain = [gains[:, 0:S], gains[:, S : 2 * S]]
         for quad in range(4):
@@ -129,8 +128,9 @@ def tile_list_trench_dispute_features_kernel(
             )
         nc.sync.dma_start(out=gain[CLAIMS], in_=wg1)
         load_w1(1)
-        nc.gpsimd.memset(w1_s[1][:].bitcast(I32), 0)
-        load_scale_rows(w1_s[1], w1_scales, slice(EARLY, H))
+        for plane in w1_s[1:]:
+            nc.gpsimd.memset(plane[:].bitcast(I32), 0)
+        load_scale_rows(w1_s[1], w1_scales, w1_pieces[1])
         for page in pages[CLAIMS][:2]:
             nc.vector.memset(page[:].bitcast(I32), 0)
         make_identity(nc, ident[:])
@@ -167,7 +167,7 @@ def tile_list_trench_dispute_features_kernel(
 
         def load_cons(c):
             rows = ring.tile([P, T2], F32, name="cons_rows", bufs=LAST) if c < LAST else slot("cons_last", T2, F32)
-            nc.sync.dma_start(out=rows[:], in_=cons[ROWS[c] * P : (ROWS[c] + 1) * P, :])
+            nc.sync.dma_start(out=rows[:], in_=cons[c * P : (c + 1) * P, :])
             cons_rows[c] = rows
 
         chunk_words = PASSES * W2_CHUNK * P
@@ -203,40 +203,40 @@ def tile_list_trench_dispute_features_kernel(
 
         def stationary(kind, c, a):
             if kind == CLAIMS:
-                piece = (ROWS[c] > 0) + (ROWS[c] > 3)
-                first, count = w1_pieces[piece]
-                col = a * count + ROWS[c] * P - first
-                late = int(ROWS[c] * P >= EARLY)
-                row = a * (EARLY, H - EARLY)[late] + ROWS[c] * P - late * EARLY
-                return w1_w[piece][:, 2 * col : 2 * (col + P)].bitcast(FP4X4), w1_s[late][:, row : row + P]
-            g, tile = divmod(ROWS[c], W2_CHUNK)
+                piece = min(c // 2, 2)
+                cols = w1_pieces[piece]
+                col = a * (cols.stop - cols.start) + c * P - cols.start
+                return w1_w[piece][:, 2 * col : 2 * (col + P)].bitcast(FP4X4), w1_s[piece][:, col : col + P]
+            g, tile = divmod(c, W2_CHUNK)
             col = ((PASSES * g + a) * W2_CHUNK + tile) * P
             return w2_w[:, col : col + P].bitcast(FP8X4), w2_s[:, col : col + P]
 
         h = {}
 
         def first_features():
+            width = S // FIRST_PARTS
             for part in range(FIRST_PARTS):
-                bank, width = banks[6 + part], S // FIRST_PARTS
-                for a in range(PASSES):
-                    codes, scales = stationary(CLAIMS, 0, a)
-                    nc.tensor.matmul_mx(
-                        out=bank[:, 0:width],
-                        lhsT=codes,
-                        lhsT_scale=scales,
-                        rhs=v_w[a][:, entries(part)].bitcast(FP8X4),
-                        rhs_scale=v_s[a][:, entries(part)],
-                        start=(a == 0),
-                        stop=(a == PASSES - 1),
-                    )
-                values = h[CLAIMS, 0][:, entries(part)]
-                if part == 0:
-                    nc.vector.tensor_tensor(values, bank[:, 0:width], gains[:, entries(part)], MULT)
-                else:
-                    nc.scalar.copy(values, bank[:, 0:width])
-                    nc.gpsimd.tensor_tensor(values, values, gains[:, entries(part)], MULT)
-                window = pages[CLAIMS][3 * part][:].indirect(idx_pages[CLAIMS][:, list_columns(part)])
-                nc.vector.tensor_copy(window, values)
+                for c in range(2):
+                    bank = banks[4 + 2 * part + c]
+                    for a in range(PASSES):
+                        codes, scales = stationary(CLAIMS, c, a)
+                        nc.tensor.matmul_mx(
+                            out=bank[:, 0:width],
+                            lhsT=codes,
+                            lhsT_scale=scales,
+                            rhs=v_w[a][:, entries(part)].bitcast(FP8X4),
+                            rhs_scale=v_s[a][:, entries(part)],
+                            start=(a == 0),
+                            stop=(a == PASSES - 1),
+                        )
+                    values = h[CLAIMS, c][:, entries(part)]
+                    if (part, c) == (0, 0):
+                        nc.vector.tensor_tensor(values, bank[:, 0:width], gains[:, entries(part)], MULT)
+                    else:
+                        nc.scalar.copy(values, bank[:, 0:width])
+                        nc.gpsimd.tensor_tensor(values, values, gains[:, entries(part)], MULT)
+                    window = page_of(CLAIMS, c)[:].indirect(idx_pages[CLAIMS][:, list_columns(part)])
+                    nc.vector.tensor_copy(window, values)
 
         def product(kind, c, bank):
             for a in range(PASSES):
@@ -286,7 +286,7 @@ def tile_list_trench_dispute_features_kernel(
             pieces = [(bank, sum(widths[:n]), widths[n]) for n, bank in enumerate(page_banks)]
             terms = [cons_rows[c], page_of(kind, c)] if kind == CLAIMS else [page_of(kind, c)]
             if (kind, c) == (CLAIMS, 0):
-                terms.append(pages[CLAIMS][3])
+                terms.reverse()
             if result is None:
                 result = ring.tile([P, T2], F32, name=f"squares{kind}", bufs=(4, 3)[kind])
             squares[kind, c] = result
@@ -316,7 +316,7 @@ def tile_list_trench_dispute_features_kernel(
                 )
 
         def difference(c):
-            b, quad = divmod(ROWS[c], PACK)
+            b, quad = divmod(c, PACK)
             nc.gpsimd.tensor_tensor(
                 z_t[b][:].rearrange("t (g x) -> t g x", g=16)[:, :, 64 * quad : 64 * (quad + 1)],
                 squares[CLAIMS, c][:].rearrange("t (g x) -> t g x", g=16),
@@ -421,6 +421,7 @@ def tile_list_trench_dispute_features_kernel(
         for g in range(2, W2_CHUNKS):
             load_w2(g)
         load_w1(2)
+        load_scale_rows(w1_s[2], w1_scales, w1_pieces[2])
         for c in range(ROW_TILES):
             load_cons(c)
         for b in range(PASSES):
@@ -428,44 +429,50 @@ def tile_list_trench_dispute_features_kernel(
 
         chunk_values = PACK * chunk_words
         opening = keep.tile([P, 3 * S], F32, name="opening")
-        h[CLAIMS, 0] = opening[:, :S]
+        h[CLAIMS, 0], h[CLAIMS, 1] = opening[:, :S], opening[:, S : 2 * S]
         first_features()
         features(CLAIMS, 3, 0, opening[:, 2 * S :])
         gain_one(CLAIMS, 3, h[CLAIMS, 3])
-        features(CLAIMS, 1, 1, opening[:, S : 2 * S])
-        product(CLAIMS, 2, 0)
+        product(CLAIMS, 2, 1)
         rounded = [slot(f"rounded{g}", chunk_values, BF16) for g in range(2)]
         late_rounded = slot("late_rounded", 2 * chunk_values, BF16)
         round_w2(0, rounded[0])
         h[CLAIMS, 2] = slot("raw1", S, F32)[:]
-        nc.scalar.copy(h[CLAIMS, 2], banks[0][:])
-        scatter(CLAIMS, 1, fused=True)
-        round_w2(1, rounded[1])
+        nc.scalar.copy(h[CLAIMS, 2], banks[1][:])
         quantize_w2(0, 1, rounded[0][:])
-        features(EVIDENCE, 0, 1, slot("raw3", S, F32)[:])
+        round_w2(1, rounded[1])
         scatter(CLAIMS, 2, fused=True)
+        product(EVIDENCE, 0, 1)
         quantize_w2(1, 1, rounded[1][:])
         product(EVIDENCE, 1, 0)
         round_w2(2, late_rounded[:, :chunk_values])
+        h[EVIDENCE, 0] = slot("raw5", S, F32)[:]
+        nc.scalar.copy(h[EVIDENCE, 0], banks[1][:])
         scatter(EVIDENCE, 0, fused=True)
         round_w2(3, late_rounded[:, chunk_values:])
-        held = slot("raw_last", 5 * S, F32)
+        held = slot("raw_last", 4 * S, F32)
         h[EVIDENCE, 1] = held[:, :S]
         nc.scalar.copy(h[EVIDENCE, 1], banks[0][:])
         features(EVIDENCE, 2, 1, held[:, S : 2 * S])
-        pair = feature_pair(4, 3, held[:, 3 * S :], (6, 7))
         quantize_w2(2, 2, late_rounded[:])
-        z_t[0] = slot("late_rounded", PACK * T2, BF16)
-        squared(CLAIMS, 0, (0, 1))
+        gained = slot("late_rounded", 4 * S, F32)
+        squared(CLAIMS, 0, (2, 0))
+        pair = feature_pair(4, 3, held[:, 2 * S :], (6, 7))
         squared(EVIDENCE, 0, (6, 7))
-        scatter(EVIDENCE, 1, fused=True)
+        scatter(CLAIMS, 3)
 
-        gain_one(EVIDENCE, 2, held[:, :S])
-        gain_pair(4, 3, pair, held[:, S : 3 * S])
+        nc.gpsimd.tensor_tensor(
+            gained[:, : 2 * S].rearrange("p (c s) -> p c s", c=2),
+            held[:, : 2 * S].rearrange("p (c s) -> p c s", c=2),
+            gain[EVIDENCE].unsqueeze(1).to_broadcast([P, 2, S]),
+            MULT,
+        )
+        h[EVIDENCE, 1], h[EVIDENCE, 2] = gained[:, :S], gained[:, S : 2 * S]
+        gain_pair(4, 3, pair, gained[:, 2 * S :])
         difference(0)
         squared(CLAIMS, 1, (0, 1))
+        scatter(EVIDENCE, 1)
         squared(EVIDENCE, 1, (4, 5))
-        scatter(CLAIMS, 3)
         difference(1)
         pairs = {5: feature_pair(5, 4, slot("raw4", 2 * S, F32)[:], (2, 3))}
         squared(CLAIMS, 2, (6, 7))

@@ -442,22 +442,23 @@ def tile_list_trench_dispute_features_kernel(
         quantize_w2(0, 1, rounded[0][:])
         round_w2(1, rounded[1])
         scatter(CLAIMS, 2, fused=True)
-        product(EVIDENCE, 0, 1)
+        features(EVIDENCE, 0, 1, slot("raw3", S, F32)[:])
         quantize_w2(1, 1, rounded[1][:])
         product(EVIDENCE, 1, 0)
         round_w2(2, late_rounded[:, :chunk_values])
-        h[EVIDENCE, 0] = slot("raw5", S, F32)[:]
-        nc.scalar.copy(h[EVIDENCE, 0], banks[1][:])
-        scatter(EVIDENCE, 0, fused=True)
-        round_w2(3, late_rounded[:, chunk_values:])
-        held = slot("raw_last", 4 * S, F32)
-        h[EVIDENCE, 1] = held[:, :S]
+        h[EVIDENCE, 1] = slot("raw5", S, F32)[:]
         nc.scalar.copy(h[EVIDENCE, 1], banks[0][:])
-        features(EVIDENCE, 2, 1, held[:, S : 2 * S])
+        scatter(EVIDENCE, 0, fused=True)
+        product(EVIDENCE, 2, 0)
+        round_w2(3, late_rounded[:, chunk_values:])
+        scatter(EVIDENCE, 1, fused=True)
+        held = slot("raw_last", 3 * S, F32)
+        nc.scalar.copy(held[:, :S], banks[0][:])
+        features(EVIDENCE, 3, 7, held[:, S : 2 * S])
         quantize_w2(2, 2, late_rounded[:])
-        gained = slot("late_rounded", 4 * S, F32)
-        squared(CLAIMS, 0, (2, 0))
-        pair = feature_pair(4, 3, held[:, 2 * S :], (6, 7))
+        gained = slot("late_rounded", 3 * S, F32)
+        squared(CLAIMS, 0, (0, 1))
+        features(CLAIMS, 4, 6, held[:, 2 * S :])
         squared(EVIDENCE, 0, (6, 7))
         scatter(CLAIMS, 3)
 
@@ -467,15 +468,14 @@ def tile_list_trench_dispute_features_kernel(
             gain[EVIDENCE].unsqueeze(1).to_broadcast([P, 2, S]),
             MULT,
         )
-        h[EVIDENCE, 1], h[EVIDENCE, 2] = gained[:, :S], gained[:, S : 2 * S]
-        gain_pair(4, 3, pair, gained[:, 2 * S :])
+        h[EVIDENCE, 2], h[EVIDENCE, 3] = gained[:, :S], gained[:, S : 2 * S]
+        gain_one(CLAIMS, 4, gained[:, 2 * S :])
         difference(0)
         squared(CLAIMS, 1, (0, 1))
-        scatter(EVIDENCE, 1)
-        squared(EVIDENCE, 1, (4, 5))
+        squared(EVIDENCE, 1, (6, 7))
         difference(1)
         pairs = {5: feature_pair(5, 4, slot("raw4", 2 * S, F32)[:], (2, 3))}
-        squared(CLAIMS, 2, (6, 7))
+        squared(CLAIMS, 2, (4, 5))
         squared(CLAIMS, 3, (0, 1))
         scatter(EVIDENCE, 2)
         gain_pair(5, 4, pairs[5], pairs[5])

@@ -61,10 +61,9 @@ def tile_list_trench_dispute_features_kernel(
         w1_s = [keep.tile([P, PASSES * 2 * P], U8, name="w1_s0", align_bytes=64)]
         v_w = [keep.tile([P, S], U32, name=f"v_w{a}", align_bytes=64) for a in range(PASSES)]
         v_s = [v_planes[:, a * S : (a + 1) * S] for a in range(PASSES)]
-        ident = keep.tile([P, P], F32, name="ident")
         pages = [
             [keep.tile([P, T2], F32, name=f"page{kind}_{i}") for i in range(count)]
-            for kind, count in ((CLAIMS, 3), (EVIDENCE, 2))
+            for kind, count in ((CLAIMS, 3), (EVIDENCE, 1))
         ]
         w2_w = keep.tile([P, PASSES * H], U32, name="w2_w", align_bytes=64)
         w2_s = keep.tile([P, PASSES * H], U8, name="w2_s", align_bytes=64)
@@ -131,11 +130,12 @@ def tile_list_trench_dispute_features_kernel(
         for plane in w1_s[1:]:
             nc.gpsimd.memset(plane[:].bitcast(I32), 0)
         load_scale_rows(w1_s[1], w1_scales, w1_pieces[1])
-        for page in pages[CLAIMS][:2]:
+        for page in pages[CLAIMS] + pages[EVIDENCE]:
             nc.vector.memset(page[:].bitcast(I32), 0)
+        ident = slot("ident", P, F32)
         make_identity(nc, ident[:])
-        for page in pages[CLAIMS][2:] + pages[EVIDENCE]:
-            nc.gpsimd.memset(page[:].bitcast(I32), 0)
+        pages[EVIDENCE].append(slot("last_page", T2, F32))
+        nc.gpsimd.memset(pages[EVIDENCE][1][:].bitcast(I32), 0)
 
         def entries(part):
             return slice(part * S // FIRST_PARTS, (part + 1) * S // FIRST_PARTS)

from contextlib import ExitStack

import concourse.mybir as mybir
from concourse.masks import make_identity

K, H, N, T, S, T2 = 1024, 1024, 512, 2048, 512, 1024
FLOPS = 2 * (2 * K * H * S + H * N * T2)

F32 = mybir.dt.float32
BF16 = mybir.dt.bfloat16
I32 = mybir.dt.int32
U32 = mybir.dt.uint32
U16 = mybir.dt.uint16
U8 = mybir.dt.uint8
FP8X4 = mybir.dt.float8_e4m3fn_x4
FP4X4 = mybir.dt.float4_e2m1fn_x4
MULT = mybir.AluOpType.mult
SUBTRACT = mybir.AluOpType.subtract
SQUARE = mybir.ActivationFunctionType.Square

P = 128
PACK = 4
K_PASS = P * PACK
PASSES = K // K_PASS
ROW_TILES = H // P
LAST = ROW_TILES - 1
BANK = 512
HALVES = T2 // BANK
QUARTER = 256
QUARTERS = T2 // QUARTER
LIST_COLUMNS = S // 16
W2_CHUNK = 2
W2_CHUNKS = ROW_TILES // W2_CHUNK
FIRST_PARTS = 2
CLAIMS, EVIDENCE = 0, 1


def tile_list_trench_dispute_features_kernel(
    tc, tab_words, tab_scales, offs, offs2, offs3, w1_words, w1_scales, w2, wg1, wg2, cons, w3, out_0, out_1, out_2
):
    nc = tc.nc
    with ExitStack() as ctx:
        lists = ctx.enter_context(tc.tile_pool(name="lists", bufs=1))
        keep = ctx.enter_context(tc.tile_pool(name="keep", bufs=1))
        tables = ctx.enter_context(tc.tile_pool(name="tables", bufs=1))
        psum = ctx.enter_context(tc.psum_pool(name="psum", bufs=1))

        banks = [psum.tile([P, BANK], F32, name=f"bank{i}") for i in range(8)]

        def table_slot(a, columns, dtype):
            return tables.tile([P, columns], dtype, name=f"table{a}", bufs=1, align_bytes=64)

        idx_notes = lists.tile([P, LIST_COLUMNS], U16, name="idx_notes")
        idx_pages = [lists.tile([P, LIST_COLUMNS], U16, name=f"idx_page{kind}") for kind in (CLAIMS, EVIDENCE)]

        tab_w = [table_slot(a, T, U32) for a in range(PASSES)]
        picked_s = keep.tile([P, S], U8, name="picked_s", align_bytes=64)
        v_planes = keep.tile([P, PASSES * S], U8, name="v_planes", align_bytes=64)
        w1_pieces = [slice(0, 2 * P), slice(2 * P, 4 * P), slice(4 * P, H)]
        w1_w = [keep.tile([P, PASSES * 4 * P], U8, name="w1_w0", align_bytes=64)]
        w1_s = [keep.tile([P, PASSES * 2 * P], U8, name="w1_s0", align_bytes=64)]
        v_w = [keep.tile([P, S], U32, name=f"v_w{a}", align_bytes=64) for a in range(PASSES)]
        v_s = [v_planes[:, a * S : (a + 1) * S] for a in range(PASSES)]
        pages = [
            [keep.tile([P, T2], F32, name=f"page{kind}_{i}") for i in range(count)]
            for kind, count in ((CLAIMS, 3), (EVIDENCE, 1))
        ]
        w2_w = keep.tile([P, PASSES * H], U32, name="w2_w", align_bytes=64)
        w2_s = keep.tile([P, PASSES * H], U8, name="w2_s", align_bytes=64)
        w3_s = keep.tile([P, PASSES * N], U8, name="w3_s", align_bytes=64)
        z_t = [keep.tile([P, PACK * T2], BF16, name=f"z_t{b}") for b in range(PASSES)]
        z_s = [keep.tile([P, T2], U8, name=f"z_s{b}", align_bytes=64) for b in range(PASSES)]
        z_last = keep.tile([P, T2], U32, name="z_last", align_bytes=64)
        y_w = keep.tile([P, T2], U32, name="y_w", align_bytes=64)
        y_s = keep.tile([P, T2], U8, name="y_s", align_bytes=64)

        def load_scale_rows(plane, scales, cols):
            for quad in range(4):
                nc.sync.dma_start(
                    out=plane[32 * quad : 32 * quad + 4, :].bitcast(I32).rearrange("i (a c) -> i a c", a=PASSES),
                    in_=scales[:, 4 * quad : 4 * quad + 4, cols].bitcast(I32).rearrange("a i c -> i a c"),
                )

        def load_w1(piece):
            cols = w1_pieces[piece]
            nc.sync.dma_start(
                out=w1_w[piece][:].bitcast(I32).rearrange("p (a c) -> p a c", a=PASSES),
                in_=w1_words[:, :, 2 * cols.start : 2 * cols.stop].bitcast(I32).rearrange("a p c -> p a c"),
            )

        def load_tab_words(a):
            nc.sync.dma_start(
                out=tab_w[a][:].bitcast(I32), in_=tab_words[a].rearrange("p t i -> p (t i)").bitcast(I32)
            )

        with tc.tile_pool(name="early", bufs=1) as early:
            tab_s = early.tile([P, T], U8, name="tab_s", align_bytes=64)
            nc.vector.memset(tab_s[:].bitcast(I32), 0)
            nc.vector.memset(w1_s[0][:].bitcast(I32), 0)
            nc.vector.memset(v_planes[:].bitcast(I32), 0)
            nc.sync.dma_start(idx_notes[:], offs)
            load_tab_words(0)
            nc.scalar.dma_start(
                out=tab_s[0:P:4, :].bitcast(I32), in_=tab_scales.bitcast(I32).rearrange("a q c -> q a c")
            )
            nc.sync.dma_start(idx_pages[CLAIMS][:], offs2)
            load_scale_rows(w1_s[0], w1_scales, w1_pieces[0])
            load_tab_words(1)
            nc.sync.dma_start(idx_pages[EVIDENCE][:], offs3)
            load_w1(0)
            nc.vector.tensor_copy(picked_s[:], tab_s[:].indirect(idx_notes[:]))

        ring = ctx.enter_context(tc.tile_pool(name="ring", bufs=1))

        def slot(name, columns, dtype):
            return ring.tile([P, columns], dtype, name=name, bufs=1, align_bytes=64)

        for piece, cols in list(enumerate(w1_pieces))[1:]:
            w1_w.append(slot(f"w1_w{piece}", PASSES * 2 * (cols.stop - cols.start), U8))
            w1_s.append(slot(f"w1_s{piece}", PASSES * (cols.stop - cols.start), U8))
        gains = slot("gains", 2 * S, F32)
        gain = [gains[:, 0:S], gains[:, S : 2 * S]]
        for quad in range(4):
            nc.sync.dma_start(
                out=v_planes[32 * quad : 32 * quad + 4, :].bitcast(I32),
                in_=picked_s[32 * quad : 32 * quad + 32 : 4, :].bitcast(I32),
            )
        nc.sync.dma_start(out=gain[CLAIMS], in_=wg1)
        load_w1(1)
        for plane in w1_s[1:]:
            nc.gpsimd.memset(plane[:].bitcast(I32), 0)
        load_scale_rows(w1_s[1], w1_scales, w1_pieces[1])
        for page in pages[CLAIMS] + pages[EVIDENCE]:
            nc.vector.memset(page[:].bitcast(I32), 0)
        ident = slot("ident", P, F32)
        make_identity(nc, ident[:])
        pages[EVIDENCE].append(slot("last_page", T2, F32))
        nc.gpsimd.memset(pages[EVIDENCE][1][:].bitcast(I32), 0)

        def entries(part):
            return slice(part * S // FIRST_PARTS, (part + 1) * S // FIRST_PARTS)

        def list_columns(part):
            return slice(part * LIST_COLUMNS // FIRST_PARTS, (part + 1) * LIST_COLUMNS // FIRST_PARTS)

        nc.vector.tensor_copy(v_w[0][:], tab_w[0][:].indirect(idx_notes[:]))
        for part in range(FIRST_PARTS):
            nc.vector.tensor_copy(v_w[1][:, entries(part)], tab_w[1][:].indirect(idx_notes[:, list_columns(part)]))

        w2_raw, w3_raw, cons_rows = {}, {}, {}

        def load_w2(g):
            width = PACK * W2_CHUNK * P
            both = slot("raw_last", PASSES * width, F32) if g == W2_CHUNKS - 1 else None
            for a in range(PASSES):
                raw = slot(f"raw{PASSES * g + a}", width, F32) if both is None else both[:, a * width : (a + 1) * width]
                rows = w2[a * K_PASS : (a + 1) * K_PASS, g * W2_CHUNK * P : (g + 1) * W2_CHUNK * P]
                nc.sync.dma_start(
                    out=raw[:].rearrange("p (j w) -> p j w", j=PACK), in_=rows.rearrange("(p j) w -> p j w", j=PACK)
                )
                w2_raw[g, a] = raw

        def load_w3(b):
            raw = table_slot(b, PACK * N, F32)
            nc.sync.dma_start(out=raw[:], in_=w3[b * K_PASS : (b + 1) * K_PASS, :].rearrange("(p j) n -> p (j n)", j=PACK))
            w3_raw[b] = raw

        def load_cons(c):
            rows = ring.tile([P, T2], F32, name="cons_rows", bufs=LAST) if c < LAST else slot("cons_last", T2, F32)
            nc.sync.dma_start(out=rows[:], in_=cons[c * P : (c + 1) * P, :])
            cons_rows[c] = rows

        chunk_words = PASSES * W2_CHUNK * P

        def round_w2(g, rounded):
            for a in range(PASSES):
                width = PACK * W2_CHUNK * P
                nc.scalar.copy(
                    rounded[:, a * width : (a + 1) * width].rearrange("p (c i j) -> p c j i", i=4, j=PACK),
                    w2_raw[g, a][:].rearrange("p (j c i) -> p c j i", j=PACK, i=4),
                )

        def quantize_w2(first, count, rounded):
            cols = slice(first * chunk_words, (first + count) * chunk_words)
            nc.vector.quantize_mx(out=w2_w[:, cols].bitcast(FP8X4), scales=w2_s[:, cols], in_=rounded)

        w3_rounded, w3_w = {}, {}

        def round_w3(b, name):
            rounded = slot(name, PACK * N, BF16)
            w3_rounded[b] = rounded
            dst = rounded[:].rearrange("p (s m j) -> p m j s", s=PACK, j=PACK)
            src = w3_raw[b][:].rearrange("p (j m s) -> p m j s", j=PACK, s=PACK)
            for half in range(2):
                rows = slice(half * P // 2, (half + 1) * P // 2)
                nc.scalar.copy(dst[:, rows], src[:, rows])

        def quantize_w3(b, codes):
            w3_w[b] = codes
            nc.vector.quantize_mx(
                out=codes.bitcast(FP8X4), scales=w3_s[:, b * N : (b + 1) * N], in_=w3_rounded[b][:]
            )

        def stationary(kind, c, a):
            if kind == CLAIMS:
                piece = min(c // 2, 2)
                cols = w1_pieces[piece]
                col = a * (cols.stop - cols.start) + c * P - cols.start
                return w1_w[piece][:, 2 * col : 2 * (col + P)].bitcast(FP4X4), w1_s[piece][:, col : col + P]
            g, tile = divmod(c, W2_CHUNK)
            col = ((PASSES * g + a) * W2_CHUNK + tile) * P
            return w2_w[:, col : col + P].bitcast(FP8X4), w2_s[:, col : col + P]

        h = {}

        def first_features():
            width = S // FIRST_PARTS
            for part in range(FIRST_PARTS):
                for c in range(2):
                    bank = banks[4 + 2 * part + c]
                    for a in range(PASSES):
                        codes, scales = stationary(CLAIMS, c, a)
                        nc.tensor.matmul_mx(
                            out=bank[:, 0:width],
                            lhsT=codes,
                            lhsT_scale=scales,
                            rhs=v_w[a][:, entries(part)].bitcast(FP8X4),
                            rhs_scale=v_s[a][:, entries(part)],
                            start=(a == 0),
                            stop=(a == PASSES - 1),
                        )
                    values = h[CLAIMS, c][:, entries(part)]
                    if (part, c) == (0, 0):
                        nc.vector.tensor_tensor(values, bank[:, 0:width], gains[:, entries(part)], MULT)
                    else:
                        nc.scalar.copy(values, bank[:, 0:width])
                        nc.gpsimd.tensor_tensor(values, values, gains[:, entries(part)], MULT)
                    window = page_of(CLAIMS, c)[:].indirect(idx_pages[CLAIMS][:, list_columns(part)])
                    nc.vector.tensor_copy(window, values)

        def product(kind, c, bank):
            for a in range(PASSES):
                codes, scales = stationary(kind, c, a)
                nc.tensor.matmul_mx(
                    out=banks[bank][:],
                    lhsT=codes,
                    lhsT_scale=scales,
                    rhs=v_w[a][:].bitcast(FP8X4),
                    rhs_scale=v_s[a],
                    start=(a == 0),
                    stop=(a == PASSES - 1),
                )

        def features(kind, c, bank, into):
            product(kind, c, bank)
            nc.scalar.copy(into, banks[bank][:])
            h[kind, c] = into

        def feature_pair(claim, evid, both, pair_banks):
            features(CLAIMS, claim, pair_banks[0], both[:, :S])
            features(EVIDENCE, evid, pair_banks[1], both[:, S:])
            return both

        def gain_pair(claim, evid, both, result):
            nc.gpsimd.tensor_tensor(result, both, gains[:], MULT)
            h[CLAIMS, claim], h[EVIDENCE, evid] = result[:, :S], result[:, S:]

        def gain_one(kind, c, result):
            nc.gpsimd.tensor_tensor(result, h[kind, c], gain[kind], MULT)
            h[kind, c] = result

        def page_of(kind, c):
            return pages[kind][((0, 1, 2, 0, 0, 0, 2, 1), (0, 1, 0, 1, 1, 0, 1, 1))[kind][c]]

        def scatter(kind, c, fused=False):
            window = page_of(kind, c)[:].indirect(idx_pages[kind][:])
            if fused:
                nc.vector.tensor_tensor(window, h[kind, c], gain[kind], MULT)
            else:
                nc.vector.tensor_copy(window, h[kind, c])

        squares = {}

        def squared(kind, c, page_banks, result=None, widths=None):
            widths = widths or [T2 // P // len(page_banks)] * len(page_banks)
            pieces = [(bank, sum(widths[:n]), widths[n]) for n, bank in enumerate(page_banks)]
            terms = [cons_rows[c], page_of(kind, c)] if kind == CLAIMS else [page_of(kind, c)]
            if (kind, c) == (CLAIMS, 0):
                terms.reverse()
            if result is None:
                result = ring.tile([P, T2], F32, name=f"squares{kind}", bufs=(4, 3)[kind])
            squares[kind, c] = result
            groups = result[:].rearrange("t (f h u q e) -> t f h u q e", f=HALVES, h=2, u=4, e=2)

            def transposes(i, bank, first, blocks):
                for u in range(blocks):
                    nc.tensor.matmul(
                        banks[bank][:, u * P : (u + 1) * P],
                        lhsT=terms[i][:, (first + u) * P : (first + u + 1) * P],
                        rhs=ident[:],
                        is_transpose=True,
                        start=(len(terms) == 1 or (i == 0 and u == 0)),
                        stop=(len(terms) == 1 or (i == len(terms) - 1 and u == blocks - 1)),
                    )

            for i in range(len(terms) - 1):
                for piece in pieces:
                    transposes(i, *piece)
            for bank, first, blocks in pieces:
                transposes(len(terms) - 1, bank, first, blocks)
                f, u = divmod(first, 4)
                nc.scalar.activation(
                    groups[:, f, :, u : u + blocks],
                    banks[bank][:, : blocks * P].rearrange("t (u q h e) -> t h u q e", h=2, e=2, q=32),
                    SQUARE,
                )

        def difference(c):
            b, quad = divmod(c, PACK)
            nc.gpsimd.tensor_tensor(
                z_t[b][:].rearrange("t (g x) -> t g x", g=16)[:, :, 64 * quad : 64 * (quad + 1)],
                squares[CLAIMS, c][:].rearrange("t (g x) -> t g x", g=16),
                squares[EVIDENCE, c][:].rearrange("t (g x) -> t g x", g=16),
                SUBTRACT,
            )

        def last_difference(first, blocks):
            b, quad = divmod(LAST, PACK)
            f, u = divmod(first, 4)
            views = [
                tile[:].rearrange("t (f h u x) -> t f h u x", f=2, h=2, u=4)[:, f, :, u : u + blocks, :]
                for tile in (z_t[b], squares[CLAIMS, LAST], squares[EVIDENCE, LAST])
            ]
            nc.vector.tensor_tensor(views[0][:, :, :, 64 * quad : 64 * (quad + 1)], views[1], views[2], SUBTRACT)

        def turn_z(b, first, blocks, bank, rounded):
            words = z_t[b][:].bitcast(F32)
            f, u0 = divmod(first, 4)
            for u in range(blocks):
                for half in range(2):
                    g = 8 * f + 4 * half + u0 + u
                    nc.tensor.transpose(
                        banks[bank][:, (2 * u + half) * P : (2 * u + half + 1) * P],
                        words[:, g * P : (g + 1) * P],
                        ident[:],
                    )
            (nc.vector.tensor_copy if b == PASSES - 1 and first == 6 else nc.scalar.copy)(
                rounded.bitcast(F32).rearrange("p (u t h) -> p u t h", u=blocks, h=2),
                banks[bank][:, : 2 * blocks * P].rearrange("p (u h t) -> p u t h", u=blocks, h=2),
            )

        z_w = {}

        def quantize_z(b, first, count, rounded, codes):
            for i in range(count):
                z_w[b, first + i] = codes[:, i * QUARTER : (i + 1) * QUARTER]
            cols = slice(first * QUARTER, (first + count) * QUARTER)
            nc.vector.quantize_mx(out=codes.bitcast(FP8X4), scales=z_s[b][:, cols], in_=rounded)

        y_banks = [(0, 1), (2, 3), (5, 6), (7, 4)]

        def y_pass(b, quarter, rows=range(PACK)):
            cols = slice(quarter * QUARTER, (quarter + 1) * QUARTER)
            for j in rows:
                nc.tensor.matmul_mx(
                    out=banks[y_banks[quarter][j // 2]][:, (j % 2) * QUARTER : (j % 2 + 1) * QUARTER],
                    lhsT=w3_w[b][:, j * P : (j + 1) * P].bitcast(FP8X4),
                    lhsT_scale=w3_s[:, b * N + j * P : b * N + (j + 1) * P],
                    rhs=z_w[b, quarter].bitcast(FP8X4),
                    rhs_scale=z_s[b][:, cols],
                    start=(b == 0 and j % 2 == 0),
                    stop=(b == PASSES - 1 and j % 2 == 1),
                )

        def y_block(b, block):
            cols = slice(block * P, (block + 1) * P)
            for j in range(PACK):
                nc.tensor.matmul_mx(
                    out=banks[y_banks[0][block]][:, j * P : (j + 1) * P],
                    lhsT=w3_w[b][:, j * P : (j + 1) * P].bitcast(FP8X4),
                    lhsT_scale=w3_s[:, b * N + j * P : b * N + (j + 1) * P],
                    rhs=z_w[b, 0][:, cols].bitcast(FP8X4),
                    rhs_scale=z_s[b][:, cols],
                    start=(b == 0 and j == 0),
                    stop=(b == PASSES - 1 and j == PACK - 1),
                )

        y_rows = out_0.rearrange("(p j) t -> p j t", j=PACK)
        y_words = out_1[0].rearrange("p t i -> p (t i)").bitcast(I32)

        y_bf16 = {}

        def quantize_y(quarter):
            cols = slice(quarter * QUARTER, (quarter + 1) * QUARTER)
            nc.vector.quantize_mx(out=y_w[:, cols].bitcast(FP8X4), scales=y_s[:, cols], in_=y_bf16[quarter][:])

        def finish(quarter):
            cols = slice(quarter * QUARTER, (quarter + 1) * QUARTER)
            y_all = ring.tile([P, PACK * QUARTER], F32, name="cons_rows", bufs=LAST)
            for i, bank in enumerate(y_banks[quarter]):
                part = y_all[:, i * BANK : (i + 1) * BANK]
                nc.scalar.copy(part, banks[bank][:])
                if quarter == 0:
                    target, rows = y_rows[:, :, i * P : (i + 1) * P], PACK
                else:
                    target, rows = y_rows[:, 2 * i : 2 * i + 2, cols], 2
                nc.sync.dma_start(out=target, in_=part.rearrange("p (j t) -> p j t", j=rows))
            y_rounded = ring.tile([P, PACK * QUARTER], BF16, name="y_rounded", bufs=QUARTERS, align_bytes=64)
            blocks = 2 if quarter == 0 else 1
            nc.vector.tensor_copy(
                y_rounded[:].rearrange("p (b c i j) -> p b c j i", b=blocks, i=4, j=PACK),
                y_all[:].rearrange("p (b j c i) -> p b c j i", b=blocks, j=PACK, i=4),
            )
            y_bf16[quarter] = y_rounded
            if quarter > 0:
                quantize_y(quarter - 1)

        load_w2(0)
        load_w2(1)
        nc.sync.dma_start(out=gain[EVIDENCE], in_=wg2)
        for g in range(2, W2_CHUNKS):
            load_w2(g)
        load_w1(2)
        load_scale_rows(w1_s[2], w1_scales, w1_pieces[2])
        for c in range(ROW_TILES):
            load_cons(c)
        for b in range(PASSES):
            load_w3(b)

        chunk_values = PACK * chunk_words
        opening = keep.tile([P, 3 * S], F32, name="opening")
        h[CLAIMS, 0], h[CLAIMS, 1] = opening[:, :S], opening[:, S : 2 * S]
        first_features()
        features(CLAIMS, 3, 0, opening[:, 2 * S :])
        gain_one(CLAIMS, 3, h[CLAIMS, 3])
        product(CLAIMS, 2, 1)
        rounded = [slot(f"rounded{g}", chunk_values, BF16) for g in range(2)]
        late_rounded = slot("late_rounded", 2 * chunk_values, BF16)
        round_w2(0, rounded[0])
        h[CLAIMS, 2] = slot("raw1", S, F32)[:]
        nc.scalar.copy(h[CLAIMS, 2], banks[1][:])
        quantize_w2(0, 1, rounded[0][:])
        round_w2(1, rounded[1])
        scatter(CLAIMS, 2, fused=True)
        features(EVIDENCE, 0, 1, slot("raw3", S, F32)[:])
        quantize_w2(1, 1, rounded[1][:])
        product(EVIDENCE, 1, 0)
        round_w2(2, late_rounded[:, :chunk_values])
        h[EVIDENCE, 1] = slot("raw5", S, F32)[:]
        nc.scalar.copy(h[EVIDENCE, 1], banks[0][:])
        scatter(EVIDENCE, 0, fused=True)
        product(EVIDENCE, 2, 0)
        round_w2(3, late_rounded[:, chunk_values:])
        scatter(EVIDENCE, 1, fused=True)
        held = slot("raw_last", 3 * S, F32)
        nc.scalar.copy(held[:, :S], banks[0][:])
        features(EVIDENCE, 3, 7, held[:, S : 2 * S])
        quantize_w2(2, 2, late_rounded[:])
        gained = slot("late_rounded", 3 * S, F32)
        squared(CLAIMS, 0, (0, 1))
        features(CLAIMS, 4, 6, held[:, 2 * S :])
        squared(EVIDENCE, 0, (6, 7))
        scatter(CLAIMS, 3)

        nc.gpsimd.tensor_tensor(
            gained[:, : 2 * S].rearrange("p (c s) -> p c s", c=2),
            held[:, : 2 * S].rearrange("p (c s) -> p c s", c=2),
            gain[EVIDENCE].unsqueeze(1).to_broadcast([P, 2, S]),
            MULT,
        )
        h[EVIDENCE, 2], h[EVIDENCE, 3] = gained[:, :S], gained[:, S : 2 * S]
        gain_one(CLAIMS, 4, gained[:, 2 * S :])
        difference(0)
        squared(CLAIMS, 1, (0, 1))
        squared(EVIDENCE, 1, (6, 7))
        difference(1)
        pairs = {5: feature_pair(5, 4, slot("raw4", 2 * S, F32)[:], (2, 3))}
        squared(CLAIMS, 2, (4, 5))
        squared(CLAIMS, 3, (0, 1))
        scatter(EVIDENCE, 2)
        gain_pair(5, 4, pairs[5], pairs[5])
        squared(EVIDENCE, 2, (4, 5))
        features(EVIDENCE, 5, 7, slot("raw5", S, F32)[:])
        scatter(EVIDENCE, 3)
        difference(2)
        squared(EVIDENCE, 3, (4, 5))
        pairs[6] = feature_pair(6, 6, slot("raw2", 2 * S, F32)[:], (6, 7))
        scatter(CLAIMS, 4)
        difference(3)
        gain_one(EVIDENCE, 5, h[EVIDENCE, 5])
        gain_pair(6, 6, pairs[6], pairs[6])
        squared(CLAIMS, 4, (2, 3))
        round_w3(0, "rounded0")
        scatter(EVIDENCE, 4)
        squared(EVIDENCE, 4, (4, 5))
        pairs[7] = feature_pair(7, 7, slot("raw1", 2 * S, F32)[:], (6, 7))
        scatter(CLAIMS, 5)
        difference(4)
        gain_pair(7, 7, pairs[7], pairs[7])
        squared(CLAIMS, 5, (2, 3))
        scatter(EVIDENCE, 5)
        squared(EVIDENCE, 5, (4, 5))
        first_pass = [slot(name, 2 * PACK * QUARTER, BF16) for name in ("raw0", "raw3")]
        for quarter in range(QUARTERS):
            f, pair_of = divmod(quarter, 2)
            turn_z(0, 2 * quarter, 2, (0, 1, 6, 7)[quarter], first_pass[f][:, pair_of * PACK * QUARTER : (pair_of + 1) * PACK * QUARTER])
        round_w3(1, "rounded1")
        scatter(CLAIMS, 6)
        difference(5)
        squared(CLAIMS, 6, (2, 3))
        scatter(EVIDENCE, 6)
        squared(EVIDENCE, 6, (0, 1))
        difference(6)
        scatter(CLAIMS, LAST)
        squared(CLAIMS, LAST, (2, 4, 5, 6, 7, 0, 1), widths=[2, 1, 1, 1, 1, 1, 1])
        for a in (0, 1, 0):
            codes, scales = stationary(EVIDENCE, LAST, a)
            nc.tensor.matmul_mx(
                out=banks[2][:],
                lhsT=codes,
                lhsT_scale=scales,
                rhs=v_w[a][:].bitcast(FP8X4),
                rhs_scale=v_s[a],
                start=True,
                stop=True,
            )
        scatter(EVIDENCE, LAST)

        def quantize_first(quarter, codes):
            f, pair_of = divmod(quarter, 2)
            width = PACK * QUARTER
            quantize_z(0, quarter, 1, first_pass[f][:, pair_of * width : (pair_of + 1) * width], codes)

        def quantize_last(quarter):
            quantize_z(1, quarter, 1, turned[2 * quarter][:], z_last[:, quarter * QUARTER : (quarter + 1) * QUARTER])

        pieces = [(0, 1), (1, 1), (2, 2), (4, 2), (6, 2)]
        codes = slot("cons_last", QUARTER + N, U32)
        quantize_first(0, codes[:, :QUARTER])
        quantize_w3(0, codes[:, QUARTER:])
        squared(EVIDENCE, LAST, (4, 5, 6, 7, 3), slot("raw6", T2, F32), widths=[blocks for first, blocks in pieces])
        for first, blocks in pieces:
            last_difference(first, blocks)
        quantize_w3(1, slot("raw6", N, U32)[:])
        for block in range(2):
            y_block(0, block)
        turned = {
            first: slot(f"turned{first}", blocks * PACK * P, BF16) for first, blocks in pieces
        }
        for (first, blocks), bank in zip(pieces[:-1], (4, 5, 6, 7)):
            turn_z(1, first, blocks, bank, turned[first][:])
        z_w[1, 0] = z_last[:, :QUARTER]
        for block in range(2):
            cols = slice(block * P, (block + 1) * P)
            nc.vector.quantize_mx(out=z_last[:, cols].bitcast(FP8X4), scales=z_s[1][:, cols], in_=turned[block][:])
        quantize_first(1, slot("turned0", QUARTER, U32)[:])
        quantize_last(1)
        quantize_first(2, slot("turned1", QUARTER, U32)[:])
        turn_z(1, 6, 2, 4, turned[6][:])
        quantize_last(2)
        quantize_first(3, slot("turned2", QUARTER, U32)[:])
        quantize_last(3)
        for block in range(2):
            y_block(1, block)
        finish(0)
        for quarter in range(1, QUARTERS):
            for rows in ((0, 1), (2, 3)):
                y_pass(0, quarter, rows)
                y_pass(1, quarter, rows)
            finish(quarter)
        quantize_y(QUARTERS - 1)
        for cols in (slice(0, 3 * QUARTER), slice(3 * QUARTER, T2)):
            nc.sync.dma_start(out=y_words[:, cols], in_=y_w[:, cols].bitcast(I32))
        for quad in range(4):
            (nc.sync, nc.scalar)[quad % 2].dma_start(
                out=out_2[0, 4 * quad : 4 * quad + 4, :].bitcast(I32), in_=y_s[32 * quad : 32 * quad + 4, :].bitcast(I32)
            )
